import numpy as np, ml_dtypes
CORES = [16,18,20,22]
N = 4
import mx_ref
BF = ml_dtypes.bfloat16
def pick(q, e):
    c = np.concatenate([q[0].reshape(128, -1, 4), np.zeros((128, 1, 4), np.uint8)], axis=1); s = np.concatenate([q[1], np.ones((16, 1), np.uint8)], axis=1)
    return (np.ascontiguousarray(c[:, e].reshape(128, -1)), np.ascontiguousarray(s[:, e]))
def join(*qs):
    return (np.concatenate([q[0] for q in qs], axis=1), np.concatenate([q[1] for q in qs], axis=1))
def put(q, e, v):
    c, s = q[0].reshape(128, -1, 4).copy(), q[1].copy(); c[:, e] = v[0].reshape(128, -1, 4); s[:, e] = v[1]
    return (c.reshape(128, -1), s)
def pk(c, s):
    return (np.ascontiguousarray(c), mx_ref.live(s))
def emit(q):
    return q[0], q[1]
def tile(rs):
    return np.stack(rs, axis=2).reshape(128, -1).astype(BF)
def f(rng, *shape):
    return mx_ref.flush((rng.standard_normal(shape, dtype=np.float32) * np.exp2(rng.integers(-2, 3, shape[:-1] + (1,)))).astype(BF))
def wide(rng, *shape, cols=0):
    v = rng.standard_normal(shape, dtype=np.float32) * np.exp2(rng.integers(-12, 13, shape)).astype(np.float32)
    if cols: v *= np.repeat(np.exp2(rng.integers(-cols, cols + 1, shape[:-2] + (1, shape[-1] // 4))) * (rng.random(shape[:-2] + (1, shape[-1] // 4)) > 0.0625), 4, axis=-1).astype(np.float32)
    return mx_ref.flush(v.astype(BF))
P, K, CAPP, R, L, B = 192, 24, 16, 3, 2, 10
def falling(s):
    return np.argsort(-(s + np.float32(0)), kind="stable")
def bits(g, first, n):
    return np.sum([(g[first + i] > 0) * 2 ** i for i in range(n)], axis=0)
def astile(v):
    s, n = v.shape[:-2], v.shape[-1]
    return np.ascontiguousarray(np.swapaxes(v.reshape(s + (128, 4, n)), -1, -2)).reshape(s + (128, 4 * n))
def weigh(rng, t):
    c, s = mx_ref.quantize(np.ascontiguousarray(t))
    p = mx_ref.plane(s, rng)
    return {"wc": np.stack([c] * N), "ws": np.stack([p] * N)}
def steer(rng, sign, low, at, free, same=False, xs=1.0, us=2.0 ** 13, lean=None):
    v = np.zeros((N, 512, P), np.float32)
    v[:, :128] = np.where(sign < 0, 112, 0)[:, None, :]
    v[:, 128:256] = np.where(sign > 0, 112, 0)[:, None, :]
    for t in range(3):
        for k in range(3): v[:, 256 + 3 * t + k] = low[t] // 8 ** k % 8
    if lean is not None: v[:, 265:266 + B] = lean
    for k in range(4):
        for i in range(L):
            one = at[:, :, k] // 2 ** i % 2
            v[:, 288 + 8 * k + 2 * i] = one
            v[:, 289 + 8 * k + 2 * i] = 1 - one
    v[:, 320:] = free
    a = np.zeros((2, 512, 512), np.float32)
    for m in range(2):
        j = np.arange(256)
        a[m, j, j] = 20
        j = np.arange(9)
        a[m, 256 + j, 256 + (j + 3) % 9] = 20
        j = np.arange(265, 265 + B)
        a[m, j, j] = 20
        a[m, 280 + 4 * m, 265 + B] = 20
        j = np.arange(32)
        a[m, 288 + j, 288 + (j + 8 * (m + 1)) % 32] = 20
        a[m, 320:, 320:] = rng.standard_normal((192, 192))
        if same and m == 0: a[m, 320:, 320:] = 20 * np.eye(192)
    w = np.concatenate([astile(np.ascontiguousarray(a[m][b::4].T)) for m in range(2) for b in range(4)], axis=1)
    h = np.zeros((512, 128), np.float32)
    h[:128, 0] = -448
    h[128:256, 0] = 448
    h[256:259, 0] = [1, 8, 64]
    for i in range(L):
        h[288 + 2 * i, 1 + i] = 1
        h[289 + 2 * i, 1 + i] = -1
    for i in range(B):
        h[265 + i, 1 + L + i] = 256
        h[265 + i, 1 + L + (i + 1) % B] = -256
    h[280, 1 + L:1 + L + B] = -256
    h[284, 1 + L:1 + L + B] = 256
    k = rng.standard_normal((192, B))
    h[320:, 1 + L:1 + L + B] = k - np.mean(k, axis=0)
    h[:, 1 + L + B:] = rng.standard_normal((512, 127 - L - B))
    x = mx_ref.flush((astile(v) * np.float32(xs)).astype(BF))
    u = mx_ref.flush((astile(h) * np.float32(us)).astype(BF))
    return {"x": x, "u": np.stack([u] * N), **weigh(rng, mx_ref.flush(w.astype(BF)))}
def setup_inputs(rng):
    return {"x": f(rng, N, 128, 4 * P), "u": np.stack([f(rng, 128, 512)] * N), **weigh(rng, f(rng, 128, 4096))}
def setup_inputs_close(rng):
    low = rng.integers(0, P // 2 - 1, (3, N, P))
    low[0] = P // 2 + (np.arange(P) + 1) // 2
    best = np.argsort(-low[0, 0], kind="stable")
    low[1][:, best[R * K - 1]] = P // 2 - 1
    at, free = rng.integers(0, N, (N, P, 4)), rng.standard_normal((N, 192, P))
    free[:, :, best[R * K:]] = 0
    lean = np.zeros((N, B + 1, P))
    for r in range(N):
        lean[r, rng.integers(0, B, R * K), best[:R * K]] = 1
        for t in range(R):
            to, e = rng.permutation(np.arange(2 * K) % N), best[t * K:t * K + K]
            at[r, e, 1], at[r, e, 2] = to[0::2], to[1::2]
    z, s = [int(k) for k in np.sort(rng.permutation(N)[:2])]
    for r in (z, s):
        low[1, r, best[0]] = P // 2 - 1
        free[r, :, best[0]] = 0
        lean[r, :, best[0]] = 0
    lean[s, B, best[0]] = 1
    return steer(rng, np.full((N, P), -1), low, at, free, lean=lean)
def setup_inputs_ties(rng):
    n, own = P // 4, K // 4
    def some(*shape):
        return rng.integers(4, 8, shape) * np.exp2(rng.integers(-1, 2, shape)) * (rng.random(shape) < 0.25)
    low, at, free = rng.integers(0, 4, (3, n)), rng.integers(0, N, (n, 4)), some(192, n)
    low[0] = np.arange(n) % 2
    e = np.stack([rng.permutation(np.arange(P) % n) for r in range(N)])
    lows, ats = low[:, e], at[e]
    frees = np.stack([free[:, e[r]] for r in range(N)])
    none = []
    for r in range(N):
        p = rng.permutation(P)
        k = p[:own]
        none.append(p[own:own + 2])
        lows[0, r, k], lows[1, r, k] = 2, 400
        ats[r, k] = rng.integers(0, N, (own, 4))
        ats[r, k, 1], ats[r, k, 2] = r, (r + 1) % N
        frees[r][:, k] = some(192, own)
    d = steer(rng, np.full((N, P), -1), lows, ats, frees, same=True)
    x, u = np.array(d["x"]), np.array(d["u"])
    for r in 1 + rng.permutation(N - 1)[:2]:
        for j in none[r]: x[r, :, 4 * j:4 * j + 4] = 0
    u[:, 80:, 4 * (1 + L):4 * (2 + L)] = np.abs(u[:, 80:, 4 * (1 + L):4 * (2 + L)].astype(np.float32)).astype(BF)
    return {**d, "x": x, "u": u}
def setup_inputs_crowd(rng):
    a, b, c, d = [int(k) for k in rng.permutation(N)[:4]]
    low = np.stack([np.stack([rng.permutation(P) for r in range(N)])] * 3)
    low[1] = 2 * P - low[0]
    low[2] = rng.integers(400, 500, (N, P))
    at, free = rng.integers(0, N, (N, P, 4)), rng.standard_normal((N, 192, P))
    for r in range(N):
        to = rng.choice(np.delete(np.arange(N), d), 2 * K)
        if r == a or r == b: to[:] = b
        elif r == c:
            to[:] = c
            to[:CAPP] = b
            to[CAPP:2 * CAPP + 1] = a
        else: to[:CAPP + int(rng.integers(1, 3))] = b
        to = rng.permutation(to)
        top = np.argsort(-low[0, r], kind="stable")[:K]
        at[r, top, 1], at[r, top, 2] = to[0::2], to[1::2]
    top = np.argsort(-low[0, a], kind="stable")[:K]
    e = top[:CAPP // 2]
    low[1, a, top[CAPP // 2:]] += P - K
    for t in range(3): low[t, a, e] = low[t, a, e[0]]
    at[a, e] = at[a, e[0]]
    free[a][:, e] = free[a][:, e[:1]]
    return steer(rng, np.full((N, P), -1), low, at, free)
def setup_inputs_huge(rng):
    sign = np.full((N, P), -1)
    for r in rng.permutation(N)[:N // 2]: sign[r, rng.permutation(P)[:K // 2]] = 1
    return steer(rng, sign, rng.integers(0, 512, (3, N, P)), rng.integers(0, N, (N, P, 4)), rng.standard_normal((N, 192, P)), xs=2.0 ** 23, us=2.0 ** 21)
def setup_inputs_spread(rng):
    return {**setup_inputs(rng), "x": wide(rng, N, 128, 4 * P, cols=6)}
def check_inputs(d):
    b = []
    for k in ("x", "u"):
        v = np.abs(d[k].astype(np.float32))
        if not (np.isfinite(v).all() and ((v == 0) | (v >= 2.0 ** -30) & (v <= 2.0 ** 30)).all()): b.append("a value of " + k)
    for k in ("u", "wc", "ws"):
        v = d[k].astype(np.float32)
        if (v != v[:1]).any(): b.append(k + " is not the same on every rank")
    if ((d["wc"] & 127) == 127).any(): b.append("a code of wc")
    zero, least, most = [int(mx_ref.quantize(np.full((128, 16), k, np.float32).astype(BF))[1].max()) for k in (0.0, 2.0 ** -30, 2.0 ** 30)]
    for r in range(N):
        s = mx_ref.live(d["ws"][r]).astype(int)
        if ((s != zero) & ((s < least) | (s > most))).any():
            b.append("a scale of ws")
            break
    return b
def reference(x, u, wc, ws):
    y, oc, osc = np.zeros((N, 128, R * P), np.float32), np.zeros((N, 128, 4 * P), np.uint8), np.zeros((N, 16, P), np.uint8)
    held = [mx_ref.quantize(np.ascontiguousarray(x[r])) for r in range(N)]
    qu = [mx_ref.quantize(np.ascontiguousarray(u[r])) for r in range(N)]
    w = []
    for r in range(N):
        q = pk(wc[r], ws[r])
        w.append([pick(q, np.arange(128 * i, 128 * i + 128)) for i in range(8)])
    for t in range(R):
        g = [mx_ref.matmul(qu[r], held[r]) for r in range(N)]
        top = [falling(g[r][0])[:K] for r in range(N)]
        kids, to = [], []
        for r in range(N):
            v = pick(held[r], top[r])
            z = [mx_ref.matmul(w[r][i], v) for i in range(8)]
            rs = [np.stack([z[b], z[4 + b]], axis=2).reshape(128, -1) for b in range(4)]
            kids.append(mx_ref.quantize(tile([np.maximum(e, np.float32(0)) * np.float32(0.05) for e in rs])))
            to.append(bits(mx_ref.matmul(qu[r], kids[r]), 1, L))
        for q in range(N):
            e = np.full((N, CAPP), -1)
            for r in range(N):
                k = np.flatnonzero(to[r] == q)[:CAPP]
                e[r, :len(k)] = k
            came = join(*[pick(kids[r], e[r]) for r in range(N)])
            h = mx_ref.matmul(qu[q], came)
            mark = bits(h, 1 + L, B)
            seen = set(np.delete(bits(g[q], 1 + L, B), top[q]).tolist())
            new = []
            for j in np.flatnonzero(e.reshape(-1) >= 0):
                if int(mark[j]) not in seen:
                    seen.add(int(mark[j]))
                    new.append(int(j))
            new = np.array(new, dtype=int)
            new = new[falling(h[0][new])][:K]
            if len(new): held[q] = put(held[q], np.sort(top[q])[:len(new)], pick(came, new))
            y[q, :, P * t:P * t + P] = mx_ref.matmul(w[q][0], held[q])
    for q in range(N): oc[q], osc[q] = emit(held[q])
    return {"y": y, "oc": oc, "osc": osc}

@@ -1,0 +1,707 @@
+import numpy as np
+from concourse.bass import DstId, RemoteDMATransfer
+from concourse.mybir import dt, AluOpType, AxisListType, ActivationFunctionType
+
+P, K, R, N = 192, 24, 3, 4
+TINY = 2.0 ** -100
+LOW = -1e29
+C05 = float(np.float32(0.05))
+X4, U8, U16, F32, BF, I32 = "float8_e4m3fn_x4", "uint8", "uint16", "float32", "bfloat16", "int32"
+KB = (392, 200, 8)
+O0, O1, PW = 584, 720, 912
+EW = 368
+
+SCRATCH = {"ps": ("psum", [128, 4096], F32)}
+
+
+def _decl(dtype, **kw):
+    for k, n in kw.items():
+        SCRATCH[k] = ("sbuf", [128, n], dtype)
+
+
+for _n, _w in (("qu", 128), ("um", 512), ("qx", 192), ("wm", 1024), ("sd0", 32), ("sd1", 48), ("pa", PW), ("pb", PW), ("pc", PW),
+               ("par1", 128), ("par2", 128), ("hw", 288), ("fin", 192)):
+    _decl(X4, **{_n + "c": _w})
+    _decl(U8, **{_n + "s": _w})
+_decl(BF, xt=768, ut=512, ones=224, flip0=448, e0=448, junk=1400, ms=24, hd=96, kt0=768, kt1=768, kt2=768, fa=192, fb=192, fz=192, cum=192,
+      le=192, lp=192, seg48=192, b49=192, pbw=196, pab=64, tb=96, ee=2 * EW, rm=2 * EW, eo=2 * EW, fr=64, thr=128, dd=128, cmpm=128, bt=128,
+      nn=192, fl=192, cm=200, cm2=80, r3=208, r3c=96, r3d=384, r3t=384)
+_decl(F32, io=376, cst=48, sm=88, v0=448, rr=64, su=320, cand=32, mcol=24, vf=208, t192=80, s192=80,
+      dg=80, seg16=80, dup=24, kid=196, mb=192, mkall=280, scp=328, sc=96, idr=96, plr=80, skw=196, asw=96, akw=96, aiw=96, wr=64,
+      at=64, ai=64, kb=96, vv=192, rv=96, nsr=32, nkr=32, tsc=96, tid=96, e3=312, flip3=312, v3=312, pv=104,
+      d32=64, s64=64, yc=208, yn=32, zero=80)
+_decl(U16, ofu=32, ofi=8, mk16=8, al16=8, mland=32, aland=32, alw=6, idw=6, rem=272, ofe=4, idx=2, olw=2, ofp=6, oni=2, ol=12, of3=12, ofd=24)
+_decl(I32, pi=4, mi=24)
+
+PART = {"scol": ("sm", 0, 2), "ini": ("sm", 2, 2), "gn": ("sm", 4, 4), "best": ("sm", 8, 8), "alf": ("sm", 16, 8), "mf": ("sm", 24, 8),
+        "ya": ("sm", 32, 6), "d2": ("sm", 40, 4), "b5": ("sm", 48, 8), "a5": ("sm", 56, 8), "yb": ("sm", 64, 6), "y6": ("sm", 72, 6),
+        "ib": ("sm", 80, 2), "mk192": ("mkall", 0, 200), "mka": ("mkall", 200, 80)}
+WAKE, LAND, FIRST = 100, {"am": 4500, "ap": 3600, "ar": 4500, "al": 3000}, {"ap": 3000}
+DMAS = ["x", "u", "wc", "ws", "cb0", "cb1", "cc0", "cc1", "y0", "y1", "y2", "oc", "os0", "os1", "os2", "os3"]
+SEMAPHORES = ["qv", "qs", "qt", "qg", "rl", "am", "ap", "ar", "al"] + ["d" + n for n in DMAS]
+A, AF = AluOpType, ActivationFunctionType
+
+
+def rank_program(g, core, T, topo):
+    rank = T.rank_of(core)
+    if rank is None:
+        return
+    ops = []
+    beta = [(rank - 1 - r) % N for r in range(N)]
+
+    def V(n, c0=0, c1=None, s=1, p=(0, 128)):
+        if n in PART:
+            n, c0, c1 = PART[n][0], PART[n][1] + c0, PART[n][1] + (PART[n][2] if c1 is None else c1)
+        if c1 is None:
+            c1 = T[n].shape[1]
+        return {"ap": T[n][p[0]:p[1], c0:c1:s] if s > 1 else T[n][p[0]:p[1], c0:c1], "n": n, "p": p, "c": (c0, c1), "s": s}
+
+    def col(n, c, p=(0, 128)):
+        return V(n, c, c + 1, 1, p)
+
+    def bc(v, d):
+        return dict(v, ap=v["ap"].bitcast(d))
+
+    def ind(w, o):
+        return dict(w, ap=w["ap"].indirect(o["ap"]), off=o)
+
+    def G(q):
+        return (32 * q, 32 * q + 32)
+
+    def op(q, name, args, kw=None, nout=1, sem=None, rd=None):
+        kw = kw or {}
+        w = [a for a in args[:nout]] + [kw[k] for k in kw if k == "accum_out"]
+        r = [a for a in args[nout:] if isinstance(a, dict)] + [kw[k] for k in kw if k != "accum_out" and isinstance(kw[k], dict)] + (rd or [])
+        r = r + [a["off"] for a in w + r if "off" in a]
+        ops.append({"q": q, "name": name, "args": args, "kw": kw, "w": w, "r": r, "sem": sem})
+
+    def ts(o, i, s1, o0, s2=None, o1=None):
+        op("v", "tensor_scalar", [o, i, s1, s2, o0] + ([o1] if s2 is not None else []))
+
+    def tt(o, a, b, f):
+        op("v", "tensor_tensor", [o, a, b, f])
+
+    def cp(o, i):
+        op("v", "tensor_copy", [o, i])
+
+    def act(o, i, f, **kw):
+        op("s", "activation", [o, i, f], kw)
+
+    def scan(o, a, b, init, o0, o1):
+        op("v", "tensor_tensor_scan", [o, a, b, init, o0, o1])
+
+    def tr(o, i):
+        op("v", "transpose", [o, i])
+
+    def red(o, i, f, ab=False):
+        op("v", "tensor_reduce", [o, i, AxisListType.X, f], {"apply_absolute_value": True} if ab else {})
+
+    def ms(o, c):
+        op("v", "memset", [o, c])
+
+    def fill(o, k):
+        act(o, V("io", 1, 1 + -(-(o["c"][1] - o["c"][0]) // o["s"])), AF.Sign, scale=k)
+
+    def iota(o, pat, base, cm):
+        op("g", "iota", [o, pat, base, cm], {} if o["n"] == "pi" else {"allow_small_or_imprecise_dtypes": True})
+
+    def bank(b, c0=0, c1=512):
+        return V("ps", 512 * b + c0, 512 * b + c1)
+
+    def mm(b, st, s0, mv, m0, n):
+        op("t", "matmul_mx", [bank(b, 0, n), V(st + "c", s0, s0 + 128), V(st + "s", s0, s0 + 128), V(mv + "c", m0, m0 + n), V(mv + "s", m0, m0 + n), True, True])
+
+    def quant(n, c0, c1, i):
+        op("v", "quantize_mx", [V(n + "c", c0, c1), V(n + "s", c0, c1), i], nout=2)
+
+    def pick(o, c0, c1, w, off):
+        cp(bc(V(o + "c", c0, c1), dt.uint32), ind(bc(V(w + "c"), dt.uint32), off))
+        act(V(o + "s", c0, c1), ind(V(w + "s"), off), AF.Copy)
+
+    def dma(q, sem, o, i):
+        op(q, "dma_start", [o, i], sem="d" + sem)
+
+    peers = [r for r in range(N) if r != rank]
+    sent = [0]
+
+    def mask_of(r):
+        mask = -1
+        for q in range(N):
+            if q != r:
+                mask &= topo.mask(T.cores[r], T.cores[q])
+        return mask
+
+    def send(src, dst, sem):
+        ids = [DstId(rid=topo.addr(T.cores[r])[0], pnc=topo.addr(T.cores[r])[1]) for r in peers]
+        t = RemoteDMATransfer(dst_ids=ids, dma_engine_mask=mask_of(rank), remote_sem=T.sem[sem], srcs=[src["ap"]], dsts=[dst(r)["ap"] for r in peers])
+        op("g", "remote_dma_fused", [[t]], {"local_sem": T.sem.rl}, nout=0, rd=[src], sem="rl")
+        ops[-1]["to"] = sem
+        sent[0] += bin(mask_of(rank)).count("1")
+
+    def arrive(sem, calls, views):
+        ops.append({"q": "arr", "name": sem, "w": views, "r": [], "sem": sem, "val": calls * sum(bin(mask_of(r)).count("1") for r in peers)})
+
+    (P16, P32, Q0, TAUB, PSC, PBI, NREV, TG, B24, B2, OLC, PAD3, TP, NT, C32, ALC, T16, HALF, GE8, H16) = (
+        0, 1, 4, 5, 6, 7, 8, 9, 14, 15, 16, 18, 21, 23, 24, 27, 32, 34, 35, 36)
+
+    def c(k, p=(0, 128)):
+        return col("cst", k, p)
+
+    dma("y", "x", V("xt"), V("x"))
+    ms(V("ut", 80, 512), 0.0)
+    dma("s", "u", V("ut", 0, 80), V("u", 0, 80))
+    dma("y", "wc", bc(V("wmc"), dt.uint8), V("wc"))
+    dma("y", "ws", V("wms"), V("ws"))
+    iota(V("pi", 0, 1), [[0, 1]], 0, 1)
+    iota(V("io"), [[1, 376]], 0, 0)
+    ms(V("ones"), 1.0)
+    ms(V("ofu", 0, 8), 0)
+    ms(V("ofu", 16, 24), 1)
+    ms(V("ofu", 24, 28), 20)
+    ms(V("ofu", 28, 32), 2)
+    ts(V("pi", 1, 2), V("pi", 0, 1), 15, A.bitwise_and)
+    ts(V("pi", 2, 3), V("pi", 0, 1), 31, A.bitwise_and)
+    cp(V("cst", P16, P16 + 2), V("pi", 1, 3))
+    ms(c(NT), -TINY)
+    for t in range(2):
+        ms(V("e0", 224 * t + 192, 224 * t + 224), 0.0)
+    ts(V("ofu", 8, 16), V("ones", 0, 8), c(P16), A.mult, 2.0, A.add)
+    for t in range(2):
+        op("g", "affine_select", [V("flip0", 224 * t, 224 * t + 224), V("ones", 0, 224), [[1, 224]], A.not_equal, -1.0, -64 * t, -1])
+        ts(col("e0", 224 * t + 192), V("pi", 0, 1), 64.0 * t, A.add, -1.0 / 256, A.mult)
+    iota(V("dg"), [[0, 5], [1, 16]], 0, 0)
+    iota(V("kid", 0, 196), [[48, 4], [1, 49]], 0, 0)
+    iota(V("b49"), [[49, 4], [0, 48]], 0, 0)
+    ts(V("ut", 80, 84), V("ut", 8, 12), -1.0, A.mult)
+    quant("qu", 0, 128, V("ut"))
+    pick("um", 0, 256, "qu", V("ofu", 0, 16))
+    ms(V("hd"), 1.0)
+    ms(V("mk16"), 0)
+    ts(c(HALF), c(P16), 2.0, A.mult, -192.0, A.add)
+    for o in (0, 48):
+        ms(V("hd", o + 1, o + 11), 2.0)
+        ms(V("hd", o, o + 1), 0.0)
+    ts(V("cst", TG, TG + 2), V("io", 0, 2), 32.0, A.mult, c(HALF), A.add)
+    ts(V("cst", TG + 2, TG + 5), V("io", 0, 3), 32.0, A.mult, c(HALF), A.add)
+    ts(V("cst", TG + 2, TG + 5), V("cst", TG + 2, TG + 5), 48.0, A.add)
+    ms(V("vf", 0, 192), -192.0)
+
+    quant("qx", 0, 192, V("xt"))
+    mm(2, "qx", 0, "um", 0, 128)
+    mm(3, "qx", 64, "um", 0, 128)
+    mm(0, "um", 0, "qx", 0, 192)
+    mm(1, "um", 0, "qx", 0, 192)
+    mm(4, "qx", 0, "um", 128, 128)
+    mm(5, "qx", 64, "um", 128, 128)
+    for t in range(2):
+        cp(col("scol", t), bank(2 + t, 0, 1))
+    for t in range(2):
+        act(V("ms", 12 * t, 12 * t + 10), bank(4 + t, 1, 11), AF.Sign, bias=c(NT))
+    for t in range(2):
+        ts(V("e0", 224 * t, 224 * t + 192), bank(0, 0, 192), col("scol", t), A.is_equal)
+        act(V("junk", 192 * t, 192 * t + 192), bank(1, 0, 192), AF.Sign, bias=col("scol", t), scale=-1.0, accum_out=col("gn", t))
+    for t in range(2):
+        scan(V("mcol", 12 * t, 12 * t + 10), V("hd", 1, 11), V("ms", 12 * t, 12 * t + 10), 1.0, A.mult, A.add)
+
+    def src6(b):
+        return (0, b) if b < 4 else (1, b - 2)
+
+    for b in range(6):
+        cp(col("mk16", b, G(rank)), col("mcol", 12 * src6(b)[0] + 9, G(src6(b)[1])))
+    send(V("mk16", 0, 6), lambda r: V("mland", 8 * rank, 8 * rank + 6), "am")
+    for t in range(2):
+        scan(V("v0", 224 * t, 224 * t + 224), V("flip0", 224 * t, 224 * t + 224), V("e0", 224 * t, 224 * t + 224), col("gn", t), A.mult, A.subtract)
+    for t in range(2):
+        tr(V("rr", 32 * t, 32 * t + 32), V("v0", 224 * t + 192, 224 * t + 224))
+
+    def spread(cols):
+        k0, k1 = cols[0], cols[-1] + 1
+        for k in cols:
+            ts(V("su", 64 * k, 64 * k + 64), V("rr"), c(TG + k), A.subtract)
+        for k in cols:
+            red(col("cand", k), V("su", 64 * k, 64 * k + 64), A.min, True)
+        moves = [(2, (0, 64), (64, 128)), (2, (64, 128), (0, 64))] + [(d, G(q), G(q ^ d)) for d in (1, 3) for q in range(4)]
+        for i, (d, to, fr) in enumerate(moves):
+            if i % 2:
+                act(V("cand", 8 * d + k0, 8 * d + k1, 1, to), V("cand", k0, k1, 1, fr), AF.Copy)
+            else:
+                cp(V("cand", 8 * d + k0, 8 * d + k1, 1, to), V("cand", k0, k1, 1, fr))
+        for k in cols:
+            red(col("best", k), V("cand", k, 32, 8), A.min)
+        ts(V("ofi", k0, k1), V("best", k0, k1), 256.0, A.mult)
+
+    def there(n, base, w):
+        def f(r):
+            c0 = base + w * ((r - 1 - rank) % N)
+            return bc(V(n, c0, c0 + w), dt.uint8) if n == "pac" else V(n, c0, c0 + w)
+        return f
+
+    spread([0, 1])
+    pick("sd0", 0, 32, "qx", V("ofi", 0, 2))
+    send(bc(V("sd0c", 0, 24), dt.uint8), there("pac", O0, 24), "ap")
+    send(V("sd0s", 0, 24), there("pas", O0, 24), "ap")
+    spread([2, 3, 4])
+    pick("sd1", 0, 48, "qx", V("ofi", 2, 5))
+    pick("pa", O0 + 72, O1, "qx", V("ofi", 0, 4))
+    for b in range(6):
+        t, q = src6(b)
+        act(V("vf", 32 * b, 32 * b + 32, 1, G(rank)), V("rr", 32 * t, 32 * t + 32, 1, G(q)), AF.Copy)
+    ts(V("vf", 192, 208), V("io", 192, 208), 1.0 / 256, A.mult, -192.0, A.add)
+    ts(V("cst", ALC, ALC + 5), V("io", 0, 5), 16.0, A.mult, c(P16), A.add)
+    cp(V("cst", T16, T16 + 2), V("cst", ALC, ALC + 2))
+    ts(V("cst", H16, H16 + 5), V("cst", ALC, ALC + 5), 0.5, A.add)
+    act(V("cm", 192, 200), V("io", 73, 81), AF.Copy)
+    ts(V("cst", ALC, ALC + 2), V("cst", T16, T16 + 2), -1.0, A.mult)
+    ts(V("fl"), V("vf", 0, 192), -49.0, A.is_lt)
+    ts(V("seg16"), V("dg"), 0.0, A.not_equal)
+    scan(V("cm", 0, 192), V("ones", 0, 192), V("fl"), 0.0, A.mult, A.add)
+    ts(V("dg"), V("dg"), c(P16), A.is_equal)
+    for k in range(5):
+        act(V("junk", 384 + 200 * k, 584 + 200 * k), V("cm"), AF.Sign, bias=c(H16 + k), scale=-1.0, accum_out=col("alf", k))
+    pick("um", 256, 512, "qu", V("ofu", 16, 32))
+    ts(V("alw", 0, 5), V("alf", 0, 5), 0.5, A.mult, 100.0, A.add)
+    cp(V("plr"), ind(V("vf"), V("alw", 0, 5)))
+    tt(V("t192"), V("plr"), V("dg"), A.mult)
+    scan(V("s192"), V("seg16"), V("t192"), 0.0, A.mult, A.add)
+    ts(V("al16", 0, 5), V("s192", 15, 80, 16), 192.0, A.add, 256.0, A.mult)
+    send(V("al16", 0, 5), lambda r: V("aland", 8 * rank, 8 * rank + 5), "al")
+    send(bc(V("sd1c"), dt.uint8), there("pac", O1, 48), "ar")
+    send(V("sd1s"), there("pas", O1, 48), "ar")
+    pick("pa", O1 + 144, PW, "qx", V("ofi", 2, 5))
+
+    ts(V("pi", 3, 4), V("pi", 0, 1), 32, A.bitwise_and)
+    ts(c(Q0), V("pi", 3, 4), 0.0, A.is_gt)
+    for q in range(4):
+        ms(c(B24, G(q)), 24.0 * beta[q])
+    ts(c(B2), c(B24), 112.0, A.add)
+    ms(c(TAUB, (0, 64)), -TINY)
+    ms(c(TAUB, (64, 128)), 0.0)
+    ts(c(PSC), c(P32), 0.5, A.is_gt)
+    ts(c(PBI), c(P32), 10.5, A.is_lt)
+    tt(c(PSC), c(PSC), c(PBI), A.mult)
+    ts(c(44), c(P32), 0.0, A.is_equal)
+    ts(c(PBI), c(PSC), -TINY, A.mult, c(44), A.add)
+    ts(c(NREV), c(P16), -1.0, A.mult, 15.0, A.add)
+    ts(V("cst", C32, C32 + 3), V("io", 0, 3), -32.0, A.mult, c(P32), A.subtract)
+    ts(V("cst", OLC, OLC + 2), V("cst", C32, C32 + 2), -1.0 / 256, A.mult, 256.0, A.add)
+    ts(c(PAD3), c(P32), 7.5, A.is_gt, -1000.0, A.mult)
+    ts(c(GE8), c(P16), 7.5, A.is_gt)
+    ts(c(TP), c(P16), 2.0, A.mult, -72.0, A.add)
+    ts(c(42), c(GE8), 1000.0, A.mult, c(TP), A.add)
+    ts(c(TP + 1), c(42), 32.0, A.add, 500.0, A.min)
+    ts(c(45), c(42), -1016.0, A.add, -500.0, A.max)
+    ts(c(46), c(TP), 16.0, A.add)
+    for q in range(4):
+        if beta[q] % 2:
+            cp(V("cst", TP, TP + 2, 1, G(q)), V("cst", 45, 47, 1, G(q)))
+    iota(V("pv", 96, 98), [[-1000, 2]], 500, 0)
+    for b in range(2):
+        fill(V("rm", EW * b + 66, EW * b + EW), 0.0)
+        fill(V("rm", EW * b, EW * b + 1), 0.0)
+    for b in range(3):
+        act(V("flip3", 104 * b, 104 * b + 104), V("io", 0, 104), AF.Abs, bias=c(C32 + b))
+    for b in range(2):
+        act(V("rm", EW * b + 1, EW * b + 66), V("flip3", 104 * b, 104 * b + 65), AF.Relu, scale=-1.0, bias=1.0)
+        act(V("thr", 64 * b, 64 * b + 64), V("io", 0, 64), AF.Sign, bias=c(C32 + b))
+    ms(c(43), -0.5)
+    act(V("flip3"), V("flip3"), AF.Sign, bias=c(43))
+    act(V("thr"), V("thr"), AF.Relu, scale=0.5)
+    act(V("thr"), V("thr"), AF.Identity, scale=-1.0, bias=-3.0)
+    fill(V("seg48"), 1.0)
+    fill(V("seg48", 0, 192, 48), 0.0)
+    fill(V("tb"), 0.0)
+    for b in range(2):
+        fill(V("ee", EW * b + 336, EW * b + EW), 1.0)
+        fill(V("nn", 96 * b + 64, 96 * b + 96), 0.0)
+    for b in range(3):
+        fill(V("e3", 104 * b + 72, 104 * b + 104), 0.0)
+    ts(V("pbw", 48, 196, 49), V("ones", 0, 4), c(P32), A.mult, 0.0, A.is_equal)
+    fill(V("skw", 48, 196, 49), 0.0)
+    fill(V("zero"), 0.0)
+    fill(V("ya"), 0.0)
+    fill(V("yb"), 0.0)
+    act(V("cm2", 72, 80), V("io", 25, 33), AF.Copy)
+    ms(V("sc", 80, 96), LOW)
+    fill(V("idr", 80, 96), 0.0)
+    fill(V("mk192", 192, 200), 0.0)
+    fill(V("yc", 192, 208), 0.0)
+    ts(V("rv", 64, 96), V("io", 0, 32), 257.0 / 256, A.mult, 0.25, A.add)
+    act(V("r3"), V("io", 0, 208), AF.Identity, bias=-128.0)
+    act(V("r3c"), V("io", 64, 160), AF.Copy)
+    iota(V("dup"), [[16, 12], [0, 2]], 0, 0)
+    ts(V("ofd"), V("dup"), c(P16), A.add)
+    quant("hw", 0, 192, V("xt"))
+    for n in ("par1", "par2"):
+        pick(n, 96, 128, "qx", V("ofi", 0, 2))
+    mm(6, "wm", 0, "qx", 0, 192)
+    act(V("yc", 0, 192), bank(6, 0, 192), AF.Copy)
+
+    arrive("am", 1, [V("mland")])
+    arrive("ap", 2, [V("pac", O0, O0 + 72), V("pas", O0, O0 + 72)])
+    arrive("ar", 2, [V("pac", O1, O1 + 144), V("pas", O1, O1 + 144)])
+    arrive("al", 1, [V("aland")])
+
+    def to_all(o, i, f=None):
+        for q in range(4):
+            if f is None:
+                cp(o(G(q)), i)
+            else:
+                ts(o(G(q)), i, f, A.mult)
+
+    def marks_in():
+        for q in range(4):
+            cp(V("mf", 0, 6, 1, G(q)), V("mk16", 0, 6, 1, G(q)) if q == rank else V("mland", 8 * q, 8 * q + 6, 1, G(q)))
+        for b in range(6):
+            act(V("mb", 32 * b, 32 * b + 32), V("zero", 0, 32), AF.Identity, bias=col("mf", b))
+        tr(V("mk192", 0, 192), V("mb"))
+
+    def state_in():
+        for q in range(4):
+            cp(V("mi", 0, 5, 1, G(q)), V("al16", 0, 5, 1, G(q)) if q == rank else V("aland", 8 * q, 8 * q + 5, 1, G(q)))
+        ts(V("mi", 8, 13), V("mi", 0, 5), 255, A.bitwise_and)
+        ts(V("mi", 16, 21), V("mi", 0, 5), 9, A.logical_shift_right)
+        cp(V("alw", 0, 5), V("mi", 8, 13))
+        ts(V("a5", 0, 5), V("mi", 16, 21), 23.5, A.is_gt, c(B2), A.mult)
+        ts(V("b5", 0, 5), V("mi", 16, 21), c(B24), A.add)
+        tt(V("a5", 0, 5), V("a5", 0, 5), V("b5", 0, 5), A.add)
+        cp(V("idw", 0, 5), V("a5", 0, 5))
+        act(V("mka"), ind(V("mk192"), V("alw", 0, 5)), AF.Copy)
+        act(V("plr"), ind(V("io"), V("alw", 0, 5)), AF.Copy)
+        ts(V("idr", 0, 80), ind(V("io"), V("idw", 0, 5)), float(O0), A.add)
+        act(V("sc", 0, 80), ind(V("scp"), V("idw", 0, 5)), AF.Copy)
+        cp(ind(V("mk192"), V("alw", 0, 5)), V("zero"))
+        ms(V("mk192", 192, 193), 1024.0)
+        cp(V("rem", 0, 200), V("mk192"))
+
+    def opened1(t):
+        if t == 0:
+            ts(V("fl", 0, 72), V("idr", 0, 72), O1 - 0.5, A.is_lt)
+        else:
+            ts(V("fl", 0, 72), V("pv", 0, 72), -25.0, A.is_lt)
+        scan(V("cm2", 0, 72), V("ones", 0, 72), V("fl", 0, 72), 0.0, A.mult, A.add)
+        for k in range(2):
+            act(V("junk", 80 * k, 80 * k + 80), V("cm2"), AF.Sign, bias=c(H16 + k), scale=-1.0, accum_out=col("d2", k))
+
+    def opened2(t):
+        ts(V("olw"), V("d2", 0, 2), 0.5, A.mult, 40.0, A.add)
+        act(V("akw", 64, 96), ind(V("mka"), V("olw")), AF.Identity, scale=-1.0)
+        act(V("aiw", 64, 96), ind(V("idr"), V("olw")), AF.Copy)
+        act(V("asw", 64, 96), ind(V("sc"), V("olw")), AF.Copy)
+        act(V("wr", 0, 32), ind(V("plr"), V("olw")), AF.Copy)
+
+    def opened3(t):
+        cp(ind(V("mka"), V("olw")), V("zero", 0, 32))
+        cp(V("rem", 200, 272), V("mka", 0, 72))
+        if t == R - 1:
+            ts(V("nsr"), V("aiw", 64, 96), 1.0 / 2048, A.mult)
+            tt(V("rv", 64, 96), V("nsr"), V("io", 0, 32), A.add)
+
+    def wrap(t, n):
+        tt(V("d32", 0, n), V("wr", 0, n), V("dg", 0, n), A.mult)
+        scan(V("s64", 0, n), V("seg16", 0, n), V("d32", 0, n), 0.0, A.mult, A.add)
+        to_all(lambda p: V("ol", 4 * t, 4 * t + n // 16, 1, p), V("s64", 15, n, 16, G(rank)))
+
+    def places(t):
+        cp(ind(V("r3"), V("ol", 4 * t, 4 * t + 2)), V("r3c", 32 * t, 32 * t + 32))
+        if t == R - 1:
+            act(V("r3d"), ind(V("r3"), V("ofd")), AF.Copy)
+            for b in range(3):
+                tr(V("r3t", 128 * b, 128 * b + 128), V("r3d", 128 * b, 128 * b + 128))
+            ts(V("of3"), V("r3t", 0, 384, 32), 128.0, A.add)
+
+    def y_mm(t):
+        mm(5, "wm", 0, "hw", 96 + 32 * t, 128)
+        act(V("yn"), bank(5, 96, 128), AF.Copy)
+
+    def y_out(t, q="y"):
+        cp(ind(V("yc"), V("ol", 4 * t, 4 * t + 2)), V("yn"))
+        dma(q, "y%d" % t, V("y", P * t, P * t + P), V("yc", 0, P))
+
+    pools = ("pa", "pb", "pc")
+    for t in range(R):
+        pool, last = pools[t], t == R - 1
+        par, p0 = ("pa", O0) if t == 0 else ("par%d" % t, 0)
+        kt = "kt%d" % t
+        if t == 0:
+            marks_in()
+        for i in range(8):
+            mm(i, "wm", 128 * i, par, p0, 128)
+            if i % 2:
+                act(V(kt, i, 768, 8), bank(i, 0, 96), AF.Relu, scale=C05)
+            else:
+                ts(V(kt, i, 768, 8), bank(i, 0, 96), 0.0, A.max, C05, A.mult)
+        quant(pool, KB[t], KB[t] + 192, V(kt))
+        mm(0, "um", 256, pool, KB[t], 192)
+        mm(1, "um", 384, pool, KB[t], 192)
+        mm(2, "um", 128, pool, KB[t], 192)
+        mm(3, "um", 0, pool, KB[t], 192)
+        if t == 0:
+            mm(4, "um", 0, "pa", O0, 328)
+            dma("y", "cb0", bc(V("pbc", KB[0], PW), dt.uint8), bc(V("pac", KB[0], PW), dt.uint8))
+            dma("y", "cb1", V("pbs", KB[0], PW), V("pas", KB[0], PW))
+        if t == 1:
+            dma("y", "cc0", bc(V("pcc", KB[1], PW), dt.uint8), bc(V("pbc", KB[1], PW), dt.uint8))
+            dma("y", "cc1", V("pcs", KB[1], PW), V("pbs", KB[1], PW))
+        if t > 0:
+            opened3(t)
+            places(t)
+        ts(V("fa"), bank(0, 0, 192), 0.0, A.is_gt, c(Q0), A.is_equal)
+        ts(V("fb"), bank(1, 0, 192), c(TAUB), A.is_gt, -1.0, A.mult)
+        for b in range(4):
+            act(V("pbw", 49 * b, 49 * b + 48), bank(2, 48 * b, 48 * b + 48), AF.Sign, bias=c(PBI), scale=c(PSC))
+        for b in range(4):
+            act(V("skw", 49 * b, 49 * b + 48), bank(3, 48 * b, 48 * b + 48), AF.Copy)
+        if t > 0:
+            y_mm(t - 1)
+        else:
+            act(V("scp"), bank(4, 0, 328), AF.Copy)
+        scan(V("fz"), V("fa"), V("fb"), 0.0, A.max, A.mult)
+        scan(V("cum"), V("seg48"), V("fz"), 0.0, A.mult, A.subtract)
+        ts(V("le"), V("cum"), c(NREV), A.is_le)
+        scan(V("lp"), V("b49"), V("le"), 0.0, A.max, A.add)
+        cp(V("ofe", 0, 4 - rank), V("lp", 48 * rank + 47, 192, 48))
+        if rank:
+            cp(V("ofe", 4 - rank, 4), V("lp", 47, 48 * rank, 48))
+        if t == 0:
+            state_in()
+            opened1(0)
+        cp(V("pab"), ind(V("pbw"), V("ofe")))
+        act(V("asw", 0, 64), ind(V("skw"), V("ofe")), AF.Copy)
+        act(V("aiw", 0, 64), ind(V("kid"), V("ofe")), AF.Identity, bias=float(KB[t]))
+        if t == 0:
+            opened2(0)
+        for b in range(2):
+            tr(V("tb", 48 * b, 48 * b + 32), V("pab", 32 * b, 32 * b + 32))
+        tr(V("at"), V("asw", 0, 64))
+        scan(V("kb"), V("hd"), V("tb"), 0.0, A.mult, A.subtract)
+        for b in range(2):
+            act(V("dd", 64 * b, 64 * b + 64), V("asw", 0, 64), AF.Sign, bias=col("at", 32 * b), scale=-1.0)
+        if t == 0:
+            opened3(0)
+            wrap(0, 32)
+            places(0)
+        for b in range(2):
+            tr(V("akw", 32 * b, 32 * b + 32), V("kb", 48 * b + 16, 48 * b + 48))
+        ts(V("ee", 64, 336), V("rem"), col("kb", 16), A.add, 0.0, A.not_equal)
+        act(V("ee", EW + 64, EW + 336), V("mkall", 0, 272), AF.Abs, bias=col("kb", 64))
+        for b in range(2):
+            ts(V("ee", EW * b, EW * b + 64), V("akw", 0, 64), col("kb", 48 * b + 16), A.not_equal)
+        if t > 0:
+            y_out(t - 1)
+        scan(V("cmpm"), V("dd"), V("thr"), -2.0, A.max, A.add)
+        ts(V("bt"), V("cmpm"), -3.25, A.is_lt, -1.0, A.mult)
+        for b in range(2):
+            scan(V("eo", EW * b, EW * b + EW), V("rm", EW * b, EW * b + EW), V("ee", EW * b, EW * b + EW), 0.0, A.max, A.min)
+        if last:
+            tr(V("ai"), V("aiw", 0, 64))
+            act(V("ib"), V("ai", 0, 64, 32), AF.Identity, scale=1.0 / 2048, bias=256.0)
+        for b in range(2):
+            tr(V("fr", 32 * b, 32 * b + 32), V("eo", EW * b + 336, EW * b + EW))
+        for b in range(2):
+            act(col("ini", b), col("eo", EW * b + 336), AF.Identity, scale=-256.0, bias=col("ib", b) if last else c(OLC + b))
+        for b in range(2):
+            scan(V("nn", 96 * b, 96 * b + 64), V("fr"), V("bt", 64 * b, 64 * b + 64), 0.0, A.max, A.mult)
+        for b in range(2):
+            scan(V("vv", 96 * b, 96 * b + 96), V("ones", 0, 96), V("nn", 96 * b, 96 * b + 96), col("ini", b), A.mult, A.subtract)
+        for b in range(2):
+            tr(V("rv", 32 * b, 32 * b + 32), V("vv", 96 * b + 64, 96 * b + 96))
+        for k in range(2):
+            act(V("su", 96 * k, 96 * k + 96), V("rv"), AF.Abs, bias=c(ALC + k))
+        for k in range(2):
+            red(col("best", k), V("su", 96 * k, 96 * k + 96), A.min)
+        if last:
+            to_all(lambda p: V("oni", 0, 2, 1, p), V("best", 0, 2, 1, G(rank)), 2048.0)
+            pick("hw", 192 + 32 * t, 224 + 32 * t, pool, V("oni"))
+            pick("fin", 0, 192, "hw", V("of3"))
+            y_mm(t)
+            dma("y", "oc", V("oc"), bc(V("finc"), dt.uint8))
+            for k in range(4):
+                dma("sy"[k % 2], "os%d" % k, V("osc", 0, P, 1, (4 * k, 4 * k + 4)), V("fins", 0, P, 1, (32 * k, 32 * k + 4)))
+            y_out(t, "s")
+            break
+        ts(V("idx"), V("best", 0, 2), 256.0, A.mult)
+        cp(V("nsr"), ind(V("asw"), V("idx")))
+        act(V("wr", 32, 64), ind(V("aiw"), V("idx")), AF.Copy)
+        act(V("nkr"), ind(V("akw"), V("idx")), AF.Identity, scale=-1.0)
+        cp(ind(V("sc"), V("olw")), V("nsr"))
+        cp(ind(V("idr"), V("olw")), V("wr", 32, 64))
+        tr(V("tsc"), V("sc"))
+        tr(V("tid"), V("idr"))
+        for b in range(3):
+            ts(V("e3", 104 * b, 104 * b + 72), V("sc", 0, 72), col("tsc", 32 * b), A.is_equal)
+            act(V("junk", 160 + 72 * b, 232 + 72 * b), V("sc", 0, 72), AF.Sign, bias=col("tsc", 32 * b), scale=-1.0, accum_out=col("gn", b))
+        act(V("e3", 72, 208, 104), V("tid", 0, 64, 32), AF.Identity, scale=-1.0 / 2048)
+        act(col("e3", 280), col("tid", 64), AF.Identity, scale=-1.0 / 2048, bias=c(PAD3))
+        for b in range(3):
+            scan(V("v3", 104 * b, 104 * b + 104), V("flip3", 104 * b, 104 * b + 104), V("e3", 104 * b, 104 * b + 104), col("gn", b), A.mult, A.subtract)
+        for b in range(3):
+            tr(V("pv", 32 * b, 32 * b + 32), V("v3", 104 * b + 72, 104 * b + 104))
+        cp(ind(V("mka"), V("olw")), V("nkr"))
+        for k in range(2):
+            act(V("su", 104 * k, 104 * k + 98), V("pv", 0, 98), AF.Abs, scale=-1.0, bias=c(TP + k))
+        for k in range(2):
+            red(col("best", k), V("su", 104 * k, 104 * k + 98), A.min)
+        for q in range(4):
+            c0 = 3 * (beta[q] // 2) + beta[q] % 2
+            o, i = V("yb" if beta[q] % 2 else "ya", c0, c0 + 2, 1, G(0)), V("best", 0, 2, 1, G(q))
+            if q % 2:
+                act(o, i, AF.Identity, scale=2048.0)
+            else:
+                ts(o, i, 2048.0, A.mult)
+        tt(V("y6", 0, 6, 1, G(0)), V("ya", 0, 6, 1, G(0)), V("yb", 0, 6, 1, G(0)), A.add)
+        for q in range(4):
+            cp(V("ofp", 0, 6, 1, G(q)), V("y6", 0, 6, 1, G(0)))
+        pick("par%d" % (t + 1), 0, 96, pool, V("ofp"))
+        opened1(t + 1)
+        opened2(t + 1)
+        wrap(t + 1, 64)
+        pick("hw", 192 + 32 * t, 224 + 32 * t, pool, V("ol", 4 * t + 6, 4 * t + 8))
+
+    emit(g, T, ops, sent[0])
+
+
+def emit(g, T, ops, sent):
+    queue = {"v": g.vector, "s": g.scalar, "t": g.tensor, "g": g, "y": g.sync}
+    size = {F32: 4, I32: 4, X4: 4, BF: 2, U16: 2, U8: 1}
+    seen = {}
+
+    def meet(a, b):
+        if a["n"] == "ps":
+            return a["c"][0] // 512 == b["c"][0] // 512
+        if a["s"] == b["s"] and (a["c"][0] - b["c"][0]) % a["s"]:
+            return False
+        return a["p"][0] < b["p"][1] and b["p"][0] < a["p"][1] and a["c"][0] < b["c"][1] and b["c"][0] < a["c"][1]
+
+    def two(v):
+        return size[SCRATCH[v["n"]][2]] == 2
+
+    def width(v):
+        return 16 * (v["off"]["c"][1] - v["off"]["c"][0]) if "off" in v else -(-(v["c"][1] - v["c"][0]) // v["s"])
+
+    def cost(o):
+        n, a = o["name"], o.get("args")
+        if o["q"] == "arr":
+            return 0, 0
+        if n == "dma_start":
+            v = a[0] if a[0]["n"] in SCRATCH else a[1]
+            return 60, 1900 + width(v) * size[SCRATCH[v["n"]][2]] * 0.6 + (4500 if v["n"] == "wms" else 0)
+        if n == "remote_dma_fused":
+            return 250, 250
+        e = width(a[0])
+        if n == "matmul_mx":
+            d = (e + 16) * 0.63
+        elif n == "quantize_mx":
+            d = 15 + 1.1 * e
+        elif n in ("iota", "affine_select"):
+            d = 150 + 2.1 * e
+        elif "off" in a[0]:
+            d = 50 + 3.6 * e
+        elif len(a) > 1 and isinstance(a[1], dict) and "off" in a[1]:
+            d = 60 + 1.7 * e
+        elif n == "tensor_reduce":
+            d = max(64, width(a[1])) * 1.04
+        elif n == "tensor_tensor":
+            d = max(64, 2 * e) * 1.04
+        else:
+            full = [v for v in a[:3 if n == "tensor_tensor_scan" else 2] if isinstance(v, dict)]
+            d = max(64, e * (0.5 if n != "activation" and all(two(v) for v in full) else 1)) * 1.04
+        return d, d
+
+    last_send, sends = None, {}
+    for i, o in enumerate(ops):
+        q = o["q"]
+        o["i"], o["dep"], o["lag"] = i, set(), {}
+        if q == "arr" or o["name"] == "dma_start":
+            for j, v in enumerate(o["w"]):
+                if v["n"] in SCRATCH:
+                    k = 16 // size[SCRATCH[v["n"]][2]]
+                    o["w"][j] = dict(v, c=(v["c"][0] - v["c"][0] % k, v["c"][1] + -v["c"][1] % k))
+        for kind, views in (("w", o["w"]), ("r", o["r"])):
+            for v in views:
+                for (k2, v2, o2) in seen.get(v["n"], []):
+                    if (kind == "w" or k2 == "w" or (v["n"] == "ps" and o2["q"] != q)) and meet(v, v2):
+                        o["dep"].add(o2["i"])
+        if o["name"] == "remote_dma_fused":
+            if last_send is not None:
+                o["lag"][last_send] = 1500 if ops[last_send]["to"] == "am" else 0
+            last_send = sends[o["to"]] = i
+        if q == "arr":
+            o["lag"][sends[o["sem"]]] = LAND[o["sem"]]
+        for kind, views in (("w", o["w"]), ("r", o["r"])):
+            for v in views:
+                seen.setdefault(v["n"], []).append((kind, v, o))
+        o["busy"], o["took"] = cost(o)
+    for o in ops:
+        o["pre"] = [(d, WAKE) for d in o["dep"]] + list(o["lag"].items())
+        o["rest"] = o["took"] + FIRST.get(o["name"], 0)
+    for o in reversed(ops):
+        for d, lag in o["pre"]:
+            ops[d]["rest"] = max(ops[d]["rest"], ops[d]["took"] + lag + o["rest"] + FIRST.get(ops[d]["name"], 0))
+    busy = {q: [] for q in list(queue) + ["arr"]}
+    for o in sorted(ops, key=lambda e: (-e["rest"], e["i"])):
+        t = max([ops[d]["t"] + ops[d]["took"] + lag for d, lag in o["pre"]] + [0])
+        for a, b in sorted(busy[o["q"]]):
+            if b > t and a < t + o["busy"]:
+                t = b
+        o["t"] = t
+        busy[o["q"]].append((t, t + o["busy"]))
+    count = {}
+    clock = {q: {} for q in queue}
+    for o in sorted(ops, key=lambda e: (e["t"], e["i"])):
+        q = o["q"]
+        if q == "arr":
+            o["key"], o["clk"] = o["sem"], {}
+            count[o["key"]] = o["val"]
+            continue
+        for o2 in sorted([ops[d] for d in o["dep"]], key=lambda e: -e["t"]):
+            key, val = o2["key"], o2["val"]
+            if clock[q].get(key, 0) < val and key != "rl":
+                queue[q].wait_ge(T.sem[key], val)
+                for k2, v2 in list(o2["clk"].items()) + [(key, val)]:
+                    clock[q][k2] = max(clock[q].get(k2, 0), v2)
+        args = [a["ap"] if isinstance(a, dict) else a for a in o["args"]]
+        kw = {k: (a["ap"] if isinstance(a, dict) else a) for k, a in o["kw"].items()}
+        ins = call(queue[q], o["name"], args, kw)
+        o["clk"] = dict(clock[q])
+        if o["name"] == "remote_dma_fused":
+            o["key"], o["val"] = "rl", sent
+        elif o["name"] == "dma_start":
+            o["key"], o["val"] = o["sem"], 16
+            ins.then_inc(T.sem[o["sem"]], 16)
+        else:
+            o["key"] = "q" + q
+            o["val"] = count.get(o["key"], 0) + 1
+            ins.then_inc(T.sem[o["key"]], 1)
+        count[o["key"]] = o["val"]
+    for key, val in count.items():
+        g.wait_ge(T.sem[key], val)
+
+
+def call(q, name, a, kw):
+    if name == "tensor_scalar":
+        return q.tensor_scalar(*a)
+    if name == "tensor_tensor":
+        return q.tensor_tensor(*a)
+    if name == "tensor_copy":
+        return q.tensor_copy(*a)
+    if name == "activation":
+        return q.activation(*a, **kw)
+    if name == "tensor_tensor_scan":
+        return q.tensor_tensor_scan(*a)
+    if name == "transpose":
+        return q.transpose(*a)
+    if name == "tensor_reduce":
+        return q.tensor_reduce(*a, **kw)
+    if name == "memset":
+        return q.memset(*a)
+    if name == "iota":
+        return q.iota(*a, **kw)
+    if name == "affine_select":
+        return q.affine_select(*a)
+    if name == "matmul_mx":
+        return q.matmul_mx(*a)
+    if name == "quantize_mx":
+        return q.quantize_mx(*a)
+    if name == "dma_start":
+        return q.dma_start(*a)
+    return q.remote_dma_fused(*a, **kw)

@@ -9,6 +9,8 @@ C05 = float(np.float32(0.05))
 X4, U8, U16, F32, BF, I32 = "float8_e4m3fn_x4", "uint8", "uint16", "float32", "bfloat16", "int32"
 KB = (392, 200, 8)
 O0, O1, PW = 584, 720, 912
+OL = (4, 0, 6)
+SC = 1.0 / 65536
 EW = 368
 
 SCRATCH = {"ps": ("psum", [128, 4096], F32)}
@@ -23,20 +25,20 @@ for _n, _w in (("qu", 128), ("um", 512), ("qx", 192), ("wm", 1024), ("sd0", 32),
                ("par1", 128), ("par2", 128), ("hw", 288), ("fin", 192)):
     _decl(X4, **{_n + "c": _w})
     _decl(U8, **{_n + "s": _w})
-_decl(BF, xt=768, ut=512, ones=224, flip0=448, e0=448, junk=1400, ms=24, hd=96, kt0=768, kt1=768, kt2=768, fa=192, fb=192, fz=192, cum=192,
-      le=192, lp=192, seg48=192, b49=192, pbw=196, pab=64, tb=96, ee=2 * EW, rm=2 * EW, eo=2 * EW, fr=64, thr=128, dd=128, cmpm=128, bt=128,
+_decl(BF, xt=768, ut=512, ones=224, flip0=448, e0=448, junk=1400, ms=24, hd=336, kt0=768, kt1=768, kt2=768, fa=192, fb=192, fz=192, cum=192,
+      le=192, lp=192, seg48=192, b49=192, pbw=224, tb=336, ee=2 * EW, rm=2 * EW, eo=2 * EW, fr=64, thr=128, dd=128, cmpm=128, bt=128,
       nn=192, fl=192, cm=200, cm2=80, r3=208, r3c=96, r3d=384, r3t=384)
 _decl(F32, io=376, cst=48, sm=88, v0=448, rr=64, su=320, cand=32, mcol=24, vf=208, t192=80, s192=80,
-      dg=80, seg16=80, dup=24, kid=196, mb=192, mkall=280, scp=328, sc=96, idr=96, plr=80, skw=196, asw=96, akw=96, aiw=96, wr=64,
-      at=64, ai=64, kb=96, vv=192, rv=96, nsr=32, nkr=32, tsc=96, tid=96, e3=312, flip3=312, v3=312, pv=104,
-      d32=64, s64=64, yc=208, yn=32, zero=80)
+      dg=96, seg16=96, dup=24, kid=196, mb=192, mkall=280, scp=328, sc=96, idr=96, plr=80, skw=196, asw=96, akw=96, aiw=96, wr=96,
+      at=64, kb=336, kr=224, vv=192, rv=96, nsr=32, nkr=32, tsc=96, tid=96, e3=312, flip3=312, v3=312, pv=104,
+      d32=96, s64=96, yc=208, yn=32, zero=80)
 _decl(U16, ofu=32, ofi=8, mk16=8, al16=8, mland=32, aland=32, alw=6, idw=6, rem=272, ofe=4, idx=2, olw=2, ofp=6, oni=2, ol=12, of3=12, ofd=24)
 _decl(I32, pi=4, mi=24)
 
 PART = {"scol": ("sm", 0, 2), "ini": ("sm", 2, 2), "gn": ("sm", 4, 4), "best": ("sm", 8, 8), "alf": ("sm", 16, 8), "mf": ("sm", 24, 8),
         "ya": ("sm", 32, 6), "d2": ("sm", 40, 4), "b5": ("sm", 48, 8), "a5": ("sm", 56, 8), "yb": ("sm", 64, 6), "y6": ("sm", 72, 6),
         "ib": ("sm", 80, 2), "mk192": ("mkall", 0, 200), "mka": ("mkall", 200, 80)}
-WAKE, LAND, FIRST = 100, {"am": 4500, "ap": 3600, "ar": 4500, "al": 3000}, {"ap": 3000}
+WAKE, LAND, FIRST = 200, {"am": 4500, "ap": 3600, "ar": 4500, "al": 3000}, {"ap": 3000}
 DMAS = ["x", "u", "wc", "ws", "cb0", "cb1", "cc0", "cc1", "y0", "y1", "y2", "oc", "os0", "os1", "os2", "os3"]
 SEMAPHORES = ["qv", "qs", "qt", "qg", "rl", "am", "ap", "ar", "al"] + ["d" + n for n in DMAS]
 A, AF = AluOpType, ActivationFunctionType
@@ -141,8 +143,8 @@ def rank_program(g, core, T, topo):
     def arrive(sem, calls, views):
         ops.append({"q": "arr", "name": sem, "w": views, "r": [], "sem": sem, "val": calls * sum(bin(mask_of(r)).count("1") for r in peers)})
 
-    (P16, P32, Q0, TAUB, PSC, PBI, NREV, TG, B24, B2, OLC, PAD3, TP, NT, C32, ALC, T16, HALF, GE8, H16) = (
-        0, 1, 4, 5, 6, 7, 8, 9, 14, 15, 16, 18, 21, 23, 24, 27, 32, 34, 35, 36)
+    (P16, P32, RCP, EIGHTH, Q0, TAUB, PSC, PBI, NREV, TG, B24, B2, OLC, PAD3, TP, NT, C32, ALC, T16, HALF, GE8, H16) = (
+        0, 1, 2, 3, 4, 5, 6, 7, 8, 9, 14, 15, 16, 18, 21, 23, 24, 27, 32, 34, 35, 36)
 
     def c(k, p=(0, 128)):
         return col("cst", k, p)
@@ -169,7 +171,7 @@ def rank_program(g, core, T, topo):
     for t in range(2):
         op("g", "affine_select", [V("flip0", 224 * t, 224 * t + 224), V("ones", 0, 224), [[1, 224]], A.not_equal, -1.0, -64 * t, -1])
         ts(col("e0", 224 * t + 192), V("pi", 0, 1), 64.0 * t, A.add, -1.0 / 256, A.mult)
-    iota(V("dg"), [[0, 5], [1, 16]], 0, 0)
+    iota(V("dg"), [[0, 6], [1, 16]], 0, 0)
     iota(V("kid", 0, 196), [[48, 4], [1, 49]], 0, 0)
     iota(V("b49"), [[49, 4], [0, 48]], 0, 0)
     ts(V("ut", 80, 84), V("ut", 8, 12), -1.0, A.mult)
@@ -178,9 +180,10 @@ def rank_program(g, core, T, topo):
     ms(V("hd"), 1.0)
     ms(V("mk16"), 0)
     ts(c(HALF), c(P16), 2.0, A.mult, -192.0, A.add)
-    for o in (0, 48):
-        ms(V("hd", o + 1, o + 11), 2.0)
-        ms(V("hd", o, o + 1), 0.0)
+    ms(V("hd", 1, 11), 2.0)
+    ms(V("hd", 0, 336, 48), 0.0)
+    for o in range(48, 336, 48):
+        act(V("hd", o + 1, o + 11), V("hd", 1, 11), AF.Copy)
     ts(V("cst", TG, TG + 2), V("io", 0, 2), 32.0, A.mult, c(HALF), A.add)
     ts(V("cst", TG + 2, TG + 5), V("io", 0, 3), 32.0, A.mult, c(HALF), A.add)
     ts(V("cst", TG + 2, TG + 5), V("cst", TG + 2, TG + 5), 48.0, A.add)
@@ -207,7 +210,8 @@ def rank_program(g, core, T, topo):
         return (0, b) if b < 4 else (1, b - 2)
 
     for b in range(6):
-        cp(col("mk16", b, G(rank)), col("mcol", 12 * src6(b)[0] + 9, G(src6(b)[1])))
+        act(col("mf", b, G(rank)), col("mcol", 12 * src6(b)[0] + 9, G(src6(b)[1])), AF.Copy)
+    cp(V("mk16", 0, 6, 1, G(rank)), V("mf", 0, 6, 1, G(rank)))
     send(V("mk16", 0, 6), lambda r: V("mland", 8 * rank, 8 * rank + 6), "am")
     for t in range(2):
         scan(V("v0", 224 * t, 224 * t + 224), V("flip0", 224 * t, 224 * t + 224), V("e0", 224 * t, 224 * t + 224), col("gn", t), A.mult, A.subtract)
@@ -261,8 +265,8 @@ def rank_program(g, core, T, topo):
     pick("um", 256, 512, "qu", V("ofu", 16, 32))
     ts(V("alw", 0, 5), V("alf", 0, 5), 0.5, A.mult, 100.0, A.add)
     cp(V("plr"), ind(V("vf"), V("alw", 0, 5)))
-    tt(V("t192"), V("plr"), V("dg"), A.mult)
-    scan(V("s192"), V("seg16"), V("t192"), 0.0, A.mult, A.add)
+    tt(V("t192"), V("plr"), V("dg", 0, 80), A.mult)
+    scan(V("s192"), V("seg16", 0, 80), V("t192"), 0.0, A.mult, A.add)
     ts(V("al16", 0, 5), V("s192", 15, 80, 16), 192.0, A.add, 256.0, A.mult)
     send(V("al16", 0, 5), lambda r: V("aland", 8 * rank, 8 * rank + 5), "al")
     send(bc(V("sd1c"), dt.uint8), there("pac", O1, 48), "ar")
@@ -284,7 +288,7 @@ def rank_program(g, core, T, topo):
     ts(c(NREV), c(P16), -1.0, A.mult, 15.0, A.add)
     ts(V("cst", C32, C32 + 3), V("io", 0, 3), -32.0, A.mult, c(P32), A.subtract)
     ts(V("cst", OLC, OLC + 2), V("cst", C32, C32 + 2), -1.0 / 256, A.mult, 256.0, A.add)
-    ts(c(PAD3), c(P32), 7.5, A.is_gt, -1000.0, A.mult)
+    ts(c(PAD3), c(P32), 7.5, A.is_lt)
     ts(c(GE8), c(P16), 7.5, A.is_gt)
     ts(c(TP), c(P16), 2.0, A.mult, -72.0, A.add)
     ts(c(42), c(GE8), 1000.0, A.mult, c(TP), A.add)
@@ -305,6 +309,10 @@ def rank_program(g, core, T, topo):
         act(V("thr", 64 * b, 64 * b + 64), V("io", 0, 64), AF.Sign, bias=c(C32 + b))
     ms(c(43), -0.5)
     act(V("flip3"), V("flip3"), AF.Sign, bias=c(43))
+    act(V("flip3", 208, 312), V("flip3", 208, 312), AF.Identity, scale=c(PAD3))
+    ts(c(47), c(P32), 1.0, A.add, SC, A.mult)
+    op("v", "reciprocal", [c(RCP), c(47)])
+    ms(c(EIGHTH), 0.125)
     act(V("thr"), V("thr"), AF.Relu, scale=0.5)
     act(V("thr"), V("thr"), AF.Identity, scale=-1.0, bias=-3.0)
     fill(V("seg48"), 1.0)
@@ -313,10 +321,9 @@ def rank_program(g, core, T, topo):
     for b in range(2):
         fill(V("ee", EW * b + 336, EW * b + EW), 1.0)
         fill(V("nn", 96 * b + 64, 96 * b + 96), 0.0)
-    for b in range(3):
-        fill(V("e3", 104 * b + 72, 104 * b + 104), 0.0)
     ts(V("pbw", 48, 196, 49), V("ones", 0, 4), c(P32), A.mult, 0.0, A.is_equal)
     fill(V("skw", 48, 196, 49), 0.0)
+    fill(V("pbw", 196, 224), 0.0)
     fill(V("zero"), 0.0)
     fill(V("ya"), 0.0)
     fill(V("yb"), 0.0)
@@ -341,16 +348,13 @@ def rank_program(g, core, T, topo):
     arrive("ar", 2, [V("pac", O1, O1 + 144), V("pas", O1, O1 + 144)])
     arrive("al", 1, [V("aland")])
 
-    def to_all(o, i, f=None):
+    def to_all(o, i, f):
         for q in range(4):
-            if f is None:
-                cp(o(G(q)), i)
-            else:
-                ts(o(G(q)), i, f, A.mult)
+            ts(o(G(q)), i, f, A.mult)
 
     def marks_in():
-        for q in range(4):
-            cp(V("mf", 0, 6, 1, G(q)), V("mk16", 0, 6, 1, G(q)) if q == rank else V("mland", 8 * q, 8 * q + 6, 1, G(q)))
+        for q in peers:
+            cp(V("mf", 0, 6, 1, G(q)), V("mland", 8 * q, 8 * q + 6, 1, G(q)))
         for b in range(6):
             act(V("mb", 32 * b, 32 * b + 32), V("zero", 0, 32), AF.Identity, bias=col("mf", b))
         tr(V("mk192", 0, 192), V("mb"))
@@ -366,8 +370,8 @@ def rank_program(g, core, T, topo):
         tt(V("a5", 0, 5), V("a5", 0, 5), V("b5", 0, 5), A.add)
         cp(V("idw", 0, 5), V("a5", 0, 5))
         act(V("mka"), ind(V("mk192"), V("alw", 0, 5)), AF.Copy)
-        act(V("plr"), ind(V("io"), V("alw", 0, 5)), AF.Copy)
-        ts(V("idr", 0, 80), ind(V("io"), V("idw", 0, 5)), float(O0), A.add)
+        act(V("plr"), ind(V("io"), V("alw", 0, 5)), AF.Identity, scale=-SC)
+        act(V("idr", 0, 80), ind(V("io"), V("idw", 0, 5)), AF.Identity, scale=-SC, bias=-O0 * SC)
         act(V("sc", 0, 80), ind(V("scp"), V("idw", 0, 5)), AF.Copy)
         cp(ind(V("mk192"), V("alw", 0, 5)), V("zero"))
         ms(V("mk192", 192, 193), 1024.0)
@@ -375,7 +379,7 @@ def rank_program(g, core, T, topo):
 
     def opened1(t):
         if t == 0:
-            ts(V("fl", 0, 72), V("idr", 0, 72), O1 - 0.5, A.is_lt)
+            ts(V("fl", 0, 72), V("idr", 0, 72), (0.5 - O1) * SC, A.is_gt)
         else:
             ts(V("fl", 0, 72), V("pv", 0, 72), -25.0, A.is_lt)
         scan(V("cm2", 0, 72), V("ones", 0, 72), V("fl", 0, 72), 0.0, A.mult, A.add)
@@ -387,22 +391,23 @@ def rank_program(g, core, T, topo):
         act(V("akw", 64, 96), ind(V("mka"), V("olw")), AF.Identity, scale=-1.0)
         act(V("aiw", 64, 96), ind(V("idr"), V("olw")), AF.Copy)
         act(V("asw", 64, 96), ind(V("sc"), V("olw")), AF.Copy)
-        act(V("wr", 0, 32), ind(V("plr"), V("olw")), AF.Copy)
+        act(V("wr", 0, 32) if t else V("wr", 64, 96), ind(V("plr"), V("olw")), AF.Copy)
 
     def opened3(t):
         cp(ind(V("mka"), V("olw")), V("zero", 0, 32))
-        cp(V("rem", 200, 272), V("mka", 0, 72))
+        if t:
+            cp(V("rem", 200, 272), V("mka", 0, 72))
         if t == R - 1:
-            ts(V("nsr"), V("aiw", 64, 96), 1.0 / 2048, A.mult)
+            ts(V("nsr"), V("aiw", 64, 96), -32.0, A.mult)
             tt(V("rv", 64, 96), V("nsr"), V("io", 0, 32), A.add)
 
     def wrap(t, n):
         tt(V("d32", 0, n), V("wr", 0, n), V("dg", 0, n), A.mult)
         scan(V("s64", 0, n), V("seg16", 0, n), V("d32", 0, n), 0.0, A.mult, A.add)
-        to_all(lambda p: V("ol", 4 * t, 4 * t + n // 16, 1, p), V("s64", 15, n, 16, G(rank)))
+        to_all(lambda p: V("ol", 6 * t - 6, 6 * t - 6 + n // 16, 1, p), V("s64", 15, n, 16, G(rank)), -65536.0)
 
     def places(t):
-        cp(ind(V("r3"), V("ol", 4 * t, 4 * t + 2)), V("r3c", 32 * t, 32 * t + 32))
+        cp(ind(V("r3"), V("ol", OL[t], OL[t] + 2)), V("r3c", 32 * t, 32 * t + 32))
         if t == R - 1:
             act(V("r3d"), ind(V("r3"), V("ofd")), AF.Copy)
             for b in range(3):
@@ -414,7 +419,7 @@ def rank_program(g, core, T, topo):
         act(V("yn"), bank(5, 96, 128), AF.Copy)
 
     def y_out(t, q="y"):
-        cp(ind(V("yc"), V("ol", 4 * t, 4 * t + 2)), V("yn"))
+        cp(ind(V("yc"), V("ol", OL[t], OL[t] + 2)), V("yn"))
         dma(q, "y%d" % t, V("y", P * t, P * t + P), V("yc", 0, P))
 
     pools = ("pa", "pb", "pc")
@@ -449,6 +454,12 @@ def rank_program(g, core, T, topo):
         ts(V("fb"), bank(1, 0, 192), c(TAUB), A.is_gt, -1.0, A.mult)
         for b in range(4):
             act(V("pbw", 49 * b, 49 * b + 48), bank(2, 48 * b, 48 * b + 48), AF.Sign, bias=c(PBI), scale=c(PSC))
+        for b in range(7):
+            tr(V("tb", 48 * b, 48 * b + 32), V("pbw", 32 * b, 32 * b + 32))
+        scan(V("kb", 0, 192), V("hd", 0, 192), V("tb", 0, 192), 0.0, A.mult, A.subtract)
+        scan(V("kb", 192, 336), V("hd", 192, 336), V("tb", 192, 336), 0.0, A.mult, A.subtract)
+        for b in range(7):
+            tr(V("kr", 32 * b, 32 * b + 32), V("kb", 48 * b + 16, 48 * b + 48))
         for b in range(4):
             act(V("skw", 49 * b, 49 * b + 48), bank(3, 48 * b, 48 * b + 48), AF.Copy)
         if t > 0:
@@ -465,27 +476,21 @@ def rank_program(g, core, T, topo):
         if t == 0:
             state_in()
             opened1(0)
-        cp(V("pab"), ind(V("pbw"), V("ofe")))
+        cp(V("akw", 0, 64), ind(V("kr"), V("ofe")))
         act(V("asw", 0, 64), ind(V("skw"), V("ofe")), AF.Copy)
-        act(V("aiw", 0, 64), ind(V("kid"), V("ofe")), AF.Identity, bias=float(KB[t]))
+        act(V("aiw", 0, 64), ind(V("kid"), V("ofe")), AF.Identity, scale=-SC, bias=-KB[t] * SC)
         if t == 0:
             opened2(0)
-        for b in range(2):
-            tr(V("tb", 48 * b, 48 * b + 32), V("pab", 32 * b, 32 * b + 32))
+        tr(V("d32", 0, 64), V("akw", 0, 64))
         tr(V("at"), V("asw", 0, 64))
-        scan(V("kb"), V("hd"), V("tb"), 0.0, A.mult, A.subtract)
         for b in range(2):
             act(V("dd", 64 * b, 64 * b + 64), V("asw", 0, 64), AF.Sign, bias=col("at", 32 * b), scale=-1.0)
         if t == 0:
             opened3(0)
-            wrap(0, 32)
-            places(0)
+        ts(V("ee", 64, 336), V("rem") if t else V("mkall", 0, 272), col("d32", 0), A.add, 0.0, A.not_equal)
+        act(V("ee", EW + 64, EW + 336), V("mkall", 0, 272), AF.Abs, bias=col("d32", 32))
         for b in range(2):
-            tr(V("akw", 32 * b, 32 * b + 32), V("kb", 48 * b + 16, 48 * b + 48))
-        ts(V("ee", 64, 336), V("rem"), col("kb", 16), A.add, 0.0, A.not_equal)
-        act(V("ee", EW + 64, EW + 336), V("mkall", 0, 272), AF.Abs, bias=col("kb", 64))
-        for b in range(2):
-            ts(V("ee", EW * b, EW * b + 64), V("akw", 0, 64), col("kb", 48 * b + 16), A.not_equal)
+            ts(V("ee", EW * b, EW * b + 64), V("akw", 0, 64), col("d32", 32 * b), A.not_equal)
         if t > 0:
             y_out(t - 1)
         scan(V("cmpm"), V("dd"), V("thr"), -2.0, A.max, A.add)
@@ -493,8 +498,8 @@ def rank_program(g, core, T, topo):
         for b in range(2):
             scan(V("eo", EW * b, EW * b + EW), V("rm", EW * b, EW * b + EW), V("ee", EW * b, EW * b + EW), 0.0, A.max, A.min)
         if last:
-            tr(V("ai"), V("aiw", 0, 64))
-            act(V("ib"), V("ai", 0, 64, 32), AF.Identity, scale=1.0 / 2048, bias=256.0)
+            tr(V("tid", 0, 64), V("aiw", 0, 64))
+            act(V("ib"), V("tid", 0, 64, 32), AF.Identity, scale=-32.0, bias=256.0)
         for b in range(2):
             tr(V("fr", 32 * b, 32 * b + 32), V("eo", EW * b + 336, EW * b + EW))
         for b in range(2):
@@ -526,12 +531,11 @@ def rank_program(g, core, T, topo):
         cp(ind(V("sc"), V("olw")), V("nsr"))
         cp(ind(V("idr"), V("olw")), V("wr", 32, 64))
         tr(V("tsc"), V("sc"))
-        tr(V("tid"), V("idr"))
+        for b in range(3):
+            tr(V("e3", 104 * b + 72, 104 * b + 104), V("idr", 32 * b, 32 * b + 32))
         for b in range(3):
             ts(V("e3", 104 * b, 104 * b + 72), V("sc", 0, 72), col("tsc", 32 * b), A.is_equal)
             act(V("junk", 160 + 72 * b, 232 + 72 * b), V("sc", 0, 72), AF.Sign, bias=col("tsc", 32 * b), scale=-1.0, accum_out=col("gn", b))
-        act(V("e3", 72, 208, 104), V("tid", 0, 64, 32), AF.Identity, scale=-1.0 / 2048)
-        act(col("e3", 280), col("tid", 64), AF.Identity, scale=-1.0 / 2048, bias=c(PAD3))
         for b in range(3):
             scan(V("v3", 104 * b, 104 * b + 104), V("flip3", 104 * b, 104 * b + 104), V("e3", 104 * b, 104 * b + 104), col("gn", b), A.mult, A.subtract)
         for b in range(3):
@@ -545,17 +549,19 @@ def rank_program(g, core, T, topo):
             c0 = 3 * (beta[q] // 2) + beta[q] % 2
             o, i = V("yb" if beta[q] % 2 else "ya", c0, c0 + 2, 1, G(0)), V("best", 0, 2, 1, G(q))
             if q % 2:
-                act(o, i, AF.Identity, scale=2048.0)
+                act(o, i, AF.Identity, scale=c(RCP, G(q)), bias=c(EIGHTH, G(q)))
             else:
-                ts(o, i, 2048.0, A.mult)
+                ts(o, i, c(RCP, G(q)), A.mult, 0.125, A.add)
         tt(V("y6", 0, 6, 1, G(0)), V("ya", 0, 6, 1, G(0)), V("yb", 0, 6, 1, G(0)), A.add)
         for q in range(4):
             cp(V("ofp", 0, 6, 1, G(q)), V("y6", 0, 6, 1, G(0)))
         pick("par%d" % (t + 1), 0, 96, pool, V("ofp"))
         opened1(t + 1)
         opened2(t + 1)
-        wrap(t + 1, 64)
-        pick("hw", 192 + 32 * t, 224 + 32 * t, pool, V("ol", 4 * t + 6, 4 * t + 8))
+        wrap(t + 1, 64 if t else 96)
+        if t == 0:
+            places(0)
+        pick("hw", 192 + 32 * t, 224 + 32 * t, pool, V("ol", 6 * t + 2, 6 * t + 4))
 
     emit(g, T, ops, sent[0])
 
@@ -592,6 +598,8 @@ def emit(g, T, ops, sent):
             d = (e + 16) * 0.63
         elif n == "quantize_mx":
             d = 15 + 1.1 * e
+        elif n == "reciprocal":
+            d = 200
         elif n in ("iota", "affine_select"):
             d = 150 + 2.1 * e
         elif "off" in a[0]:
@@ -692,6 +700,8 @@ def call(q, name, a, kw):
         return q.transpose(*a)
     if name == "tensor_reduce":
         return q.tensor_reduce(*a, **kw)
+    if name == "reciprocal":
+        return q.reciprocal(*a)
     if name == "memset":
         return q.memset(*a)
     if name == "iota":

@@ -21,18 +21,18 @@ def _decl(dtype, **kw):
         SCRATCH[k] = ("sbuf", [128, n], dtype)
 
 
-for _n, _w in (("qu", 128), ("um", 512), ("qx", 192), ("wm", 1024), ("sd0", 32), ("sd1", 48), ("pa", PW), ("pb", PW), ("pc", PW),
+for _n, _w in (("qu", 128), ("um", 512), ("qx", 224), ("qn", 128), ("wm", 1024), ("sd0", 32), ("sd1", 48), ("pa", PW), ("pb", PW), ("pc", PW),
                ("par1", 128), ("par2", 128), ("hw", 288), ("fin", 192)):
     _decl(X4, **{_n + "c": _w})
     _decl(U8, **{_n + "s": _w})
-_decl(BF, xt=768, ut=512, ones=224, flip0=448, e0=448, junk=1400, ms=24, hd=336, kt0=768, kt1=768, kt2=768, fa=192, fb=192, fz=192, cum=192,
-      le=192, lp=192, seg48=192, b49=192, pbw=224, tb=336, ee=2 * EW, rm=2 * EW, eo=2 * EW, fr=64, thr=128, dd=128, cmpm=128, bt=128,
-      nn=192, fl=192, cm=200, cm2=80, r3=208, r3c=96, r3d=384, r3t=384)
+_decl(BF, xt=896, ut=1024, ones=224, flip0=448, e0=448, junk=1400, ms=24, hd=336, kt0=768, kt1=768, kt2=768, fa=192, fb=192, fz=192, cum=192,
+      le=192, seg48=192, pbw=224, tb=336, ee=2 * EW, rm=2 * EW, eo=2 * EW, fr=64, thr=128, dd=128, cmpm=128, bt=128,
+      nn=256, fl=192, cm=200, cm2=80, r3=208, r3c=96, r3d=384, r3t=384)
 _decl(F32, io=376, cst=48, sm=88, v0=448, rr=64, su=320, cand=32, mcol=24, vf=208, t192=80, s192=80,
-      dg=96, seg16=96, dup=24, kid=196, mb=192, mkall=280, scp=328, sc=96, idr=96, plr=80, skw=196, asw=96, akw=96, aiw=96, wr=96,
-      at=64, kb=336, kr=224, vv=192, rv=96, nsr=32, nkr=32, tsc=96, tid=96, e3=312, flip3=312, v3=312, pv=104,
-      d32=96, s64=96, yc=208, yn=32, zero=80)
-_decl(U16, ofu=32, ofi=8, mk16=8, al16=8, mland=32, aland=32, alw=6, idw=6, rem=272, ofe=4, idx=2, olw=2, ofp=6, oni=2, ol=12, of3=12, ofd=24)
+      dg=96, seg16=96, kid=196, mb=192, mkall=280, scp=328, sc=96, idr=96, plr=80, skw=196, asw=96, akw=96, aiw=96, wr=96,
+      at=64, kb=336, kr=224, vv=256, rv=192, nsr=32, nkr=32, tsc=96, tid=96, e3=312, flip3=312, v3=312, pv=104,
+      d32=96, s64=96, yc=208, yn=32, yp=PW, zero=80)
+_decl(U16, ofu=32, ofi=8, mk16=8, al16=8, mland=32, aland=32, alw=12, idw=6, rem=272, ofe=4, idx=2, olw=2, ofp=6, ol=12, of3=12, ofd=24)
 _decl(I32, pi=4, mi=24)
 
 PART = {"scol": ("sm", 0, 2), "ini": ("sm", 2, 2), "gn": ("sm", 4, 4), "best": ("sm", 8, 8), "alf": ("sm", 16, 8), "mf": ("sm", 24, 8),
@@ -149,7 +149,8 @@ def rank_program(g, core, T, topo):
     def c(k, p=(0, 128)):
         return col("cst", k, p)
 
-    dma("y", "x", V("xt"), V("x"))
+    dma("y", "x", V("xt", 0, 768), V("x"))
+    ms(V("xt", 768, 896), 0.0)
     ms(V("ut", 80, 512), 0.0)
     dma("s", "u", V("ut", 0, 80), V("u", 0, 80))
     dma("y", "wc", bc(V("wmc"), dt.uint8), V("wc"))
@@ -169,14 +170,16 @@ def rank_program(g, core, T, topo):
         ms(V("e0", 224 * t + 192, 224 * t + 224), 0.0)
     ts(V("ofu", 8, 16), V("ones", 0, 8), c(P16), A.mult, 2.0, A.add)
     for t in range(2):
-        op("g", "affine_select", [V("flip0", 224 * t, 224 * t + 224), V("ones", 0, 224), [[1, 224]], A.not_equal, -1.0, -64 * t, -1])
-        ts(col("e0", 224 * t + 192), V("pi", 0, 1), 64.0 * t, A.add, -1.0 / 256, A.mult)
+        op("g", "affine_select", [V("flip0", 224 * t, 224 * t + 224), V("ones", 0, 224), [[1, 224]], A.not_equal, -1.0, -96 * t, -1])
+        ts(col("e0", 224 * t + 192), V("pi", 0, 1), 96.0 * t, A.add, -1.0 / 256, A.mult)
     iota(V("dg"), [[0, 6], [1, 16]], 0, 0)
     iota(V("kid", 0, 196), [[48, 4], [1, 49]], 0, 0)
-    iota(V("b49"), [[49, 4], [0, 48]], 0, 0)
-    ts(V("ut", 80, 84), V("ut", 8, 12), -1.0, A.mult)
-    quant("qu", 0, 128, V("ut"))
-    pick("um", 0, 256, "qu", V("ofu", 0, 16))
+    quant("qu", 0, 128, V("ut", 0, 512))
+    pick("um", 0, 128, "qu", V("ofu", 0, 8))
+    pick("um", 128, 256, "qu", V("ofu", 8, 16))
+    act(V("ut", 512, 1024), V("ut", 0, 512), AF.Copy)
+    ts(V("ut", 592, 596), V("ut", 8, 12), -1.0, A.mult)
+    quant("qn", 0, 128, V("ut", 512, 1024))
     ms(V("hd"), 1.0)
     ms(V("mk16"), 0)
     ts(c(HALF), c(P16), 2.0, A.mult, -192.0, A.add)
@@ -189,13 +192,13 @@ def rank_program(g, core, T, topo):
     ts(V("cst", TG + 2, TG + 5), V("cst", TG + 2, TG + 5), 48.0, A.add)
     ms(V("vf", 0, 192), -192.0)
 
-    quant("qx", 0, 192, V("xt"))
+    quant("qx", 0, 224, V("xt"))
     mm(2, "qx", 0, "um", 0, 128)
-    mm(3, "qx", 64, "um", 0, 128)
+    mm(3, "qx", 96, "um", 0, 128)
     mm(0, "um", 0, "qx", 0, 192)
     mm(1, "um", 0, "qx", 0, 192)
     mm(4, "qx", 0, "um", 128, 128)
-    mm(5, "qx", 64, "um", 128, 128)
+    mm(5, "qx", 96, "um", 128, 128)
     for t in range(2):
         cp(col("scol", t), bank(2 + t, 0, 1))
     for t in range(2):
@@ -207,7 +210,7 @@ def rank_program(g, core, T, topo):
         scan(V("mcol", 12 * t, 12 * t + 10), V("hd", 1, 11), V("ms", 12 * t, 12 * t + 10), 1.0, A.mult, A.add)
 
     def src6(b):
-        return (0, b) if b < 4 else (1, b - 2)
+        return (b // 3, b % 3)
 
     for b in range(6):
         act(col("mf", b, G(rank)), col("mcol", 12 * src6(b)[0] + 9, G(src6(b)[1])), AF.Copy)
@@ -221,18 +224,18 @@ def rank_program(g, core, T, topo):
     def spread(cols):
         k0, k1 = cols[0], cols[-1] + 1
         for k in cols:
-            ts(V("su", 64 * k, 64 * k + 64), V("rr"), c(TG + k), A.subtract)
+            ts(V("su", 64 * k, 64 * k + 64), V("rr"), c(TG + k), A.subtract, 256.0, A.mult)
         for k in cols:
-            red(col("cand", k), V("su", 64 * k, 64 * k + 64), A.min, True)
-        moves = [(2, (0, 64), (64, 128)), (2, (64, 128), (0, 64))] + [(d, G(q), G(q ^ d)) for d in (1, 3) for q in range(4)]
+            red(col("cand", k, (0, 96)), V("su", 64 * k, 64 * k + 64, 1, (0, 96)), A.min, True)
+        moves = [(1, (64, 128), (0, 64)), (1, G(0), G(1)), (1, G(1), G(0)), (2, G(0), G(2)), (2, G(1), G(2)), (2, G(2), G(1)), (2, G(3), G(0)),
+                 (0, G(3), G(2))]
         for i, (d, to, fr) in enumerate(moves):
             if i % 2:
                 act(V("cand", 8 * d + k0, 8 * d + k1, 1, to), V("cand", k0, k1, 1, fr), AF.Copy)
             else:
                 cp(V("cand", 8 * d + k0, 8 * d + k1, 1, to), V("cand", k0, k1, 1, fr))
         for k in cols:
-            red(col("best", k), V("cand", k, 32, 8), A.min)
-        ts(V("ofi", k0, k1), V("best", k0, k1), 256.0, A.mult)
+            ts(col("ofi", k), col("cand", k), col("cand", 8 + k), A.min, col("cand", 16 + k), A.min)
 
     def there(n, base, w):
         def f(r):
@@ -262,7 +265,7 @@ def rank_program(g, core, T, topo):
     ts(V("dg"), V("dg"), c(P16), A.is_equal)
     for k in range(5):
         act(V("junk", 384 + 200 * k, 584 + 200 * k), V("cm"), AF.Sign, bias=c(H16 + k), scale=-1.0, accum_out=col("alf", k))
-    pick("um", 256, 512, "qu", V("ofu", 16, 32))
+    pick("um", 256, 512, "qn", V("ofu", 16, 32))
     ts(V("alw", 0, 5), V("alf", 0, 5), 0.5, A.mult, 100.0, A.add)
     cp(V("plr"), ind(V("vf"), V("alw", 0, 5)))
     tt(V("t192"), V("plr"), V("dg", 0, 80), A.mult)
@@ -285,7 +288,7 @@ def rank_program(g, core, T, topo):
     tt(c(PSC), c(PSC), c(PBI), A.mult)
     ts(c(44), c(P32), 0.0, A.is_equal)
     ts(c(PBI), c(PSC), -TINY, A.mult, c(44), A.add)
-    ts(c(NREV), c(P16), -1.0, A.mult, 15.0, A.add)
+    ts(c(NREV), c(P16), -1.0, A.mult, 15.5, A.add)
     ts(V("cst", C32, C32 + 3), V("io", 0, 3), -32.0, A.mult, c(P32), A.subtract)
     ts(V("cst", OLC, OLC + 2), V("cst", C32, C32 + 2), -1.0 / 256, A.mult, 256.0, A.add)
     ts(c(PAD3), c(P32), 7.5, A.is_lt)
@@ -320,11 +323,15 @@ def rank_program(g, core, T, topo):
     fill(V("tb"), 0.0)
     for b in range(2):
         fill(V("ee", EW * b + 336, EW * b + EW), 1.0)
-        fill(V("nn", 96 * b + 64, 96 * b + 96), 0.0)
+        fill(V("nn", 128 * b + 65, 128 * b + 128), 1.0)
+        fill(V("nn", 128 * b + 64, 128 * b + 65), 0.0)
+        ms(V("nn", 128 * b + 80, 128 * b + 128, 32), -15.0)
     ts(V("pbw", 48, 196, 49), V("ones", 0, 4), c(P32), A.mult, 0.0, A.is_equal)
     fill(V("skw", 48, 196, 49), 0.0)
     fill(V("pbw", 196, 224), 0.0)
     fill(V("zero"), 0.0)
+    fill(V("yp", 0, 200), 0.0)
+    fill(V("yp", 200, 392), 0.0)
     fill(V("ya"), 0.0)
     fill(V("yb"), 0.0)
     act(V("cm2", 72, 80), V("io", 25, 33), AF.Copy)
@@ -332,12 +339,14 @@ def rank_program(g, core, T, topo):
     fill(V("idr", 80, 96), 0.0)
     fill(V("mk192", 192, 200), 0.0)
     fill(V("yc", 192, 208), 0.0)
-    ts(V("rv", 64, 96), V("io", 0, 32), 257.0 / 256, A.mult, 0.25, A.add)
+    ts(V("cst", ALC + 2, ALC + 4), V("cst", ALC, ALC + 2), 0.25, A.add)
+    for k in range(2):
+        ts(V("rv", 96 * k + 64, 96 * k + 96), V("io", 0, 32), 257.0 / 256, A.mult, c(ALC + 2 + k), A.add)
     act(V("r3"), V("io", 0, 208), AF.Identity, bias=-128.0)
     act(V("r3c"), V("io", 64, 160), AF.Copy)
-    iota(V("dup"), [[16, 12], [0, 2]], 0, 0)
-    ts(V("ofd"), V("dup"), c(P16), A.add)
-    quant("hw", 0, 192, V("xt"))
+    iota(V("t192", 0, 24), [[16, 12], [0, 2]], 0, 0)
+    ts(V("ofd"), V("t192", 0, 24), c(P16), A.add)
+    quant("hw", 0, 192, V("xt", 0, 768))
     for n in ("par1", "par2"):
         pick(n, 96, 128, "qx", V("ofi", 0, 2))
     mm(6, "wm", 0, "qx", 0, 192)
@@ -365,6 +374,7 @@ def rank_program(g, core, T, topo):
         ts(V("mi", 8, 13), V("mi", 0, 5), 255, A.bitwise_and)
         ts(V("mi", 16, 21), V("mi", 0, 5), 9, A.logical_shift_right)
         cp(V("alw", 0, 5), V("mi", 8, 13))
+        cp(V("alw", 6, 11), V("mi", 16, 21))
         ts(V("a5", 0, 5), V("mi", 16, 21), 23.5, A.is_gt, c(B2), A.mult)
         ts(V("b5", 0, 5), V("mi", 16, 21), c(B24), A.add)
         tt(V("a5", 0, 5), V("a5", 0, 5), V("b5", 0, 5), A.add)
@@ -379,7 +389,7 @@ def rank_program(g, core, T, topo):
 
     def opened1(t):
         if t == 0:
-            ts(V("fl", 0, 72), V("idr", 0, 72), (0.5 - O1) * SC, A.is_gt)
+            ts(V("fl", 0, 80), ind(V("io"), V("alw", 6, 11)), 23.5, A.is_lt)
         else:
             ts(V("fl", 0, 72), V("pv", 0, 72), -25.0, A.is_lt)
         scan(V("cm2", 0, 72), V("ones", 0, 72), V("fl", 0, 72), 0.0, A.mult, A.add)
@@ -399,7 +409,9 @@ def rank_program(g, core, T, topo):
             cp(V("rem", 200, 272), V("mka", 0, 72))
         if t == R - 1:
             ts(V("nsr"), V("aiw", 64, 96), -32.0, A.mult)
-            tt(V("rv", 64, 96), V("nsr"), V("io", 0, 32), A.add)
+            tt(V("nkr"), V("nsr"), V("io", 0, 32), A.add)
+            for k in range(2):
+                ts(V("rv", 96 * k + 64, 96 * k + 96), V("nkr"), c(ALC + k), A.add)
 
     def wrap(t, n):
         tt(V("d32", 0, n), V("wr", 0, n), V("dg", 0, n), A.mult)
@@ -414,9 +426,8 @@ def rank_program(g, core, T, topo):
                 tr(V("r3t", 128 * b, 128 * b + 128), V("r3d", 128 * b, 128 * b + 128))
             ts(V("of3"), V("r3t", 0, 384, 32), 128.0, A.add)
 
-    def y_mm(t):
-        mm(5, "wm", 0, "hw", 96 + 32 * t, 128)
-        act(V("yn"), bank(5, 96, 128), AF.Copy)
+    def y_new(t):
+        act(V("yn"), ind(V("yp"), V("idx") if t == R - 1 else V("ol", 6 * t + 2, 6 * t + 4)), AF.Copy)
 
     def y_out(t, q="y"):
         cp(ind(V("yc"), V("ol", OL[t], OL[t] + 2)), V("yn"))
@@ -440,8 +451,12 @@ def rank_program(g, core, T, topo):
         mm(1, "um", 384, pool, KB[t], 192)
         mm(2, "um", 128, pool, KB[t], 192)
         mm(3, "um", 0, pool, KB[t], 192)
+        mm(5, "wm", 0, pool, KB[t], 192)
+        act(V("yp", KB[t], KB[t] + 192), bank(5, 0, 192), AF.Copy)
         if t == 0:
             mm(4, "um", 0, "pa", O0, 328)
+            mm(6, "wm", 0, "pa", O0, 328)
+            act(V("yp", O0, PW), bank(6, 0, 328), AF.Copy)
             dma("y", "cb0", bc(V("pbc", KB[0], PW), dt.uint8), bc(V("pac", KB[0], PW), dt.uint8))
             dma("y", "cb1", V("pbs", KB[0], PW), V("pas", KB[0], PW))
         if t == 1:
@@ -463,16 +478,15 @@ def rank_program(g, core, T, topo):
         for b in range(4):
             act(V("skw", 49 * b, 49 * b + 48), bank(3, 48 * b, 48 * b + 48), AF.Copy)
         if t > 0:
-            y_mm(t - 1)
+            y_new(t - 1)
         else:
             act(V("scp"), bank(4, 0, 328), AF.Copy)
         scan(V("fz"), V("fa"), V("fb"), 0.0, A.max, A.mult)
         scan(V("cum"), V("seg48"), V("fz"), 0.0, A.mult, A.subtract)
-        ts(V("le"), V("cum"), c(NREV), A.is_le)
-        scan(V("lp"), V("b49"), V("le"), 0.0, A.max, A.add)
-        cp(V("ofe", 0, 4 - rank), V("lp", 48 * rank + 47, 192, 48))
-        if rank:
-            cp(V("ofe", 4 - rank, 4), V("lp", 47, 48 * rank, 48))
+        for k in range(4):
+            b = (rank + k) % 4
+            act(V("le", 48 * b, 48 * b + 48), V("cum", 48 * b, 48 * b + 48), AF.Sign, bias=c(NREV), scale=-1.0, accum_out=col("alf", k))
+            ts(col("ofe", k), col("alf", k), 0.5, A.mult, 24.0 + 49 * b, A.add)
         if t == 0:
             state_in()
             opened1(0)
@@ -505,20 +519,19 @@ def rank_program(g, core, T, topo):
         for b in range(2):
             act(col("ini", b), col("eo", EW * b + 336), AF.Identity, scale=-256.0, bias=col("ib", b) if last else c(OLC + b))
         for b in range(2):
-            scan(V("nn", 96 * b, 96 * b + 64), V("fr"), V("bt", 64 * b, 64 * b + 64), 0.0, A.max, A.mult)
+            scan(V("nn", 128 * b, 128 * b + 64), V("fr"), V("bt", 64 * b, 64 * b + 64), 0.0, A.max, A.mult)
         for b in range(2):
-            scan(V("vv", 96 * b, 96 * b + 96), V("ones", 0, 96), V("nn", 96 * b, 96 * b + 96), col("ini", b), A.mult, A.subtract)
-        for b in range(2):
-            tr(V("rv", 32 * b, 32 * b + 32), V("vv", 96 * b + 64, 96 * b + 96))
+            scan(V("vv", 128 * b, 128 * b + 128), V("ones", 0, 128), V("nn", 128 * b, 128 * b + 128), col("ini", b), A.mult, A.subtract)
         for k in range(2):
-            act(V("su", 96 * k, 96 * k + 96), V("rv"), AF.Abs, bias=c(ALC + k))
+            for b in range(2):
+                tr(V("rv", 96 * k + 32 * b, 96 * k + 32 * b + 32), V("vv", 128 * b + 64 + 32 * k, 128 * b + 96 + 32 * k))
         for k in range(2):
-            red(col("best", k), V("su", 96 * k, 96 * k + 96), A.min)
+            red(col("best", k), V("rv", 96 * k, 96 * k + 96), A.min, True)
         if last:
-            to_all(lambda p: V("oni", 0, 2, 1, p), V("best", 0, 2, 1, G(rank)), 2048.0)
-            pick("hw", 192 + 32 * t, 224 + 32 * t, pool, V("oni"))
+            to_all(lambda p: V("idx", 0, 2, 1, p), V("best", 0, 2, 1, G(rank)), 2048.0)
+            pick("hw", 192 + 32 * t, 224 + 32 * t, pool, V("idx"))
             pick("fin", 0, 192, "hw", V("of3"))
-            y_mm(t)
+            y_new(t)
             dma("y", "oc", V("oc"), bc(V("finc"), dt.uint8))
             for k in range(4):
                 dma("sy"[k % 2], "os%d" % k, V("osc", 0, P, 1, (4 * k, 4 * k + 4)), V("fins", 0, P, 1, (32 * k, 32 * k + 4)))

@@ -5,11 +5,12 @@ from concourse.mybir import dt, AluOpType, AxisListType, ActivationFunctionType
 P, K, R, N = 192, 24, 3, 4
 TINY = 2.0 ** -100
 LOW = -1e29
+EPS = 2.0 ** -20
 C05 = float(np.float32(0.05))
 X4, U8, U16, F32, BF, I32 = "float8_e4m3fn_x4", "uint8", "uint16", "float32", "bfloat16", "int32"
-KB = (392, 200, 8)
-O0, O1, PW = 584, 720, 912
-OL = (4, 0, 6)
+O0, O1, B0, B1, B2, S0, S1, PW = 8, 144, 336, 528, 720, 912, 1168, 1424
+CT = 512
+OL = (2, 0, 4)
 SC = 1.0 / 65536
 EW = 368
 
@@ -21,26 +22,39 @@ def _decl(dtype, **kw):
         SCRATCH[k] = ("sbuf", [128, n], dtype)
 
 
-for _n, _w in (("qu", 128), ("um", 512), ("qx", 224), ("qn", 128), ("wm", 1024), ("sd0", 32), ("sd1", 48), ("pa", PW), ("pb", PW), ("pc", PW),
+for _n, _w in (("qu", 128), ("um", 512), ("qx", 224), ("qn", 128), ("wm", 1024), ("sd0", 32), ("sd1", 48), ("pa", B2), ("pb", S1), ("pc", PW),
                ("par1", 128), ("par2", 128), ("hw", 288), ("fin", 192)):
     _decl(X4, **{_n + "c": _w})
     _decl(U8, **{_n + "s": _w})
-_decl(BF, xt=896, ut=1024, ones=224, flip0=448, e0=448, junk=1400, ms=24, hd=336, kt0=768, kt1=768, kt2=768, fa=192, fb=192, fz=192, cum=192,
-      le=192, seg48=192, pbw=224, tb=336, ee=2 * EW, rm=2 * EW, eo=2 * EW, fr=64, thr=128, dd=128, cmpm=128, bt=128,
+_decl(BF, xt=896, ut=1024, ones=224, flip0=448, e0=448, junk=1400, pb0=192, prow=208, ms=24, hd=96, kt0=768, ktb=768, ktc=768, kt1=1024,
+      kt2=1024, fa=256, fb=256, fz=192, cum=256, fzt=PW - CT, pbt=PW - CT, fzr=256, pbr=256, abw=64, pbh=32, tb2=48, seg64=256,
+      le=256, seg48=192, pbw=208, tb=96, ee=2 * EW, rm=2 * EW, eo=2 * EW, fr=64, thr=128, dd=128, cmpm=128, bt=128,
       nn=256, fl=192, cm=200, cm2=80, r3=208, r3c=96, r3d=384, r3t=384)
-_decl(F32, io=376, cst=48, sm=88, v0=448, rr=64, su=320, cand=32, mcol=24, vf=208, t192=80, s192=80,
-      dg=96, seg16=96, kid=196, mb=192, mkall=280, scp=328, sc=96, idr=96, plr=80, skw=196, asw=96, akw=96, aiw=96, wr=96,
-      at=64, kb=336, kr=224, vv=256, rv=192, nsr=32, nkr=32, tsc=96, tid=96, e3=312, flip3=312, v3=312, pv=104,
-      d32=96, s64=96, yc=208, yn=32, yp=PW, zero=80)
-_decl(U16, ofu=32, ofi=8, mk16=8, al16=8, mland=32, aland=32, alw=12, idw=6, rem=272, ofe=4, idx=2, olw=2, ofp=6, ol=12, of3=12, ofd=24)
-_decl(I32, pi=4, mi=24)
+_decl(F32, io=376, cst=48, sm=96, v0=448, rr=64, su=320, cand=32, mcol=24, t192=80, p80=80, u80=80, s192=80, t24=24,
+      dg=96, seg16=96, kid=196, mb=192, mkall=280, stb=PW, sc=96, idr=80, cbr=96, tcb=96, alt=32, hcb=64, plr=80, skw=196, asw=64, akw=64,
+      aiw=64, wr=64, iob=S1, skr=256, kidr=256, kb2=48, nk1=32, nk2=32, nid=32, hl=8, cl=16,
+      at=64, kb=96, vv=256, rv=192, nsr=32, nkr=32, tsc=96, tid=64, e3=312, flip3=312, v3=312, pv=96,
+      d32=64, s64=64, yc=208, yn=32, yp=PW, zero=80)
+_decl(U16, ofu=32, ofi=8, mk16=8, mland=32, alw=6, idw=6, rem=272, ofe=4, idx=2, olw=2, ofh=16, ofc=16, ol=6, of3=12, ofd=24)
+_decl(I32, pi=4, mi=8)
 
-PART = {"scol": ("sm", 0, 2), "ini": ("sm", 2, 2), "gn": ("sm", 4, 4), "best": ("sm", 8, 8), "alf": ("sm", 16, 8), "mf": ("sm", 24, 8),
-        "ya": ("sm", 32, 6), "d2": ("sm", 40, 4), "b5": ("sm", 48, 8), "a5": ("sm", 56, 8), "yb": ("sm", 64, 6), "y6": ("sm", 72, 6),
-        "ib": ("sm", 80, 2), "mk192": ("mkall", 0, 200), "mka": ("mkall", 200, 80)}
-WAKE, LAND, FIRST = 200, {"am": 4500, "ap": 3600, "ar": 4500, "al": 3000}, {"ap": 3000}
-DMAS = ["x", "u", "wc", "ws", "cb0", "cb1", "cc0", "cc1", "y0", "y1", "y2", "oc", "os0", "os1", "os2", "os3"]
-SEMAPHORES = ["qv", "qs", "qt", "qg", "rl", "am", "ap", "ar", "al"] + ["d" + n for n in DMAS]
+PART = {"scol": ("sm", 0, 2), "ini": ("sm", 2, 2), "gn": ("sm", 4, 4), "best": ("sm", 8, 8), "alf": ("sm", 16, 8), "mf": ("sm", 24, 12),
+        "d2": ("sm", 40, 4), "a5": ("sm", 56, 8), "ib": ("sm", 80, 2), "ns": ("sm", 82, 1), "dc": ("sm", 88, 3), "best3": ("sm", 84, 3),
+        "mk192": ("mkall", 0, 200), "mka": ("mkall", 200, 80)}
+for _b, _d, _l in (("bq", BF, "fa fb fz cum fzr pbr abw pbh tb2 seg64 le seg48 tb fr thr dd cmpm bt"),
+                   ("fq", F32, "kb2 nk1 nk2 nid hl cl at kb nsr nkr tid yn")):
+    _at = 0
+    for _n in _l.split():
+        PART[_n] = (_b, _at, SCRATCH.pop(_n)[1][1])
+        _at += -(-PART[_n][2] // 16) * 16
+    _decl(_d, **{_b: _at})
+WAKE, LAND, FIRST, CY = 200, {"am": 2500, "ap": 2500, "ar": 4000, "as": 6000}, {"ap": 6000, "ar": 5000}, 0.87
+DM, GAP, NOISE, TURNS, SPAN, SOFT, SEED = 1500, 800, 1500, 1200, 5000, 0.2, 1
+DMAS = ["hw0", "hw1", "pa0", "pa1", "pa2", "pa3", "x", "u", "wc", "ws", "cb0", "cb1", "cc0", "cc1", "cc2", "cc3", "y0", "y1", "y2", "oc",
+        "os0", "os1", "os2", "os3"]
+SEMAPHORES = ["qv", "qs", "qt", "qg", "rl", "am", "ap", "ar", "as"] + ["d" + n for n in DMAS]
+MEMO = {}
+ONS3 = (0, 1, 3, 5, 7)
 A, AF = AluOpType, ActivationFunctionType
 
 
@@ -101,11 +115,15 @@ def rank_program(g, core, T, topo):
     def ms(o, c):
         op("v", "memset", [o, c])
 
-    def fill(o, k):
-        act(o, V("io", 1, 1 + -(-(o["c"][1] - o["c"][0]) // o["s"])), AF.Sign, scale=k)
-
     def iota(o, pat, base, cm):
         op("g", "iota", [o, pat, base, cm], {} if o["n"] == "pi" else {"allow_small_or_imprecise_dtypes": True})
+
+    def fill(o, k):
+        n = -(-(o["c"][1] - o["c"][0]) // o["s"])
+        if n <= 100 and o["s"] == 1:
+            iota(o, [[0, n]], int(k), 0)
+        else:
+            act(o, V("io", 1, 1 + n), AF.Sign, scale=k)
 
     def bank(b, c0=0, c1=512):
         return V("ps", 512 * b + c0, 512 * b + c1)
@@ -122,6 +140,10 @@ def rank_program(g, core, T, topo):
 
     def dma(q, sem, o, i):
         op(q, "dma_start", [o, i], sem="d" + sem)
+
+    def copy_pool(k, o, o0, i, c0, c1):
+        dma("y", k[0], bc(V(o + "c", o0, o0 + c1 - c0), dt.uint8), bc(V(i + "c", c0, c1), dt.uint8))
+        dma("y", k[1], V(o + "s", o0, o0 + c1 - c0), V(i + "s", c0, c1))
 
     peers = [r for r in range(N) if r != rank]
     sent = [0]
@@ -143,8 +165,8 @@ def rank_program(g, core, T, topo):
     def arrive(sem, calls, views):
         ops.append({"q": "arr", "name": sem, "w": views, "r": [], "sem": sem, "val": calls * sum(bin(mask_of(r)).count("1") for r in peers)})
 
-    (P16, P32, RCP, EIGHTH, Q0, TAUB, PSC, PBI, NREV, TG, B24, B2, OLC, PAD3, TP, NT, C32, ALC, T16, HALF, GE8, H16) = (
-        0, 1, 2, 3, 4, 5, 6, 7, 8, 9, 14, 15, 16, 18, 21, 23, 24, 27, 32, 34, 35, 36)
+    (P16, P32, Q0, TAUB, PSC, PBI, NREV, TG, B24, IDB, CBB, PAD3, TP, SB, NT, C32, ALC, T16, HALF, SG, H16) = (
+        0, 1, 4, 5, 6, 7, 8, 9, 14, 16, 17, 18, 19, 22, 23, 24, 27, 32, 34, 35, 36)
 
     def c(k, p=(0, 128)):
         return col("cst", k, p)
@@ -152,6 +174,8 @@ def rank_program(g, core, T, topo):
     dma("y", "x", V("xt", 0, 768), V("x"))
     ms(V("xt", 768, 896), 0.0)
     ms(V("ut", 80, 512), 0.0)
+    ms(V("ut", 528, 592), 0.0)
+    ms(V("ut", 596, 1024), 0.0)
     dma("s", "u", V("ut", 0, 80), V("u", 0, 80))
     dma("y", "wc", bc(V("wmc"), dt.uint8), V("wc"))
     dma("y", "ws", V("wms"), V("ws"))
@@ -177,47 +201,39 @@ def rank_program(g, core, T, topo):
     quant("qu", 0, 128, V("ut", 0, 512))
     pick("um", 0, 128, "qu", V("ofu", 0, 8))
     pick("um", 128, 256, "qu", V("ofu", 8, 16))
-    act(V("ut", 512, 1024), V("ut", 0, 512), AF.Copy)
+    cp(V("ut", 512, 528), V("ut", 0, 16))
     ts(V("ut", 592, 596), V("ut", 8, 12), -1.0, A.mult)
     quant("qn", 0, 128, V("ut", 512, 1024))
     ms(V("hd"), 1.0)
-    ms(V("mk16"), 0)
     ts(c(HALF), c(P16), 2.0, A.mult, -192.0, A.add)
     ms(V("hd", 1, 11), 2.0)
-    ms(V("hd", 0, 336, 48), 0.0)
-    for o in range(48, 336, 48):
-        act(V("hd", o + 1, o + 11), V("hd", 1, 11), AF.Copy)
+    ms(V("hd", 0, 96, 48), 0.0)
+    act(V("hd", 49, 59), V("hd", 1, 11), AF.Copy)
     ts(V("cst", TG, TG + 2), V("io", 0, 2), 32.0, A.mult, c(HALF), A.add)
     ts(V("cst", TG + 2, TG + 5), V("io", 0, 3), 32.0, A.mult, c(HALF), A.add)
     ts(V("cst", TG + 2, TG + 5), V("cst", TG + 2, TG + 5), 48.0, A.add)
-    ms(V("vf", 0, 192), -192.0)
 
     quant("qx", 0, 224, V("xt"))
-    mm(2, "qx", 0, "um", 0, 128)
-    mm(3, "qx", 96, "um", 0, 128)
+    mm(2, "qx", 0, "qu", 0, 128)
+    mm(3, "qx", 96, "qu", 0, 128)
     mm(0, "um", 0, "qx", 0, 192)
     mm(1, "um", 0, "qx", 0, 192)
-    mm(4, "qx", 0, "um", 128, 128)
-    mm(5, "qx", 96, "um", 128, 128)
+    mm(4, "qx", 0, "qu", 0, 128)
+    mm(5, "qx", 96, "qu", 0, 128)
     for t in range(2):
         cp(col("scol", t), bank(2 + t, 0, 1))
     for t in range(2):
-        act(V("ms", 12 * t, 12 * t + 10), bank(4 + t, 1, 11), AF.Sign, bias=c(NT))
+        act(V("ms", 12 * t, 12 * t + 10), bank(4 + t, 3, 13), AF.Sign, bias=c(NT))
     for t in range(2):
         ts(V("e0", 224 * t, 224 * t + 192), bank(0, 0, 192), col("scol", t), A.is_equal)
         act(V("junk", 192 * t, 192 * t + 192), bank(1, 0, 192), AF.Sign, bias=col("scol", t), scale=-1.0, accum_out=col("gn", t))
     for t in range(2):
         scan(V("mcol", 12 * t, 12 * t + 10), V("hd", 1, 11), V("ms", 12 * t, 12 * t + 10), 1.0, A.mult, A.add)
-
-    def src6(b):
-        return (b // 3, b % 3)
-
-    for b in range(6):
-        act(col("mf", b, G(rank)), col("mcol", 12 * src6(b)[0] + 9, G(src6(b)[1])), AF.Copy)
-    cp(V("mk16", 0, 6, 1, G(rank)), V("mf", 0, 6, 1, G(rank)))
-    send(V("mk16", 0, 6), lambda r: V("mland", 8 * rank, 8 * rank + 6), "am")
     for t in range(2):
         scan(V("v0", 224 * t, 224 * t + 224), V("flip0", 224 * t, 224 * t + 224), V("e0", 224 * t, 224 * t + 224), col("gn", t), A.mult, A.subtract)
+    cp(V("mk16", 0, 2), V("mcol", 9, 24, 12))
+    ts(V("mk16", 2, 4), V("v0", 192, 448, 224), 191.6, A.add, 0.5, A.mult)
+    send(V("mk16", 0, 4), lambda r: V("mland", 8 * rank, 8 * rank + 4), "am")
     for t in range(2):
         tr(V("rr", 32 * t, 32 * t + 32), V("v0", 224 * t + 192, 224 * t + 224))
 
@@ -249,38 +265,27 @@ def rank_program(g, core, T, topo):
     send(V("sd0s", 0, 24), there("pas", O0, 24), "ap")
     spread([2, 3, 4])
     pick("sd1", 0, 48, "qx", V("ofi", 2, 5))
+    for k, sem in enumerate(("ar", "as")):
+        send(bc(V("sd1c", 24 * k, 24 * k + 24), dt.uint8), there("pac", O1 + 96 * k, 24), sem)
+        send(V("sd1s", 24 * k, 24 * k + 24), there("pas", O1 + 96 * k, 24), sem)
     pick("pa", O0 + 72, O1, "qx", V("ofi", 0, 4))
-    for b in range(6):
-        t, q = src6(b)
-        act(V("vf", 32 * b, 32 * b + 32, 1, G(rank)), V("rr", 32 * t, 32 * t + 32, 1, G(q)), AF.Copy)
-    ts(V("vf", 192, 208), V("io", 192, 208), 1.0 / 256, A.mult, -192.0, A.add)
     ts(V("cst", ALC, ALC + 5), V("io", 0, 5), 16.0, A.mult, c(P16), A.add)
     cp(V("cst", T16, T16 + 2), V("cst", ALC, ALC + 2))
     ts(V("cst", H16, H16 + 5), V("cst", ALC, ALC + 5), 0.5, A.add)
-    act(V("cm", 192, 200), V("io", 73, 81), AF.Copy)
-    ts(V("cst", ALC, ALC + 2), V("cst", T16, T16 + 2), -1.0, A.mult)
-    ts(V("fl"), V("vf", 0, 192), -49.0, A.is_lt)
+    iota(V("cm", 192, 200), [[1, 8]], 73, 0)
     ts(V("seg16"), V("dg"), 0.0, A.not_equal)
-    scan(V("cm", 0, 192), V("ones", 0, 192), V("fl"), 0.0, A.mult, A.add)
     ts(V("dg"), V("dg"), c(P16), A.is_equal)
-    for k in range(5):
-        act(V("junk", 384 + 200 * k, 584 + 200 * k), V("cm"), AF.Sign, bias=c(H16 + k), scale=-1.0, accum_out=col("alf", k))
     pick("um", 256, 512, "qn", V("ofu", 16, 32))
-    ts(V("alw", 0, 5), V("alf", 0, 5), 0.5, A.mult, 100.0, A.add)
-    cp(V("plr"), ind(V("vf"), V("alw", 0, 5)))
-    tt(V("t192"), V("plr"), V("dg", 0, 80), A.mult)
-    scan(V("s192"), V("seg16", 0, 80), V("t192"), 0.0, A.mult, A.add)
-    ts(V("al16", 0, 5), V("s192", 15, 80, 16), 192.0, A.add, 256.0, A.mult)
-    send(V("al16", 0, 5), lambda r: V("aland", 8 * rank, 8 * rank + 5), "al")
-    send(bc(V("sd1c"), dt.uint8), there("pac", O1, 48), "ar")
-    send(V("sd1s"), there("pas", O1, 48), "ar")
-    pick("pa", O1 + 144, PW, "qx", V("ofi", 2, 5))
+    copy_pool(("pa0", "pa1"), "pa", O1 + 72, "sd1", 0, 24)
+    copy_pool(("pa2", "pa3"), "pa", O1 + 168, "sd1", 24, 48)
 
     ts(V("pi", 3, 4), V("pi", 0, 1), 32, A.bitwise_and)
     ts(c(Q0), V("pi", 3, 4), 0.0, A.is_gt)
     for q in range(4):
         ms(c(B24, G(q)), 24.0 * beta[q])
-    ts(c(B2), c(B24), 112.0, A.add)
+        ms(c(45, G(q)), 32.0 * beta[q])
+    ts(c(IDB), c(B24), float(O0), A.add, -SC, A.mult)
+    ts(c(CBB), c(B24), (B1 - CT) / 2 - (O1 - O0), A.add, -2 * SC, A.mult)
     ms(c(TAUB, (0, 64)), -TINY)
     ms(c(TAUB, (64, 128)), 0.0)
     ts(c(PSC), c(P32), 0.5, A.is_gt)
@@ -290,18 +295,29 @@ def rank_program(g, core, T, topo):
     ts(c(PBI), c(PSC), -TINY, A.mult, c(44), A.add)
     ts(c(NREV), c(P16), -1.0, A.mult, 15.5, A.add)
     ts(V("cst", C32, C32 + 3), V("io", 0, 3), -32.0, A.mult, c(P32), A.subtract)
-    ts(V("cst", OLC, OLC + 2), V("cst", C32, C32 + 2), -1.0 / 256, A.mult, 256.0, A.add)
     ts(c(PAD3), c(P32), 7.5, A.is_lt)
-    ts(c(GE8), c(P16), 7.5, A.is_gt)
-    ts(c(TP), c(P16), 2.0, A.mult, -72.0, A.add)
-    ts(c(42), c(GE8), 1000.0, A.mult, c(TP), A.add)
-    ts(c(TP + 1), c(42), 32.0, A.add, 500.0, A.min)
-    ts(c(45), c(42), -1016.0, A.add, -500.0, A.max)
-    ts(c(46), c(TP), 16.0, A.add)
-    for q in range(4):
-        if beta[q] % 2:
-            cp(V("cst", TP, TP + 2, 1, G(q)), V("cst", 45, 47, 1, G(q)))
-    iota(V("pv", 96, 98), [[-1000, 2]], 500, 0)
+    ts(c(SG), c(Q0), 2.0, A.mult, -1.0, A.add)
+    ts(c(SB), c(SG), -TINY, A.mult)
+    ts(V("mi", 6, 7), V("pi", 1, 2), 1, A.logical_shift_right)
+    ts(c(42), V("mi", 6, 7), 2.0, A.mult, -72.0, A.add)
+    ts(V("cst", TP, TP + 3), V("io", 0, 3), 16.0, A.mult, c(42), A.add)
+    for o in range(0, S1, 292):
+        iota(V("iob", o, o + 292), [[1, 292]], o, 0)
+    for t in range(2):
+        h = (S0, S1)[t] - CT
+        ts(V("hcb", 32 * t, 32 * t + 32), V("iob", h, h + 32), c(45), A.add, -SC, A.mult)
+    fill(V("cl"), 0.0)
+    for n, o in (("fzt", B2 - CT), ("pbt", B2 - CT), ("stb", B2)):
+        iota(V(n, o, o + 192), [[0, 192]], 0, 0)
+    fill(V("fzt", 0, 16), 0.0)
+    for o in (0, 128):
+        op("g", "affine_select", [V("seg64", o, o + 128), V("ones", 0, 128), [[0, 2], [1, 64]], A.not_equal, 0.0, 0, 0])
+    fill(V("tb2"), 0.0)
+    fill(V("stb", 0, 8), 0.0)
+    fill(V("yp", 0, 8), 0.0)
+    fill(V("cbr", 80, 96), 0.0)
+    fill(V("prow", 192, 208), 0.0)
+    ts(V("pbt", 0, 16), V("ones", 0, 16), c(P32), A.mult, 0.0, A.is_equal)
     for b in range(2):
         fill(V("rm", EW * b + 66, EW * b + EW), 0.0)
         fill(V("rm", EW * b, EW * b + 1), 0.0)
@@ -313,13 +329,9 @@ def rank_program(g, core, T, topo):
     ms(c(43), -0.5)
     act(V("flip3"), V("flip3"), AF.Sign, bias=c(43))
     act(V("flip3", 208, 312), V("flip3", 208, 312), AF.Identity, scale=c(PAD3))
-    ts(c(47), c(P32), 1.0, A.add, SC, A.mult)
-    op("v", "reciprocal", [c(RCP), c(47)])
-    ms(c(EIGHTH), 0.125)
     act(V("thr"), V("thr"), AF.Relu, scale=0.5)
     act(V("thr"), V("thr"), AF.Identity, scale=-1.0, bias=-3.0)
-    fill(V("seg48"), 1.0)
-    fill(V("seg48", 0, 192, 48), 0.0)
+    op("g", "affine_select", [V("seg48"), V("ones", 0, 192), [[0, 4], [1, 48]], A.not_equal, 0.0, 0, 0])
     fill(V("tb"), 0.0)
     for b in range(2):
         fill(V("ee", EW * b + 336, EW * b + EW), 1.0)
@@ -328,68 +340,64 @@ def rank_program(g, core, T, topo):
         ms(V("nn", 128 * b + 80, 128 * b + 128, 32), -15.0)
     ts(V("pbw", 48, 196, 49), V("ones", 0, 4), c(P32), A.mult, 0.0, A.is_equal)
     fill(V("skw", 48, 196, 49), 0.0)
-    fill(V("pbw", 196, 224), 0.0)
     fill(V("zero"), 0.0)
-    fill(V("yp", 0, 200), 0.0)
-    fill(V("yp", 200, 392), 0.0)
-    fill(V("ya"), 0.0)
-    fill(V("yb"), 0.0)
-    act(V("cm2", 72, 80), V("io", 25, 33), AF.Copy)
+    iota(V("cm2", 72, 80), [[1, 8]], 25, 0)
     ms(V("sc", 80, 96), LOW)
-    fill(V("idr", 80, 96), 0.0)
     fill(V("mk192", 192, 200), 0.0)
     fill(V("yc", 192, 208), 0.0)
-    ts(V("cst", ALC + 2, ALC + 4), V("cst", ALC, ALC + 2), 0.25, A.add)
-    for k in range(2):
-        ts(V("rv", 96 * k + 64, 96 * k + 96), V("io", 0, 32), 257.0 / 256, A.mult, c(ALC + 2 + k), A.add)
-    act(V("r3"), V("io", 0, 208), AF.Identity, bias=-128.0)
-    act(V("r3c"), V("io", 64, 160), AF.Copy)
-    iota(V("t192", 0, 24), [[16, 12], [0, 2]], 0, 0)
-    ts(V("ofd"), V("t192", 0, 24), c(P16), A.add)
-    quant("hw", 0, 192, V("xt", 0, 768))
-    for n in ("par1", "par2"):
-        pick(n, 96, 128, "qx", V("ofi", 0, 2))
+    iota(V("r3"), [[1, 208]], -128, 0)
+    iota(V("r3c"), [[1, 96]], 64, 0)
+    iota(V("t24"), [[16, 12], [0, 2]], 0, 0)
+    iota(V("alt"), [[0, 16], [-2, 2]], 1, 0)
+    ts(V("ofd"), V("t24"), c(P16), A.add)
+    copy_pool(("hw0", "hw1"), "hw", 0, "qx", 0, 192)
     mm(6, "wm", 0, "qx", 0, 192)
     act(V("yc", 0, 192), bank(6, 0, 192), AF.Copy)
 
     arrive("am", 1, [V("mland")])
     arrive("ap", 2, [V("pac", O0, O0 + 72), V("pas", O0, O0 + 72)])
-    arrive("ar", 2, [V("pac", O1, O1 + 144), V("pas", O1, O1 + 144)])
-    arrive("al", 1, [V("aland")])
+    arrive("ar", 2, [V("pac", O1, O1 + 72), V("pas", O1, O1 + 72)])
+    arrive("as", 2, [V("pac", O1 + 96, O1 + 168), V("pas", O1 + 96, O1 + 168)])
 
     def to_all(o, i, f):
         for q in range(4):
             ts(o(G(q)), i, f, A.mult)
 
-    def marks_in():
-        for q in peers:
-            cp(V("mf", 0, 6, 1, G(q)), V("mland", 8 * q, 8 * q + 6, 1, G(q)))
-        for b in range(6):
-            act(V("mb", 32 * b, 32 * b + 32), V("zero", 0, 32), AF.Identity, bias=col("mf", b))
-        tr(V("mk192", 0, 192), V("mb"))
-
     def state_in():
         for q in range(4):
-            cp(V("mi", 0, 5, 1, G(q)), V("al16", 0, 5, 1, G(q)) if q == rank else V("aland", 8 * q, 8 * q + 5, 1, G(q)))
-        ts(V("mi", 8, 13), V("mi", 0, 5), 255, A.bitwise_and)
-        ts(V("mi", 16, 21), V("mi", 0, 5), 9, A.logical_shift_right)
-        cp(V("alw", 0, 5), V("mi", 8, 13))
-        cp(V("alw", 6, 11), V("mi", 16, 21))
-        ts(V("a5", 0, 5), V("mi", 16, 21), 23.5, A.is_gt, c(B2), A.mult)
-        ts(V("b5", 0, 5), V("mi", 16, 21), c(B24), A.add)
-        tt(V("a5", 0, 5), V("a5", 0, 5), V("b5", 0, 5), A.add)
-        cp(V("idw", 0, 5), V("a5", 0, 5))
+            for s in range(3):
+                cp(V("mf", s, 12, 3, G(q)), V("mk16", 0, 4, 1, G(s)) if q == rank else V("mland", 8 * q, 8 * q + 4, 1, G(s)))
+        for b in range(6):
+            act(V("pb0", 32 * b, 32 * b + 32), V("zero", 0, 32), AF.Identity, bias=col("mf", 6 + b))
+        for b in range(6):
+            act(V("mb", 32 * b, 32 * b + 32), V("zero", 0, 32), AF.Identity, bias=col("mf", b))
+        tr(V("prow", 0, 192), V("pb0"))
+        tr(V("mk192", 0, 192), V("mb"))
+        ts(V("fl"), V("prow", 0, 192), 71.5, A.is_lt)
+        scan(V("cm", 0, 192), V("ones", 0, 192), V("fl"), 0.0, A.mult, A.add)
+        for k in range(5):
+            act(V("junk", 384 + 200 * k, 520 + 200 * k), V("cm", 16 * k, 16 * k + 136), AF.Sign, bias=c(H16 + k), scale=-1.0, accum_out=col("a5", k))
+        tt(V("a5", 0, 5), V("a5", 0, 5), V("io", 136, 296, 32), A.add)
+        ts(V("alw", 0, 5), V("a5", 0, 5), 0.5, A.mult)
+        cp(V("p80"), ind(V("prow"), V("alw", 0, 5)))
+        ts(V("t192"), V("p80"), 23.5, A.is_gt, 112.0, A.mult)
+        ts(V("u80"), V("p80"), 47.5, A.is_gt, 72.0, A.mult)
+        tt(V("t192"), V("t192"), V("p80"), A.add)
+        tt(V("t192"), V("t192"), V("u80"), A.add)
+        act(V("idr"), V("t192"), AF.Identity, scale=-SC, bias=c(IDB))
+        act(V("cbr", 0, 80), V("t192"), AF.Identity, scale=-2 * SC, bias=c(CBB))
+        tt(V("u80"), V("t192"), V("dg", 0, 80), A.mult)
+        scan(V("s192"), V("seg16", 0, 80), V("u80"), 0.0, A.mult, A.add)
+        ts(V("idw", 0, 5), V("s192", 15, 80, 16), c(B24), A.add)
         act(V("mka"), ind(V("mk192"), V("alw", 0, 5)), AF.Copy)
         act(V("plr"), ind(V("io"), V("alw", 0, 5)), AF.Identity, scale=-SC)
-        act(V("idr", 0, 80), ind(V("io"), V("idw", 0, 5)), AF.Identity, scale=-SC, bias=-O0 * SC)
-        act(V("sc", 0, 80), ind(V("scp"), V("idw", 0, 5)), AF.Copy)
         cp(ind(V("mk192"), V("alw", 0, 5)), V("zero"))
         ms(V("mk192", 192, 193), 1024.0)
         cp(V("rem", 0, 200), V("mk192"))
 
     def opened1(t):
         if t == 0:
-            ts(V("fl", 0, 80), ind(V("io"), V("alw", 6, 11)), 23.5, A.is_lt)
+            ts(V("fl", 0, 72), V("p80", 0, 72), 23.5, A.is_lt)
         else:
             ts(V("fl", 0, 72), V("pv", 0, 72), -25.0, A.is_lt)
         scan(V("cm2", 0, 72), V("ones", 0, 72), V("fl", 0, 72), 0.0, A.mult, A.add)
@@ -398,154 +406,195 @@ def rank_program(g, core, T, topo):
 
     def opened2(t):
         ts(V("olw"), V("d2", 0, 2), 0.5, A.mult, 40.0, A.add)
-        act(V("akw", 64, 96), ind(V("mka"), V("olw")), AF.Identity, scale=-1.0)
-        act(V("aiw", 64, 96), ind(V("idr"), V("olw")), AF.Copy)
-        act(V("asw", 64, 96), ind(V("sc"), V("olw")), AF.Copy)
-        act(V("wr", 0, 32) if t else V("wr", 64, 96), ind(V("plr"), V("olw")), AF.Copy)
+        act(V("nk1"), ind(V("idr"), V("olw")), AF.Identity, scale=-16.0)
+        tt(V("nk2"), V("nk1"), V("io", 0, 32), A.add)
+        act(V("wr", 0, 32) if t else V("wr", 32, 64), ind(V("plr"), V("olw")), AF.Copy)
+        if t < R - 1:
+            cp(ind(V("cbr"), V("olw")), V("hcb", 32 * t, 32 * t + 32))
+            tr(V("tcb"), V("cbr"))
+            act(V("e3", 72, 312, 104), V("tcb", 0, 96, 32), AF.Copy)
+            ts(V("dc"), V("tcb", 0, 96, 32), -(S0 - CT - 0.5) * SC, A.is_lt, -127 * SC, A.mult)
+            ts(V("dc"), V("dc"), -SC, A.add)
+            for b in range(3):
+                act(V("e3", 104 * b + 73, 104 * b + 104), V("alt", 0, 31), AF.Identity, scale=col("dc", b))
 
     def opened3(t):
         cp(ind(V("mka"), V("olw")), V("zero", 0, 32))
-        if t:
-            cp(V("rem", 200, 272), V("mka", 0, 72))
-        if t == R - 1:
-            ts(V("nsr"), V("aiw", 64, 96), -32.0, A.mult)
-            tt(V("nkr"), V("nsr"), V("io", 0, 32), A.add)
-            for k in range(2):
-                ts(V("rv", 96 * k + 64, 96 * k + 96), V("nkr"), c(ALC + k), A.add)
+        cp(V("rem", 200, 272), V("mka", 0, 72))
 
     def wrap(t, n):
         tt(V("d32", 0, n), V("wr", 0, n), V("dg", 0, n), A.mult)
         scan(V("s64", 0, n), V("seg16", 0, n), V("d32", 0, n), 0.0, A.mult, A.add)
-        to_all(lambda p: V("ol", 6 * t - 6, 6 * t - 6 + n // 16, 1, p), V("s64", 15, n, 16, G(rank)), -65536.0)
+        to_all(lambda p: V("ol", 4 * t - 4, 4 * t - 4 + n // 16, 1, p), V("s64", 15, n, 16, G(rank)), -65536.0)
 
     def places(t):
         cp(ind(V("r3"), V("ol", OL[t], OL[t] + 2)), V("r3c", 32 * t, 32 * t + 32))
         if t == R - 1:
-            act(V("r3d"), ind(V("r3"), V("ofd")), AF.Copy)
             for b in range(3):
+                act(V("r3d", 128 * b, 128 * b + 128), ind(V("r3"), V("ofd", 8 * b, 8 * b + 8)), AF.Copy)
                 tr(V("r3t", 128 * b, 128 * b + 128), V("r3d", 128 * b, 128 * b + 128))
             ts(V("of3"), V("r3t", 0, 384, 32), 128.0, A.add)
 
-    def y_new(t):
-        act(V("yn"), ind(V("yp"), V("idx") if t == R - 1 else V("ol", 6 * t + 2, 6 * t + 4)), AF.Copy)
+    pools, END = ("pa", "pb", "pc"), (B1, S1, PW)
 
     def y_out(t, q="y"):
         cp(ind(V("yc"), V("ol", OL[t], OL[t] + 2)), V("yn"))
         dma(q, "y%d" % t, V("y", P * t, P * t + P), V("yc", 0, P))
 
-    pools = ("pa", "pb", "pc")
+    def children(p0, b0, kt, pool, c0, on_s):
+        for i in range(8):
+            mm(i, "wm", 128 * i, "pa", p0, 128)
+            if i in on_s:
+                act(V(kt, i, 768, 8), bank(i, b0, b0 + 96), AF.Relu, scale=C05)
+            else:
+                ts(V(kt, i, 768, 8), bank(i, b0, b0 + 96), 0.0, A.max, C05, A.mult)
+        quant(pool, c0, c0 + 192, V(kt))
+
+    def numbers(pool, c0, n, k=0, f0=0):
+        for b, s0 in enumerate((256, 384, 128, 0)):
+            mm(k + b, "um", s0, pool, c0, n)
+        act(V("fa", f0, f0 + n), bank(k, 0, n), AF.Sign, bias=c(SB), scale=c(SG))
+        ts(V("fb", f0, f0 + n), bank(k + 1, 0, n), c(TAUB), A.is_gt, -EPS, A.mult)
+        scan(V("fz") if c0 == B0 else V("fzt", c0 - CT, c0 - CT + n), V("fa", f0, f0 + n), V("fb", f0, f0 + n), 0.0, A.max, A.mult)
+        if c0 == B0:
+            for b in range(4):
+                act(V("pbw", 49 * b, 49 * b + 48), bank(2, 48 * b, 48 * b + 48), AF.Sign, bias=c(PBI), scale=c(PSC))
+            for b in range(4):
+                act(V("skw", 49 * b, 49 * b + 48), bank(3, 48 * b, 48 * b + 48), AF.Copy)
+        else:
+            act(V("pbt", c0 - CT, c0 - CT + n), bank(k + 2, 0, n), AF.Sign, bias=c(PBI), scale=c(PSC))
+        act(V("stb", c0, c0 + n), bank(k + 3, 0, n), AF.Copy)
+
+    children(O0, 0, "kt0", "pa", B0, (1, 3, 5, 7))
+    numbers("pa", B0, 192)
     for t in range(R):
         pool, last = pools[t], t == R - 1
-        par, p0 = ("pa", O0) if t == 0 else ("par%d" % t, 0)
-        kt = "kt%d" % t
         if t == 0:
-            marks_in()
-        for i in range(8):
-            mm(i, "wm", 128 * i, par, p0, 128)
-            if i % 2:
-                act(V(kt, i, 768, 8), bank(i, 0, 96), AF.Relu, scale=C05)
-            else:
-                ts(V(kt, i, 768, 8), bank(i, 0, 96), 0.0, A.max, C05, A.mult)
-        quant(pool, KB[t], KB[t] + 192, V(kt))
-        mm(0, "um", 256, pool, KB[t], 192)
-        mm(1, "um", 384, pool, KB[t], 192)
-        mm(2, "um", 128, pool, KB[t], 192)
-        mm(3, "um", 0, pool, KB[t], 192)
-        mm(5, "wm", 0, pool, KB[t], 192)
-        act(V("yp", KB[t], KB[t] + 192), bank(5, 0, 192), AF.Copy)
-        if t == 0:
-            mm(4, "um", 0, "pa", O0, 328)
-            mm(6, "wm", 0, "pa", O0, 328)
-            act(V("yp", O0, PW), bank(6, 0, 328), AF.Copy)
-            dma("y", "cb0", bc(V("pbc", KB[0], PW), dt.uint8), bc(V("pac", KB[0], PW), dt.uint8))
-            dma("y", "cb1", V("pbs", KB[0], PW), V("pas", KB[0], PW))
-        if t == 1:
-            dma("y", "cc0", bc(V("pcc", KB[1], PW), dt.uint8), bc(V("pbc", KB[1], PW), dt.uint8))
-            dma("y", "cc1", V("pcs", KB[1], PW), V("pbs", KB[1], PW))
-        if t > 0:
+            sw, seg, pb, sk = 48, 49, V("pbw", 0, 196), V("skw")
+            scan(V("cum", 0, 192), V("seg48"), V("fz"), 0.0, A.mult, A.subtract)
+        else:
+            sw, seg, pb, sk = 64, 64, V("pbr"), V("skr")
+            cp(V("fzr"), ind(V("fzt", 0, END[t] - CT), V("ofc")))
+            act(V("pbr"), ind(V("pbt", 0, END[t] - CT), V("ofc")), AF.Copy)
+            act(V("skr"), ind(V("stb", CT, END[t]), V("ofc")), AF.Copy)
+            act(V("kidr"), ind(V("iob"), V("ofc")), AF.Identity, scale=-SC, bias=-CT * SC)
+            scan(V("cum"), V("seg64"), V("fzr"), 0.0, A.mult, A.subtract)
             opened3(t)
             places(t)
-        ts(V("fa"), bank(0, 0, 192), 0.0, A.is_gt, c(Q0), A.is_equal)
-        ts(V("fb"), bank(1, 0, 192), c(TAUB), A.is_gt, -1.0, A.mult)
-        for b in range(4):
-            act(V("pbw", 49 * b, 49 * b + 48), bank(2, 48 * b, 48 * b + 48), AF.Sign, bias=c(PBI), scale=c(PSC))
-        for b in range(7):
-            tr(V("tb", 48 * b, 48 * b + 32), V("pbw", 32 * b, 32 * b + 32))
-        scan(V("kb", 0, 192), V("hd", 0, 192), V("tb", 0, 192), 0.0, A.mult, A.subtract)
-        scan(V("kb", 192, 336), V("hd", 192, 336), V("tb", 192, 336), 0.0, A.mult, A.subtract)
-        for b in range(7):
-            tr(V("kr", 32 * b, 32 * b + 32), V("kb", 48 * b + 16, 48 * b + 48))
-        for b in range(4):
-            act(V("skw", 49 * b, 49 * b + 48), bank(3, 48 * b, 48 * b + 48), AF.Copy)
-        if t > 0:
-            y_new(t - 1)
-        else:
-            act(V("scp"), bank(4, 0, 328), AF.Copy)
-        scan(V("fz"), V("fa"), V("fb"), 0.0, A.max, A.mult)
-        scan(V("cum"), V("seg48"), V("fz"), 0.0, A.mult, A.subtract)
         for k in range(4):
             b = (rank + k) % 4
-            act(V("le", 48 * b, 48 * b + 48), V("cum", 48 * b, 48 * b + 48), AF.Sign, bias=c(NREV), scale=-1.0, accum_out=col("alf", k))
-            ts(col("ofe", k), col("alf", k), 0.5, A.mult, 24.0 + 49 * b, A.add)
+            act(V("le", sw * b, sw * b + 48), V("cum", sw * b, sw * b + 48), AF.Sign, bias=c(NREV), scale=-1.0 / EPS, accum_out=col("alf", k))
+            ts(col("ofe", k), col("alf", k), 0.5, A.mult, 24.0 + seg * b, A.add)
         if t == 0:
             state_in()
             opened1(0)
-        cp(V("akw", 0, 64), ind(V("kr"), V("ofe")))
-        act(V("asw", 0, 64), ind(V("skw"), V("ofe")), AF.Copy)
-        act(V("aiw", 0, 64), ind(V("kid"), V("ofe")), AF.Identity, scale=-SC, bias=-KB[t] * SC)
+        cp(V("abw"), ind(pb, V("ofe")))
+        act(V("asw"), ind(sk, V("ofe")), AF.Copy)
         if t == 0:
+            act(V("aiw"), ind(V("kid"), V("ofe")), AF.Identity, scale=-SC, bias=-B0 * SC)
             opened2(0)
-        tr(V("d32", 0, 64), V("akw", 0, 64))
-        tr(V("at"), V("asw", 0, 64))
+        else:
+            act(V("aiw"), ind(V("kidr"), V("ofe")), AF.Copy)
         for b in range(2):
-            act(V("dd", 64 * b, 64 * b + 64), V("asw", 0, 64), AF.Sign, bias=col("at", 32 * b), scale=-1.0)
+            tr(V("tb", 48 * b, 48 * b + 32), V("abw", 32 * b, 32 * b + 32))
+        scan(V("kb"), V("hd"), V("tb"), 0.0, A.mult, A.subtract)
+        for b in range(2):
+            tr(V("akw", 32 * b, 32 * b + 32), V("kb", 48 * b + 16, 48 * b + 48))
+        tr(V("at"), V("asw"))
+        for b in range(2):
+            act(V("dd", 64 * b, 64 * b + 64), V("asw"), AF.Sign, bias=col("at", 32 * b), scale=-1.0)
         if t == 0:
             opened3(0)
-        ts(V("ee", 64, 336), V("rem") if t else V("mkall", 0, 272), col("d32", 0), A.add, 0.0, A.not_equal)
-        act(V("ee", EW + 64, EW + 336), V("mkall", 0, 272), AF.Abs, bias=col("d32", 32))
+        ts(V("ee", 64, 336), V("rem"), col("kb", 16), A.add, 0.0, A.not_equal)
+        act(V("ee", EW + 64, EW + 336), V("mkall", 0, 272), AF.Abs, bias=col("kb", 64))
         for b in range(2):
-            ts(V("ee", EW * b, EW * b + 64), V("akw", 0, 64), col("d32", 32 * b), A.not_equal)
+            ts(V("ee", EW * b, EW * b + 64), V("akw"), col("kb", 48 * b + 16), A.not_equal)
         if t > 0:
             y_out(t - 1)
         scan(V("cmpm"), V("dd"), V("thr"), -2.0, A.max, A.add)
         ts(V("bt"), V("cmpm"), -3.25, A.is_lt, -1.0, A.mult)
         for b in range(2):
             scan(V("eo", EW * b, EW * b + EW), V("rm", EW * b, EW * b + EW), V("ee", EW * b, EW * b + EW), 0.0, A.max, A.min)
-        if last:
-            tr(V("tid", 0, 64), V("aiw", 0, 64))
-            act(V("ib"), V("tid", 0, 64, 32), AF.Identity, scale=-32.0, bias=256.0)
+        tr(V("tid"), V("aiw"))
+        act(V("ib"), V("tid", 0, 64, 32), AF.Identity, scale=-16.0, bias=256.0)
         for b in range(2):
             tr(V("fr", 32 * b, 32 * b + 32), V("eo", EW * b + 336, EW * b + EW))
         for b in range(2):
-            act(col("ini", b), col("eo", EW * b + 336), AF.Identity, scale=-256.0, bias=col("ib", b) if last else c(OLC + b))
+            act(col("ini", b), col("eo", EW * b + 336), AF.Identity, scale=-256.0, bias=col("ib", b))
+        act(V("junk", 400, 464), V("fr"), AF.Identity, bias=-1.0 / 128, accum_out=V("ns"))
         for b in range(2):
             scan(V("nn", 128 * b, 128 * b + 64), V("fr"), V("bt", 64 * b, 64 * b + 64), 0.0, A.max, A.mult)
         for b in range(2):
             scan(V("vv", 128 * b, 128 * b + 128), V("ones", 0, 128), V("nn", 128 * b, 128 * b + 128), col("ini", b), A.mult, A.subtract)
+        for k in range(2):
+            ts(V("rv", 96 * k + 64, 96 * k + 96), V("nk2"), V("ns"), A.max, c(T16 + k), A.subtract)
         for k in range(2):
             for b in range(2):
                 tr(V("rv", 96 * k + 32 * b, 96 * k + 32 * b + 32), V("vv", 128 * b + 64 + 32 * k, 128 * b + 96 + 32 * k))
         for k in range(2):
             red(col("best", k), V("rv", 96 * k, 96 * k + 96), A.min, True)
         if last:
-            to_all(lambda p: V("idx", 0, 2, 1, p), V("best", 0, 2, 1, G(rank)), 2048.0)
+            to_all(lambda p: V("idx", 0, 2, 1, p), V("best", 0, 2, 1, G(rank)), 4096.0)
             pick("hw", 192 + 32 * t, 224 + 32 * t, pool, V("idx"))
             pick("fin", 0, 192, "hw", V("of3"))
-            y_new(t)
+            act(V("yn"), ind(V("yp"), V("idx")), AF.Copy)
             dma("y", "oc", V("oc"), bc(V("finc"), dt.uint8))
             for k in range(4):
                 dma("sy"[k % 2], "os%d" % k, V("osc", 0, P, 1, (4 * k, 4 * k + 4)), V("fins", 0, P, 1, (32 * k, 32 * k + 4)))
             y_out(t, "s")
             break
-        ts(V("idx"), V("best", 0, 2), 256.0, A.mult)
-        cp(V("nsr"), ind(V("asw"), V("idx")))
-        act(V("wr", 32, 64), ind(V("aiw"), V("idx")), AF.Copy)
-        act(V("nkr"), ind(V("akw"), V("idx")), AF.Identity, scale=-1.0)
+        if t == 0:
+            children(O1 - 32, 32, "ktb", "pa", B1, range(8))
+            numbers("pa", B1, 192)
+            mm(4, "um", 0, "pa", O0, 328)
+            act(V("stb", O0, B0), bank(4, 0, 328), AF.Copy)
+            act(V("sc", 0, 80), ind(V("stb", O0, B0), V("idw", 0, 5)), AF.Copy)
+            copy_pool(("cb0", "cb1"), "pb", O0, "pa", O0, B2)
+            copy_pool(("cc0", "cc1"), "pc", O0, "pa", O0, B2)
+        else:
+            children(O1 + 64, 32, "ktc", "pc", B2, range(8))
+            numbers("pc", B2, 192)
+        ts(V("idx"), V("best", 0, 2), 4096.0, A.mult)
+        cp(V("nsr"), ind(V("stb", 0, END[t]), V("idx")))
+        act(V("nid"), ind(V("iob"), V("idx")), AF.Identity, scale=-SC)
         cp(ind(V("sc"), V("olw")), V("nsr"))
-        cp(ind(V("idr"), V("olw")), V("wr", 32, 64))
+        cp(ind(V("idr"), V("olw")), V("nid"))
+        for q in range(4):
+            o, i = V("hl", 2 * beta[q], 2 * beta[q] + 2, 1, G(0)), V("best", 0, 2, 1, G(q))
+            if q:
+                act(o, i, AF.Copy)
+            else:
+                cp(o, i)
+        for q in range(4):
+            ts(V("ofh", 8 * t, 8 * t + 8, 1, G(q)), V("hl", 0, 8, 1, G(0)), 4096.0, A.mult)
+        par, c0, kt = "par%d" % (t + 1), (S0, S1)[t], "kt%d" % (t + 1)
+        pick(par, 0, 128, pool, V("ofh", 8 * t, 8 * t + 8))
+        for i in range(8):
+            mm(i, "wm", 128 * i, par, 0, 128)
+            o = V(kt, 512 * (i // 4) + i % 4, 512 * (i // 4) + 512, 4)
+            if i in ONS3:
+                act(o, bank(i, 0, 128), AF.Relu, scale=C05)
+            else:
+                ts(o, bank(i, 0, 128), 0.0, A.max, C05, A.mult)
+        act(V("yn"), bank(0, 96, 128), AF.Copy)
+        mm(6, "um", 128, par, 0, 128)
+        for q in range(4):
+            act(V("pbh", 0, 32, 1, G(q)), V("ps", 3072 + 32 * beta[q], 3104 + 32 * beta[q], 1, G(q)), AF.Sign, bias=c(PBI, G(q)), scale=c(PSC, G(q)))
+        for m in range(2):
+            quant(pools[t + 1], c0 + 128 * m, c0 + 128 * m + 128, V(kt, 512 * m, 512 * m + 512))
+            numbers(pools[t + 1], c0 + 128 * m, 128, 4 * m, 128 * m)
+        if t == 0:
+            copy_pool(("cc2", "cc3"), "pc", S0, "pb", S0, S1)
+        else:
+            for j, o in enumerate(range(O0, PW, 178)):
+                n = min(178, PW - o)
+                mm(4 + j % 4, "wm", 0, "pc", o, n)
+                act(V("yp", o, o + n), bank(4 + j % 4, 0, n), AF.Copy)
+        tr(V("tb2", 0, 32), V("pbh"))
+        scan(V("kb2"), V("hd", 0, 48), V("tb2"), 0.0, A.mult, A.add)
+        tr(V("nkr"), V("kb2", 16, 48))
+        cp(ind(V("mka"), V("olw")), V("nkr"))
         tr(V("tsc"), V("sc"))
-        for b in range(3):
-            tr(V("e3", 104 * b + 72, 104 * b + 104), V("idr", 32 * b, 32 * b + 32))
         for b in range(3):
             ts(V("e3", 104 * b, 104 * b + 72), V("sc", 0, 72), col("tsc", 32 * b), A.is_equal)
             act(V("junk", 160 + 72 * b, 232 + 72 * b), V("sc", 0, 72), AF.Sign, bias=col("tsc", 32 * b), scale=-1.0, accum_out=col("gn", b))
@@ -553,28 +602,24 @@ def rank_program(g, core, T, topo):
             scan(V("v3", 104 * b, 104 * b + 104), V("flip3", 104 * b, 104 * b + 104), V("e3", 104 * b, 104 * b + 104), col("gn", b), A.mult, A.subtract)
         for b in range(3):
             tr(V("pv", 32 * b, 32 * b + 32), V("v3", 104 * b + 72, 104 * b + 104))
-        cp(ind(V("mka"), V("olw")), V("nkr"))
-        for k in range(2):
-            act(V("su", 104 * k, 104 * k + 98), V("pv", 0, 98), AF.Abs, scale=-1.0, bias=c(TP + k))
-        for k in range(2):
-            red(col("best", k), V("su", 104 * k, 104 * k + 98), A.min)
+        for k in range(3):
+            act(V("su", 104 * k, 104 * k + 72), V("pv", 0, 72), AF.Abs, scale=-1.0, bias=c(TP + k))
+        for k in range(3):
+            red(col("best3", k), V("su", 104 * k, 104 * k + 72), A.min)
         for q in range(4):
-            c0 = 3 * (beta[q] // 2) + beta[q] % 2
-            o, i = V("yb" if beta[q] % 2 else "ya", c0, c0 + 2, 1, G(0)), V("best", 0, 2, 1, G(q))
+            o, i = V("cl", 4 * beta[q], 4 * beta[q] + 3, 1, G(0)), V("best3", 0, 3, 1, G(q))
             if q % 2:
-                act(o, i, AF.Identity, scale=c(RCP, G(q)), bias=c(EIGHTH, G(q)))
+                act(o, i, AF.Identity, scale=65536.0)
             else:
-                ts(o, i, c(RCP, G(q)), A.mult, 0.125, A.add)
-        tt(V("y6", 0, 6, 1, G(0)), V("ya", 0, 6, 1, G(0)), V("yb", 0, 6, 1, G(0)), A.add)
+                ts(o, i, 65536.0, A.mult)
         for q in range(4):
-            cp(V("ofp", 0, 6, 1, G(q)), V("y6", 0, 6, 1, G(0)))
-        pick("par%d" % (t + 1), 0, 96, pool, V("ofp"))
+            cp(V("ofc", 0, 16, 1, G(q)), V("cl", 0, 16, 1, G(0)))
         opened1(t + 1)
         opened2(t + 1)
-        wrap(t + 1, 64 if t else 96)
+        wrap(t + 1, 32 if t else 64)
         if t == 0:
             places(0)
-        pick("hw", 192 + 32 * t, 224 + 32 * t, pool, V("ol", 6 * t + 2, 6 * t + 4))
+        pick("hw", 192 + 32 * t, 224 + 32 * t, pool, V("ofh", 8 * t + 6, 8 * t + 8))
 
     emit(g, T, ops, sent[0])
 
@@ -603,30 +648,28 @@ def emit(g, T, ops, sent):
             return 0, 0
         if n == "dma_start":
             v = a[0] if a[0]["n"] in SCRATCH else a[1]
-            return 60, 1900 + width(v) * size[SCRATCH[v["n"]][2]] * 0.6 + (4500 if v["n"] == "wms" else 0)
+            return 60, DM + width(v) * size[SCRATCH[v["n"]][2]] * 0.5 + (4500 if v["n"] == "wms" else 800 if v["n"] == "yc" else 0)
         if n == "remote_dma_fused":
             return 250, 250
         e = width(a[0])
         if n == "matmul_mx":
-            d = (e + 16) * 0.63
+            d = (e + 16) * 0.6
         elif n == "quantize_mx":
-            d = 15 + 1.1 * e
-        elif n == "reciprocal":
-            d = 200
+            d = 15 + 0.92 * e
         elif n in ("iota", "affine_select"):
-            d = 150 + 2.1 * e
+            d = 150 + 2 * CY * e
         elif "off" in a[0]:
-            d = 50 + 3.6 * e
+            d = 50 + 3.5 * CY * e
         elif len(a) > 1 and isinstance(a[1], dict) and "off" in a[1]:
-            d = 60 + 1.7 * e
+            d = 60 + 1.5 * CY * e
         elif n == "tensor_reduce":
-            d = max(64, width(a[1])) * 1.04
+            d = max(64, width(a[1])) * CY
         elif n == "tensor_tensor":
-            d = max(64, 2 * e) * 1.04
+            d = max(64, 2 * e) * CY
         else:
             full = [v for v in a[:3 if n == "tensor_tensor_scan" else 2] if isinstance(v, dict)]
-            d = max(64, e * (0.5 if n != "activation" and all(two(v) for v in full) else 1)) * 1.04
-        return d, d
+            d = max(64, e * (0.5 if n != "activation" and all(two(v) for v in full) else 1)) * CY + (20 if "accum_out" in o["kw"] else 0)
+        return d, d + (1000 if a[0]["n"] == "of3" or (n == "quantize_mx" and a[2]["n"] in ("ktb", "ktc")) else 0)
 
     last_send, sends = None, {}
     for i, o in enumerate(ops):
@@ -641,7 +684,8 @@ def emit(g, T, ops, sent):
             for v in views:
                 for (k2, v2, o2) in seen.get(v["n"], []):
                     if (kind == "w" or k2 == "w" or (v["n"] == "ps" and o2["q"] != q)) and meet(v, v2):
-                        o["dep"].add(o2["i"])
+                        if q != "arr" or o2["name"] != "dma_start":
+                            o["dep"].add(o2["i"])
         if o["name"] == "remote_dma_fused":
             if last_send is not None:
                 o["lag"][last_send] = 1500 if ops[last_send]["to"] == "am" else 0
@@ -653,19 +697,82 @@ def emit(g, T, ops, sent):
                 seen.setdefault(v["n"], []).append((kind, v, o))
         o["busy"], o["took"] = cost(o)
     for o in ops:
-        o["pre"] = [(d, WAKE) for d in o["dep"]] + list(o["lag"].items())
+        o["pre"], o["post"] = [(d, WAKE) for d in sorted(o["dep"])] + list(o["lag"].items()), []
         o["rest"] = o["took"] + FIRST.get(o["name"], 0)
     for o in reversed(ops):
         for d, lag in o["pre"]:
             ops[d]["rest"] = max(ops[d]["rest"], ops[d]["took"] + lag + o["rest"] + FIRST.get(ops[d]["name"], 0))
-    busy = {q: [] for q in list(queue) + ["arr"]}
-    for o in sorted(ops, key=lambda e: (-e["rest"], e["i"])):
-        t = max([ops[d]["t"] + ops[d]["took"] + lag for d, lag in o["pre"]] + [0])
-        for a, b in sorted(busy[o["q"]]):
-            if b > t and a < t + o["busy"]:
-                t = b
-        o["t"] = t
-        busy[o["q"]].append((t, t + o["busy"]))
+            ops[d]["post"].append((o["i"], lag))
+
+    def place(order, back):
+        busy, at = {q: [] for q in list(queue) + ["arr"]}, {}
+        for o in order:
+            if back:
+                t = max([at[d] + ops[d]["busy"] + lag + o["took"] - o["busy"] for d, lag in o["post"]] + [o["took"] - o["busy"]])
+            else:
+                t = max([at[d] + ops[d]["took"] + lag for d, lag in o["pre"]] + [0])
+            line = busy[o["q"]]
+            j, hi = 0, len(line)
+            while j < hi:
+                mid = (j + hi) // 2
+                if line[mid][1] <= t:
+                    j = mid + 1
+                else:
+                    hi = mid
+            while j < len(line) and line[j][0] < t + o["busy"]:
+                t = max(t, line[j][1])
+                j += 1
+            line.insert(j, (t, t + o["busy"]))
+            at[o["i"]] = t
+        return at
+
+    tails = {}
+
+    def length(at, f):
+        free, end = {}, {}
+        for o in sorted(ops, key=lambda e: (at[e["i"]], e["i"])):
+            k = f if o["q"] in "vst" else 1
+            t = max([end[d] + lag for d, lag in o["pre"]] + [free.get(o["q"], 0)])
+            free[o["q"]] = t + k * o["busy"]
+            end[o["i"]] = t + k * o["took"]
+        if f not in tails:
+            tails[f] = {}
+            for o in reversed(topo_order(ops, at)):
+                tails[f][o["i"]] = max([lag + (f if ops[d]["q"] in "vst" else 1) * ops[d]["took"] + tails[f][d] for d, lag in o["post"]] + [0])
+        return max(end.values()) + SOFT * sum(end[i] + tails[f][i] for i in end) / len(end)
+
+    at = place(sorted(ops, key=lambda e: (-e["rest"], e["i"])), False)
+    for turn in range(4):
+        for o in ops:
+            late = o["i"] in MEMO["late"] if "late" in MEMO else at[o["i"]] + o["busy"] > at[sends["am"]] - GAP
+            if o["q"] == "g" and "to" not in o and late and (last_send, 0) not in o["pre"]:
+                o["pre"].append((last_send, 0))
+                ops[last_send]["post"].append((o["i"], 0))
+        at = place(topo_order(ops, at), False)
+    if "at" not in MEMO:
+        MEMO["late"] = {o["i"] for o in ops if (last_send, 0) in o["pre"]}
+        best, seed = None, SEED
+        for turn in range(TURNS):
+            score = length(at, 1.0) + length(at, 1.4)
+            if best is None or score < best[0]:
+                best = (score, at)
+            key = {}
+            if turn % 3 == 0:
+                seed = (seed * 1103515245 + 12345) % 2147483648
+                t0 = seed % 40000
+                for o in ops:
+                    seed = (seed * 1103515245 + 12345) % 2147483648
+                    t = best[1][o["i"]]
+                    key[o["i"]] = t + (NOISE * (seed / 2147483648) ** 3 if t0 <= t < t0 + SPAN else 0)
+            else:
+                late = place(sorted(ops, key=lambda e: (-at[e["i"]] - e["took"], -e["i"])), True)
+                for o in ops:
+                    key[o["i"]] = -late[o["i"]] - o["busy"]
+            at = place(topo_order(ops, key), False)
+        MEMO["at"], MEMO["score"] = best[1], best[0]
+    at = place(topo_order(ops, MEMO["at"]), False)
+    for o in ops:
+        o["t"] = at[o["i"]]
     count = {}
     clock = {q: {} for q in queue}
     for o in sorted(ops, key=lambda e: (e["t"], e["i"])):
@@ -698,6 +805,20 @@ def emit(g, T, ops, sent):
         g.wait_ge(T.sem[key], val)
 
 
+def topo_order(ops, key):
+    done, out = set(), []
+
+    def visit(o):
+        if o["i"] not in done:
+            done.add(o["i"])
+            for d in sorted(d for d, lag in o["pre"]):
+                visit(ops[d])
+            out.append(o)
+    for o in sorted(ops, key=lambda e: (key[e["i"]], e["i"])):
+        visit(o)
+    return out
+
+
 def call(q, name, a, kw):
     if name == "tensor_scalar":
         return q.tensor_scalar(*a)
@@ -713,8 +834,6 @@ def call(q, name, a, kw):
         return q.transpose(*a)
     if name == "tensor_reduce":
         return q.tensor_reduce(*a, **kw)
-    if name == "reciprocal":
-        return q.reciprocal(*a)
     if name == "memset":
         return q.memset(*a)
     if name == "iota":

@@ -8,7 +8,7 @@ LOW = -1e29
 EPS = 2.0 ** -20
 C05 = float(np.float32(0.05))
 X4, U8, U16, F32, BF, I32 = "float8_e4m3fn_x4", "uint8", "uint16", "float32", "bfloat16", "int32"
-O0, O1, B0, B1, B2, S0, S1, PW = 8, 144, 336, 528, 720, 912, 1168, 1424
+O0, O1, B0, B1, B2, S0, S1, PW = 8, 144, 336, 592, 784, 976, 1232, 1488
 CT = 512
 OL = (2, 0, 4)
 SC = 1.0 / 65536
@@ -26,35 +26,35 @@ for _n, _w in (("qu", 128), ("um", 512), ("qx", 224), ("qn", 128), ("wm", 1024),
                ("par1", 128), ("par2", 128), ("hw", 288), ("fin", 192)):
     _decl(X4, **{_n + "c": _w})
     _decl(U8, **{_n + "s": _w})
-_decl(BF, xt=896, ut=1024, ones=224, flip0=448, e0=448, junk=1400, pb0=192, prow=208, ms=24, hd=96, kt0=768, ktb=768, ktc=768, kt1=1024,
+_decl(BF, xt=896, ut=1024, ones=224, flip0=448, e0=448, junk=1400, pb0=192, prow=208, ms=24, hd=96, kt0=1024, ktb=768, ktc=768, kt1=1024,
       kt2=1024, fa=256, fb=256, fz=192, cum=256, fzt=PW - CT, pbt=PW - CT, fzr=256, pbr=256, abw=64, pbh=32, tb2=48, seg64=256,
       le=256, seg48=192, pbw=208, tb=96, ee=2 * EW, rm=2 * EW, eo=2 * EW, fr=64, thr=128, dd=128, cmpm=128, bt=128,
       nn=256, fl=192, cm=200, cm2=80, r3=208, r3c=96, r3d=384, r3t=384)
 _decl(F32, io=376, cst=48, sm=96, v0=448, rr=64, su=320, cand=32, mcol=24, t192=80, p80=80, u80=80, s192=80, t24=24,
-      dg=96, seg16=96, kid=196, mb=192, mkall=280, stb=PW, sc=96, idr=80, cbr=96, tcb=96, alt=32, hcb=64, plr=80, skw=196, asw=64, akw=64,
-      aiw=64, wr=64, iob=S1, skr=256, kidr=256, kb2=48, nk1=32, nk2=32, nid=32, hl=8, cl=16,
+      dg=96, seg16=96, kid=200, mb=192, mb2=192, mk0=200, mkall=280, stb=PW, sc=96, idr=80, cbr=96, tcb=96, alt=32, hcb=64, plr=80, skw=200,
+      asw=64, akw=64, aiw=64, wr=64, iob=S1, skr=256, kidr=256, kb2=48, nk1=32, nk2=32, nid=32, hl=8, cl=16,
       at=64, kb=96, vv=256, rv=192, nsr=32, nkr=32, tsc=96, tid=64, e3=312, flip3=312, v3=312, pv=96,
       d32=64, s64=64, yc=208, yn=32, yp=PW, zero=80)
-_decl(U16, ofu=32, ofi=8, mk16=8, mland=32, alw=6, idw=6, rem=272, ofe=4, idx=2, olw=2, ofh=16, ofc=16, ol=6, of3=12, ofd=24)
+_decl(U16, ofu=32, ofi=8, mk16=8, mland=32, alw=6, idw=6, rem=272, rem0=200, ofe=4, idx=2, olw=2, ofh=16, ofc=16, ol=6, of3=12, ofd=24)
 _decl(I32, pi=4, mi=8)
 
 PART = {"scol": ("sm", 0, 2), "ini": ("sm", 2, 2), "gn": ("sm", 4, 4), "best": ("sm", 8, 8), "alf": ("sm", 16, 8), "mf": ("sm", 24, 12),
-        "d2": ("sm", 40, 4), "a5": ("sm", 56, 8), "ib": ("sm", 80, 2), "ns": ("sm", 82, 1), "dc": ("sm", 88, 3), "best3": ("sm", 84, 3),
-        "mk192": ("mkall", 0, 200), "mka": ("mkall", 200, 80)}
+        "d2": ("sm", 40, 4), "a5": ("sm", 56, 8), "mz": ("sm", 64, 6), "ib": ("sm", 80, 2), "ns": ("sm", 82, 1), "dc": ("sm", 88, 3),
+        "best3": ("sm", 84, 3), "mk192": ("mkall", 0, 200), "mka": ("mkall", 200, 80)}
 for _b, _d, _l in (("bq", BF, "fa fb fz cum fzr pbr abw pbh tb2 seg64 le seg48 tb fr thr dd cmpm bt"),
-                   ("fq", F32, "kb2 nk1 nk2 nid hl cl at kb nsr nkr tid yn")):
+                   ("fq", F32, "mb mb2 mk0 kb2 nk1 nk2 nid hl cl at kb nsr nkr tid yn")):
     _at = 0
     for _n in _l.split():
         PART[_n] = (_b, _at, SCRATCH.pop(_n)[1][1])
         _at += -(-PART[_n][2] // 16) * 16
     _decl(_d, **{_b: _at})
 WAKE, LAND, FIRST, CY = 200, {"am": 2500, "ap": 2500, "ar": 4000, "as": 6000}, {"ap": 6000, "ar": 5000}, 0.87
-DM, GAP, NOISE, TURNS, SPAN, SOFT, SEED = 1500, 800, 1500, 1200, 5000, 0.2, 1
-DMAS = ["hw0", "hw1", "pa0", "pa1", "pa2", "pa3", "x", "u", "wc", "ws", "cb0", "cb1", "cc0", "cc1", "cc2", "cc3", "y0", "y1", "y2", "oc",
-        "os0", "os1", "os2", "os3"]
+DM, GAP, NOISE, TURNS, SPAN, SOFT, SEED = 1500, 800, 1500, 2300, 2500, 0.8, 11
+DMAS = ["hw0", "hw1", "hw2", "hw3", "hw4", "hw5", "pa0", "pa1", "pa2", "pa3", "x", "u", "wc", "ws", "cb0", "cb1", "cc0", "cc1", "cc2", "cc3",
+        "y0", "y1", "y2", "oc", "os0", "os1", "os2", "os3"]
 SEMAPHORES = ["qv", "qs", "qt", "qg", "rl", "am", "ap", "ar", "as"] + ["d" + n for n in DMAS]
 MEMO = {}
-ONS3 = (0, 1, 3, 5, 7)
+ONS3 = (0, 1, 2, 4, 5, 6)
 A, AF = AluOpType, ActivationFunctionType
 
 
@@ -197,7 +197,7 @@ def rank_program(g, core, T, topo):
         op("g", "affine_select", [V("flip0", 224 * t, 224 * t + 224), V("ones", 0, 224), [[1, 224]], A.not_equal, -1.0, -96 * t, -1])
         ts(col("e0", 224 * t + 192), V("pi", 0, 1), 96.0 * t, A.add, -1.0 / 256, A.mult)
     iota(V("dg"), [[0, 6], [1, 16]], 0, 0)
-    iota(V("kid", 0, 196), [[48, 4], [1, 49]], 0, 0)
+    iota(V("kid"), [[24, 4], [1, 25], [128, 2]], 0, 0)
     quant("qu", 0, 128, V("ut", 0, 512))
     pick("um", 0, 128, "qu", V("ofu", 0, 8))
     pick("um", 128, 256, "qu", V("ofu", 8, 16))
@@ -301,15 +301,16 @@ def rank_program(g, core, T, topo):
     ts(V("mi", 6, 7), V("pi", 1, 2), 1, A.logical_shift_right)
     ts(c(42), V("mi", 6, 7), 2.0, A.mult, -72.0, A.add)
     ts(V("cst", TP, TP + 3), V("io", 0, 3), 16.0, A.mult, c(42), A.add)
-    for o in range(0, S1, 292):
-        iota(V("iob", o, o + 292), [[1, 292]], o, 0)
+    for o in range(0, S1, 308):
+        iota(V("iob", o, o + 308), [[1, 308]], o, 0)
     for t in range(2):
         h = (S0, S1)[t] - CT
         ts(V("hcb", 32 * t, 32 * t + 32), V("iob", h, h + 32), c(45), A.add, -SC, A.mult)
     fill(V("cl"), 0.0)
     for n, o in (("fzt", B2 - CT), ("pbt", B2 - CT), ("stb", B2)):
         iota(V(n, o, o + 192), [[0, 192]], 0, 0)
-    fill(V("fzt", 0, 16), 0.0)
+    fill(V("fzt", 0, B1 - CT), 0.0)
+    fill(V("pbt", 16, B1 - CT), 0.0)
     for o in (0, 128):
         op("g", "affine_select", [V("seg64", o, o + 128), V("ones", 0, 128), [[0, 2], [1, 64]], A.not_equal, 0.0, 0, 0])
     fill(V("tb2"), 0.0)
@@ -338,12 +339,15 @@ def rank_program(g, core, T, topo):
         fill(V("nn", 128 * b + 65, 128 * b + 128), 1.0)
         fill(V("nn", 128 * b + 64, 128 * b + 65), 0.0)
         ms(V("nn", 128 * b + 80, 128 * b + 128, 32), -15.0)
-    ts(V("pbw", 48, 196, 49), V("ones", 0, 4), c(P32), A.mult, 0.0, A.is_equal)
-    fill(V("skw", 48, 196, 49), 0.0)
+    for m in range(2):
+        ts(V("pbw", 48 + m, 200, 50), V("ones", 0, 4), c(P32), A.mult, 0.0, A.is_equal)
+        fill(V("skw", 48 + m, 200, 50), 0.0)
+        ms(V("kt0", 512 * m + 384, 512 * m + 512), 0.0)
     fill(V("zero"), 0.0)
     iota(V("cm2", 72, 80), [[1, 8]], 25, 0)
     ms(V("sc", 80, 96), LOW)
-    fill(V("mk192", 192, 200), 0.0)
+    iota(V("mk0", 192, 200), [[0, 8]], 1024, 0)
+    iota(V("mk192", 192, 200), [[0, 8]], 1024, 0)
     fill(V("yc", 192, 208), 0.0)
     iota(V("r3"), [[1, 208]], -128, 0)
     iota(V("r3c"), [[1, 96]], 64, 0)
@@ -369,10 +373,18 @@ def rank_program(g, core, T, topo):
                 cp(V("mf", s, 12, 3, G(q)), V("mk16", 0, 4, 1, G(s)) if q == rank else V("mland", 8 * q, 8 * q + 4, 1, G(s)))
         for b in range(6):
             act(V("pb0", 32 * b, 32 * b + 32), V("zero", 0, 32), AF.Identity, bias=col("mf", 6 + b))
+        ts(V("mz"), V("mf", 6, 12), 23.5, A.is_gt)
+        tt(V("mf", 0, 6), V("mf", 0, 6), V("mz"), A.mult)
         for b in range(6):
             act(V("mb", 32 * b, 32 * b + 32), V("zero", 0, 32), AF.Identity, bias=col("mf", b))
         tr(V("prow", 0, 192), V("pb0"))
-        tr(V("mk192", 0, 192), V("mb"))
+        tr(V("mk0", 0, 192), V("mb"))
+        cp(V("rem0"), V("mk0"))
+        ts(V("mz"), V("mf", 6, 12), 71.5, A.is_gt)
+        tt(V("mz"), V("mf", 0, 6), V("mz"), A.mult)
+        for b in range(6):
+            act(V("mb2", 32 * b, 32 * b + 32), V("zero", 0, 32), AF.Identity, bias=col("mz", b))
+        tr(V("mk192", 0, 192), V("mb2"))
         ts(V("fl"), V("prow", 0, 192), 71.5, A.is_lt)
         scan(V("cm", 0, 192), V("ones", 0, 192), V("fl"), 0.0, A.mult, A.add)
         for k in range(5):
@@ -389,10 +401,8 @@ def rank_program(g, core, T, topo):
         tt(V("u80"), V("t192"), V("dg", 0, 80), A.mult)
         scan(V("s192"), V("seg16", 0, 80), V("u80"), 0.0, A.mult, A.add)
         ts(V("idw", 0, 5), V("s192", 15, 80, 16), c(B24), A.add)
-        act(V("mka"), ind(V("mk192"), V("alw", 0, 5)), AF.Copy)
+        act(V("mka"), ind(V("mk0"), V("alw", 0, 5)), AF.Copy)
         act(V("plr"), ind(V("io"), V("alw", 0, 5)), AF.Identity, scale=-SC)
-        cp(ind(V("mk192"), V("alw", 0, 5)), V("zero"))
-        ms(V("mk192", 192, 193), 1024.0)
         cp(V("rem", 0, 200), V("mk192"))
 
     def opened1(t):
@@ -413,8 +423,8 @@ def rank_program(g, core, T, topo):
             cp(ind(V("cbr"), V("olw")), V("hcb", 32 * t, 32 * t + 32))
             tr(V("tcb"), V("cbr"))
             act(V("e3", 72, 312, 104), V("tcb", 0, 96, 32), AF.Copy)
-            ts(V("dc"), V("tcb", 0, 96, 32), -(S0 - CT - 0.5) * SC, A.is_lt, -127 * SC, A.mult)
-            ts(V("dc"), V("dc"), -SC, A.add)
+            act(V("dc"), V("tcb", 0, 96, 32), AF.Sign, bias=(S0 - CT - 0.5) * SC)
+            act(V("dc"), V("dc"), AF.Identity, scale=63.5 * SC, bias=-64.5 * SC)
             for b in range(3):
                 act(V("e3", 104 * b + 73, 104 * b + 104), V("alt", 0, 31), AF.Identity, scale=col("dc", b))
 
@@ -455,26 +465,39 @@ def rank_program(g, core, T, topo):
             mm(k + b, "um", s0, pool, c0, n)
         act(V("fa", f0, f0 + n), bank(k, 0, n), AF.Sign, bias=c(SB), scale=c(SG))
         ts(V("fb", f0, f0 + n), bank(k + 1, 0, n), c(TAUB), A.is_gt, -EPS, A.mult)
-        scan(V("fz") if c0 == B0 else V("fzt", c0 - CT, c0 - CT + n), V("fa", f0, f0 + n), V("fb", f0, f0 + n), 0.0, A.max, A.mult)
-        if c0 == B0:
-            for b in range(4):
-                act(V("pbw", 49 * b, 49 * b + 48), bank(2, 48 * b, 48 * b + 48), AF.Sign, bias=c(PBI), scale=c(PSC))
-            for b in range(4):
-                act(V("skw", 49 * b, 49 * b + 48), bank(3, 48 * b, 48 * b + 48), AF.Copy)
-        else:
-            act(V("pbt", c0 - CT, c0 - CT + n), bank(k + 2, 0, n), AF.Sign, bias=c(PBI), scale=c(PSC))
+        scan(V("fzt", c0 - CT, c0 - CT + n), V("fa", f0, f0 + n), V("fb", f0, f0 + n), 0.0, A.max, A.mult)
+        act(V("pbt", c0 - CT, c0 - CT + n), bank(k + 2, 0, n), AF.Sign, bias=c(PBI), scale=c(PSC))
         act(V("stb", c0, c0 + n), bank(k + 3, 0, n), AF.Copy)
 
-    children(O0, 0, "kt0", "pa", B0, (1, 3, 5, 7))
-    numbers("pa", B0, 192)
+    for i in range(8):
+        mm(i, "wm", 128 * i, "pa", O0, 128)
+        o = V("kt0", 512 * (i // 4) + i % 4, 512 * (i // 4) + 384, 4)
+        if i % 2:
+            act(o, bank(i, 0, 96), AF.Relu, scale=C05)
+        else:
+            ts(o, bank(i, 0, 96), 0.0, A.max, C05, A.mult)
+    for m in range(2):
+        c0, k = B0 + 128 * m, 4 * m
+        quant("pa", c0, c0 + 128, V("kt0", 512 * m, 512 * m + 512))
+        for b, s0 in enumerate((256, 384, 128, 0)):
+            mm(k + b, "um", s0, "pa", c0, 128)
+        act(V("fa", 128 * m, 128 * m + 96), bank(k, 0, 96), AF.Sign, bias=c(SB), scale=c(SG))
+        ts(V("fb", 128 * m, 128 * m + 96), bank(k + 1, 0, 96), c(TAUB), A.is_gt, -EPS, A.mult)
+        scan(V("fz", m, 192, 2), V("fa", 128 * m, 128 * m + 96), V("fb", 128 * m, 128 * m + 96), 0.0, A.max, A.mult)
+        for b in range(4):
+            act(V("pbw", 50 * b + m, 50 * b + 48, 2), bank(k + 2, 24 * b, 24 * b + 24), AF.Sign, bias=c(PBI), scale=c(PSC))
+        for b in range(4):
+            act(V("skw", 50 * b + m, 50 * b + 48, 2), bank(k + 3, 24 * b, 24 * b + 24), AF.Copy)
+        act(V("stb", c0, c0 + 128), bank(k + 3, 0, 128), AF.Copy)
     for t in range(R):
         pool, last = pools[t], t == R - 1
         if t == 0:
-            sw, seg, pb, sk = 48, 49, V("pbw", 0, 196), V("skw")
+            sw, seg, pb, sk = 48, 50, V("pbw", 0, 200), V("skw")
             scan(V("cum", 0, 192), V("seg48"), V("fz"), 0.0, A.mult, A.subtract)
         else:
             sw, seg, pb, sk = 64, 64, V("pbr"), V("skr")
-            cp(V("fzr"), ind(V("fzt", 0, END[t] - CT), V("ofc")))
+            cp(V("fzr", 0, 128), ind(V("fzt", 0, END[t] - CT), V("ofc", 0, 8)))
+            act(V("fzr", 128, 256), ind(V("fzt", 0, END[t] - CT), V("ofc", 8, 16)), AF.Copy)
             act(V("pbr"), ind(V("pbt", 0, END[t] - CT), V("ofc")), AF.Copy)
             act(V("skr"), ind(V("stb", CT, END[t]), V("ofc")), AF.Copy)
             act(V("kidr"), ind(V("iob"), V("ofc")), AF.Identity, scale=-SC, bias=-CT * SC)
@@ -503,18 +526,17 @@ def rank_program(g, core, T, topo):
         tr(V("at"), V("asw"))
         for b in range(2):
             act(V("dd", 64 * b, 64 * b + 64), V("asw"), AF.Sign, bias=col("at", 32 * b), scale=-1.0)
-        if t == 0:
-            opened3(0)
-        ts(V("ee", 64, 336), V("rem"), col("kb", 16), A.add, 0.0, A.not_equal)
-        act(V("ee", EW + 64, EW + 336), V("mkall", 0, 272), AF.Abs, bias=col("kb", 64))
+        z = 0 if t else 72
+        ts(V("ee", z + 64, 336), V("rem") if t else V("rem0"), col("kb", 16), A.add, 0.0, A.not_equal)
+        act(V("ee", EW + z + 64, EW + 336), V("mkall", 0, 272) if t else V("mk0"), AF.Abs, bias=col("kb", 64))
         for b in range(2):
-            ts(V("ee", EW * b, EW * b + 64), V("akw"), col("kb", 48 * b + 16), A.not_equal)
+            ts(V("ee", EW * b + z, EW * b + z + 64), V("akw"), col("kb", 48 * b + 16), A.not_equal)
         if t > 0:
             y_out(t - 1)
         scan(V("cmpm"), V("dd"), V("thr"), -2.0, A.max, A.add)
         ts(V("bt"), V("cmpm"), -3.25, A.is_lt, -1.0, A.mult)
         for b in range(2):
-            scan(V("eo", EW * b, EW * b + EW), V("rm", EW * b, EW * b + EW), V("ee", EW * b, EW * b + EW), 0.0, A.max, A.min)
+            scan(V("eo", EW * b + z, EW * b + EW), V("rm", EW * b, EW * b + EW - z), V("ee", EW * b + z, EW * b + EW), 0.0, A.max, A.min)
         tr(V("tid"), V("aiw"))
         act(V("ib"), V("tid", 0, 64, 32), AF.Identity, scale=-16.0, bias=256.0)
         for b in range(2):
@@ -586,8 +608,8 @@ def rank_program(g, core, T, topo):
         if t == 0:
             copy_pool(("cc2", "cc3"), "pc", S0, "pb", S0, S1)
         else:
-            for j, o in enumerate(range(O0, PW, 178)):
-                n = min(178, PW - o)
+            for j, o in enumerate(range(O0, PW, 186)):
+                n = min(186, PW - o)
                 mm(4 + j % 4, "wm", 0, "pc", o, n)
                 act(V("yp", o, o + n), bank(4 + j % 4, 0, n), AF.Copy)
         tr(V("tb2", 0, 32), V("pbh"))
@@ -619,7 +641,7 @@ def rank_program(g, core, T, topo):
         wrap(t + 1, 32 if t else 64)
         if t == 0:
             places(0)
-        pick("hw", 192 + 32 * t, 224 + 32 * t, pool, V("ofh", 8 * t + 6, 8 * t + 8))
+        copy_pool(("hw%d" % (2 * t + 2), "hw%d" % (2 * t + 3)), "hw", 192 + 32 * t, par, 96, 128)
 
     emit(g, T, ops, sent[0])
 
@@ -648,7 +670,7 @@ def emit(g, T, ops, sent):
             return 0, 0
         if n == "dma_start":
             v = a[0] if a[0]["n"] in SCRATCH else a[1]
-            return 60, DM + width(v) * size[SCRATCH[v["n"]][2]] * 0.5 + (4500 if v["n"] == "wms" else 800 if v["n"] == "yc" else 0)
+            return 60, DM + width(v) * size[SCRATCH[v["n"]][2]] * 0.5 + (4500 if v["n"] == "wms" else 800 if o["sem"] in ("dy0", "dy1") else 0)
         if n == "remote_dma_fused":
             return 250, 250
         e = width(a[0])

import numpy as np
from concourse.bass import DstId, RemoteDMATransfer
from concourse.mybir import dt, AluOpType, AxisListType, ActivationFunctionType

P, K, R, N = 192, 24, 3, 4
TINY = 2.0 ** -100
LOW = -1e29
EPS = 2.0 ** -20
C05 = float(np.float32(0.05))
X4, U8, U16, F32, BF, I32 = "float8_e4m3fn_x4", "uint8", "uint16", "float32", "bfloat16", "int32"
O0, O1, B0, B1, B2, S0, S1, PW = 8, 144, 336, 592, 784, 976, 1232, 1488
CT = 512
OL = (2, 0, 4)
SC = 1.0 / 65536
EW = 368

SCRATCH = {"ps": ("psum", [128, 4096], F32)}


def _decl(dtype, **kw):
    for k, n in kw.items():
        SCRATCH[k] = ("sbuf", [128, n], dtype)


for _n, _w in (("qu", 128), ("um", 512), ("qx", 224), ("qn", 128), ("wm", 1024), ("sd0", 32), ("sd1", 48), ("pa", B2), ("pb", S1), ("pc", PW),
               ("par1", 128), ("par2", 128), ("hw", 288), ("fin", 192)):
    _decl(X4, **{_n + "c": _w})
    _decl(U8, **{_n + "s": _w})
_decl(BF, xt=896, ut=1024, ones=224, flip0=448, e0=448, junk=1400, pb0=192, prow=208, ms=24, hd=96, kt0=1024, ktb=768, ktc=768, kt1=1024,
      kt2=1024, fa=256, fb=256, fz=192, cum=256, fzt=PW - CT, pbt=PW - CT, fzr=256, pbr=256, abw=64, pbh=32, tb2=48, seg64=256,
      le=256, seg48=192, pbw=208, tb=96, ee=2 * EW, rm=2 * EW, eo=2 * EW, fr=64, thr=128, dd=128, cmpm=128, bt=128,
      nn=256, fl=192, cm=200, cm2=80, r3=208, r3c=96, r3d=384, r3t=384)
_decl(F32, io=376, cst=48, sm=96, v0=448, rr=64, su=320, cand=32, mcol=24, t192=80, p80=80, u80=80, s192=80, t24=24,
      dg=96, seg16=96, kid=200, mb=192, mb2=192, mk0=200, mkall=280, stb=PW, sc=96, idr=80, cbr=96, tcb=96, alt=32, hcb=64, plr=80, skw=200,
      asw=64, akw=64, aiw=64, wr=64, iob=S1, skr=256, kidr=256, kb2=48, nk1=32, nk2=32, nid=32, hl=8, cl=16,
      at=64, kb=96, vv=256, rv=192, nsr=32, nkr=32, tsc=96, tid=64, e3=312, flip3=312, v3=312, pv=96,
      d32=64, s64=64, yc=208, yn=32, yp=PW, zero=80)
_decl(U16, ofu=32, ofi=8, mk16=8, mland=32, alw=6, idw=6, rem=272, rem0=200, ofe=4, idx=2, olw=2, ofh=16, ofc=16, ol=6, of3=12, ofd=24)
_decl(I32, pi=4, mi=8)

PART = {"scol": ("sm", 0, 2), "ini": ("sm", 2, 2), "gn": ("sm", 4, 4), "best": ("sm", 8, 8), "alf": ("sm", 16, 8), "mf": ("sm", 24, 12),
        "d2": ("sm", 40, 4), "a5": ("sm", 56, 8), "mz": ("sm", 64, 6), "ib": ("sm", 80, 2), "ns": ("sm", 82, 1), "dc": ("sm", 88, 3),
        "best3": ("sm", 84, 3), "mk192": ("mkall", 0, 200), "mka": ("mkall", 200, 80)}
for _b, _d, _l in (("bq", BF, "fa fb fz cum fzr pbr abw pbh tb2 seg64 le seg48 tb fr thr dd cmpm bt"),
                   ("fq", F32, "mb mb2 mk0 kb2 nk1 nk2 nid hl cl at kb nsr nkr tid yn")):
    _at = 0
    for _n in _l.split():
        PART[_n] = (_b, _at, SCRATCH.pop(_n)[1][1])
        _at += -(-PART[_n][2] // 16) * 16
    _decl(_d, **{_b: _at})
WAKE, LAND, FIRST, CY = 200, {"am": 2500, "ap": 2500, "ar": 4000, "as": 6000}, {"ap": 6000, "ar": 5000}, 0.87
DM, GAP, NOISE, TURNS, SPAN, SOFT, SEED = 1500, 800, 1500, 2300, 2500, 0.8, 11
DMAS = ["hw0", "hw1", "hw2", "hw3", "hw4", "hw5", "pa0", "pa1", "pa2", "pa3", "x", "u", "wc", "ws", "cb0", "cb1", "cc0", "cc1", "cc2", "cc3",
        "y0", "y1", "y2", "oc", "os0", "os1", "os2", "os3"]
SEMAPHORES = ["qv", "qs", "qt", "qg", "rl", "am", "ap", "ar", "as"] + ["d" + n for n in DMAS]
MEMO = {}
ONS3 = (0, 1, 2, 4, 5, 6)
A, AF = AluOpType, ActivationFunctionType


def rank_program(g, core, T, topo):
    rank = T.rank_of(core)
    if rank is None:
        return
    ops = []
    beta = [(rank - 1 - r) % N for r in range(N)]

    def V(n, c0=0, c1=None, s=1, p=(0, 128)):
        if n in PART:
            n, c0, c1 = PART[n][0], PART[n][1] + c0, PART[n][1] + (PART[n][2] if c1 is None else c1)
        if c1 is None:
            c1 = T[n].shape[1]
        return {"ap": T[n][p[0]:p[1], c0:c1:s] if s > 1 else T[n][p[0]:p[1], c0:c1], "n": n, "p": p, "c": (c0, c1), "s": s}

    def col(n, c, p=(0, 128)):
        return V(n, c, c + 1, 1, p)

    def bc(v, d):
        return dict(v, ap=v["ap"].bitcast(d))

    def ind(w, o):
        return dict(w, ap=w["ap"].indirect(o["ap"]), off=o)

    def G(q):
        return (32 * q, 32 * q + 32)

    def op(q, name, args, kw=None, nout=1, sem=None, rd=None):
        kw = kw or {}
        w = [a for a in args[:nout]] + [kw[k] for k in kw if k == "accum_out"]
        r = [a for a in args[nout:] if isinstance(a, dict)] + [kw[k] for k in kw if k != "accum_out" and isinstance(kw[k], dict)] + (rd or [])
        r = r + [a["off"] for a in w + r if "off" in a]
        ops.append({"q": q, "name": name, "args": args, "kw": kw, "w": w, "r": r, "sem": sem})

    def ts(o, i, s1, o0, s2=None, o1=None):
        op("v", "tensor_scalar", [o, i, s1, s2, o0] + ([o1] if s2 is not None else []))

    def tt(o, a, b, f):
        op("v", "tensor_tensor", [o, a, b, f])

    def cp(o, i):
        op("v", "tensor_copy", [o, i])

    def act(o, i, f, **kw):
        op("s", "activation", [o, i, f], kw)

    def scan(o, a, b, init, o0, o1):
        op("v", "tensor_tensor_scan", [o, a, b, init, o0, o1])

    def tr(o, i):
        op("v", "transpose", [o, i])

    def red(o, i, f, ab=False):
        op("v", "tensor_reduce", [o, i, AxisListType.X, f], {"apply_absolute_value": True} if ab else {})

    def ms(o, c):
        op("v", "memset", [o, c])

    def iota(o, pat, base, cm):
        op("g", "iota", [o, pat, base, cm], {} if o["n"] == "pi" else {"allow_small_or_imprecise_dtypes": True})

    def fill(o, k):
        n = -(-(o["c"][1] - o["c"][0]) // o["s"])
        if n <= 100 and o["s"] == 1:
            iota(o, [[0, n]], int(k), 0)
        else:
            act(o, V("io", 1, 1 + n), AF.Sign, scale=k)

    def bank(b, c0=0, c1=512):
        return V("ps", 512 * b + c0, 512 * b + c1)

    def mm(b, st, s0, mv, m0, n):
        op("t", "matmul_mx", [bank(b, 0, n), V(st + "c", s0, s0 + 128), V(st + "s", s0, s0 + 128), V(mv + "c", m0, m0 + n), V(mv + "s", m0, m0 + n), True, True])

    def quant(n, c0, c1, i):
        op("v", "quantize_mx", [V(n + "c", c0, c1), V(n + "s", c0, c1), i], nout=2)

    def pick(o, c0, c1, w, off):
        cp(bc(V(o + "c", c0, c1), dt.uint32), ind(bc(V(w + "c"), dt.uint32), off))
        act(V(o + "s", c0, c1), ind(V(w + "s"), off), AF.Copy)

    def dma(q, sem, o, i):
        op(q, "dma_start", [o, i], sem="d" + sem)

    def copy_pool(k, o, o0, i, c0, c1):
        dma("y", k[0], bc(V(o + "c", o0, o0 + c1 - c0), dt.uint8), bc(V(i + "c", c0, c1), dt.uint8))
        dma("y", k[1], V(o + "s", o0, o0 + c1 - c0), V(i + "s", c0, c1))

    peers = [r for r in range(N) if r != rank]
    sent = [0]

    def mask_of(r):
        mask = -1
        for q in range(N):
            if q != r:
                mask &= topo.mask(T.cores[r], T.cores[q])
        return mask

    def send(src, dst, sem):
        ids = [DstId(rid=topo.addr(T.cores[r])[0], pnc=topo.addr(T.cores[r])[1]) for r in peers]
        t = RemoteDMATransfer(dst_ids=ids, dma_engine_mask=mask_of(rank), remote_sem=T.sem[sem], srcs=[src["ap"]], dsts=[dst(r)["ap"] for r in peers])
        op("g", "remote_dma_fused", [[t]], {"local_sem": T.sem.rl}, nout=0, rd=[src], sem="rl")
        ops[-1]["to"] = sem
        sent[0] += bin(mask_of(rank)).count("1")

    def arrive(sem, calls, views):
        ops.append({"q": "arr", "name": sem, "w": views, "r": [], "sem": sem, "val": calls * sum(bin(mask_of(r)).count("1") for r in peers)})

    (P16, P32, Q0, TAUB, PSC, PBI, NREV, TG, B24, IDB, CBB, PAD3, TP, SB, NT, C32, ALC, T16, HALF, SG, H16) = (
        0, 1, 4, 5, 6, 7, 8, 9, 14, 16, 17, 18, 19, 22, 23, 24, 27, 32, 34, 35, 36)

    def c(k, p=(0, 128)):
        return col("cst", k, p)

    dma("y", "x", V("xt", 0, 768), V("x"))
    ms(V("xt", 768, 896), 0.0)
    ms(V("ut", 80, 512), 0.0)
    ms(V("ut", 528, 592), 0.0)
    ms(V("ut", 596, 1024), 0.0)
    dma("s", "u", V("ut", 0, 80), V("u", 0, 80))
    dma("y", "wc", bc(V("wmc"), dt.uint8), V("wc"))
    dma("y", "ws", V("wms"), V("ws"))
    iota(V("pi", 0, 1), [[0, 1]], 0, 1)
    iota(V("io"), [[1, 376]], 0, 0)
    ms(V("ones"), 1.0)
    ms(V("ofu", 0, 8), 0)
    ms(V("ofu", 16, 24), 1)
    ms(V("ofu", 24, 28), 20)
    ms(V("ofu", 28, 32), 2)
    ts(V("pi", 1, 2), V("pi", 0, 1), 15, A.bitwise_and)
    ts(V("pi", 2, 3), V("pi", 0, 1), 31, A.bitwise_and)
    cp(V("cst", P16, P16 + 2), V("pi", 1, 3))
    ms(c(NT), -TINY)
    for t in range(2):
        ms(V("e0", 224 * t + 192, 224 * t + 224), 0.0)
    ts(V("ofu", 8, 16), V("ones", 0, 8), c(P16), A.mult, 2.0, A.add)
    for t in range(2):
        op("g", "affine_select", [V("flip0", 224 * t, 224 * t + 224), V("ones", 0, 224), [[1, 224]], A.not_equal, -1.0, -96 * t, -1])
        ts(col("e0", 224 * t + 192), V("pi", 0, 1), 96.0 * t, A.add, -1.0 / 256, A.mult)
    iota(V("dg"), [[0, 6], [1, 16]], 0, 0)
    iota(V("kid"), [[24, 4], [1, 25], [128, 2]], 0, 0)
    quant("qu", 0, 128, V("ut", 0, 512))
    pick("um", 0, 128, "qu", V("ofu", 0, 8))
    pick("um", 128, 256, "qu", V("ofu", 8, 16))
    cp(V("ut", 512, 528), V("ut", 0, 16))
    ts(V("ut", 592, 596), V("ut", 8, 12), -1.0, A.mult)
    quant("qn", 0, 128, V("ut", 512, 1024))
    ms(V("hd"), 1.0)
    ts(c(HALF), c(P16), 2.0, A.mult, -192.0, A.add)
    ms(V("hd", 1, 11), 2.0)
    ms(V("hd", 0, 96, 48), 0.0)
    act(V("hd", 49, 59), V("hd", 1, 11), AF.Copy)
    ts(V("cst", TG, TG + 2), V("io", 0, 2), 32.0, A.mult, c(HALF), A.add)
    ts(V("cst", TG + 2, TG + 5), V("io", 0, 3), 32.0, A.mult, c(HALF), A.add)
    ts(V("cst", TG + 2, TG + 5), V("cst", TG + 2, TG + 5), 48.0, A.add)

    quant("qx", 0, 224, V("xt"))
    mm(2, "qx", 0, "qu", 0, 128)
    mm(3, "qx", 96, "qu", 0, 128)
    mm(0, "um", 0, "qx", 0, 192)
    mm(1, "um", 0, "qx", 0, 192)
    mm(4, "qx", 0, "qu", 0, 128)
    mm(5, "qx", 96, "qu", 0, 128)
    for t in range(2):
        cp(col("scol", t), bank(2 + t, 0, 1))
    for t in range(2):
        act(V("ms", 12 * t, 12 * t + 10), bank(4 + t, 3, 13), AF.Sign, bias=c(NT))
    for t in range(2):
        ts(V("e0", 224 * t, 224 * t + 192), bank(0, 0, 192), col("scol", t), A.is_equal)
        act(V("junk", 192 * t, 192 * t + 192), bank(1, 0, 192), AF.Sign, bias=col("scol", t), scale=-1.0, accum_out=col("gn", t))
    for t in range(2):
        scan(V("mcol", 12 * t, 12 * t + 10), V("hd", 1, 11), V("ms", 12 * t, 12 * t + 10), 1.0, A.mult, A.add)
    for t in range(2):
        scan(V("v0", 224 * t, 224 * t + 224), V("flip0", 224 * t, 224 * t + 224), V("e0", 224 * t, 224 * t + 224), col("gn", t), A.mult, A.subtract)
    cp(V("mk16", 0, 2), V("mcol", 9, 24, 12))
    ts(V("mk16", 2, 4), V("v0", 192, 448, 224), 191.6, A.add, 0.5, A.mult)
    send(V("mk16", 0, 4), lambda r: V("mland", 8 * rank, 8 * rank + 4), "am")
    for t in range(2):
        tr(V("rr", 32 * t, 32 * t + 32), V("v0", 224 * t + 192, 224 * t + 224))

    def spread(cols):
        k0, k1 = cols[0], cols[-1] + 1
        for k in cols:
            ts(V("su", 64 * k, 64 * k + 64), V("rr"), c(TG + k), A.subtract, 256.0, A.mult)
        for k in cols:
            red(col("cand", k, (0, 96)), V("su", 64 * k, 64 * k + 64, 1, (0, 96)), A.min, True)
        moves = [(1, (64, 128), (0, 64)), (1, G(0), G(1)), (1, G(1), G(0)), (2, G(0), G(2)), (2, G(1), G(2)), (2, G(2), G(1)), (2, G(3), G(0)),
                 (0, G(3), G(2))]
        for i, (d, to, fr) in enumerate(moves):
            if i % 2:
                act(V("cand", 8 * d + k0, 8 * d + k1, 1, to), V("cand", k0, k1, 1, fr), AF.Copy)
            else:
                cp(V("cand", 8 * d + k0, 8 * d + k1, 1, to), V("cand", k0, k1, 1, fr))
        for k in cols:
            ts(col("ofi", k), col("cand", k), col("cand", 8 + k), A.min, col("cand", 16 + k), A.min)

    def there(n, base, w):
        def f(r):
            c0 = base + w * ((r - 1 - rank) % N)
            return bc(V(n, c0, c0 + w), dt.uint8) if n == "pac" else V(n, c0, c0 + w)
        return f

    spread([0, 1])
    pick("sd0", 0, 32, "qx", V("ofi", 0, 2))
    send(bc(V("sd0c", 0, 24), dt.uint8), there("pac", O0, 24), "ap")
    send(V("sd0s", 0, 24), there("pas", O0, 24), "ap")
    spread([2, 3, 4])
    pick("sd1", 0, 48, "qx", V("ofi", 2, 5))
    for k, sem in enumerate(("ar", "as")):
        send(bc(V("sd1c", 24 * k, 24 * k + 24), dt.uint8), there("pac", O1 + 96 * k, 24), sem)
        send(V("sd1s", 24 * k, 24 * k + 24), there("pas", O1 + 96 * k, 24), sem)
    pick("pa", O0 + 72, O1, "qx", V("ofi", 0, 4))
    ts(V("cst", ALC, ALC + 5), V("io", 0, 5), 16.0, A.mult, c(P16), A.add)
    cp(V("cst", T16, T16 + 2), V("cst", ALC, ALC + 2))
    ts(V("cst", H16, H16 + 5), V("cst", ALC, ALC + 5), 0.5, A.add)
    iota(V("cm", 192, 200), [[1, 8]], 73, 0)
    ts(V("seg16"), V("dg"), 0.0, A.not_equal)
    ts(V("dg"), V("dg"), c(P16), A.is_equal)
    pick("um", 256, 512, "qn", V("ofu", 16, 32))
    copy_pool(("pa0", "pa1"), "pa", O1 + 72, "sd1", 0, 24)
    copy_pool(("pa2", "pa3"), "pa", O1 + 168, "sd1", 24, 48)

    ts(V("pi", 3, 4), V("pi", 0, 1), 32, A.bitwise_and)
    ts(c(Q0), V("pi", 3, 4), 0.0, A.is_gt)
    for q in range(4):
        ms(c(B24, G(q)), 24.0 * beta[q])
        ms(c(45, G(q)), 32.0 * beta[q])
    ts(c(IDB), c(B24), float(O0), A.add, -SC, A.mult)
    ts(c(CBB), c(B24), (B1 - CT) / 2 - (O1 - O0), A.add, -2 * SC, A.mult)
    ms(c(TAUB, (0, 64)), -TINY)
    ms(c(TAUB, (64, 128)), 0.0)
    ts(c(PSC), c(P32), 0.5, A.is_gt)
    ts(c(PBI), c(P32), 10.5, A.is_lt)
    tt(c(PSC), c(PSC), c(PBI), A.mult)
    ts(c(44), c(P32), 0.0, A.is_equal)
    ts(c(PBI), c(PSC), -TINY, A.mult, c(44), A.add)
    ts(c(NREV), c(P16), -1.0, A.mult, 15.5, A.add)
    ts(V("cst", C32, C32 + 3), V("io", 0, 3), -32.0, A.mult, c(P32), A.subtract)
    ts(c(PAD3), c(P32), 7.5, A.is_lt)
    ts(c(SG), c(Q0), 2.0, A.mult, -1.0, A.add)
    ts(c(SB), c(SG), -TINY, A.mult)
    ts(V("mi", 6, 7), V("pi", 1, 2), 1, A.logical_shift_right)
    ts(c(42), V("mi", 6, 7), 2.0, A.mult, -72.0, A.add)
    ts(V("cst", TP, TP + 3), V("io", 0, 3), 16.0, A.mult, c(42), A.add)
    for o in range(0, S1, 308):
        iota(V("iob", o, o + 308), [[1, 308]], o, 0)
    for t in range(2):
        h = (S0, S1)[t] - CT
        ts(V("hcb", 32 * t, 32 * t + 32), V("iob", h, h + 32), c(45), A.add, -SC, A.mult)
    fill(V("cl"), 0.0)
    for n, o in (("fzt", B2 - CT), ("pbt", B2 - CT), ("stb", B2)):
        iota(V(n, o, o + 192), [[0, 192]], 0, 0)
    fill(V("fzt", 0, B1 - CT), 0.0)
    fill(V("pbt", 16, B1 - CT), 0.0)
    for o in (0, 128):
        op("g", "affine_select", [V("seg64", o, o + 128), V("ones", 0, 128), [[0, 2], [1, 64]], A.not_equal, 0.0, 0, 0])
    fill(V("tb2"), 0.0)
    fill(V("stb", 0, 8), 0.0)
    fill(V("yp", 0, 8), 0.0)
    fill(V("cbr", 80, 96), 0.0)
    fill(V("prow", 192, 208), 0.0)
    ts(V("pbt", 0, 16), V("ones", 0, 16), c(P32), A.mult, 0.0, A.is_equal)
    for b in range(2):
        fill(V("rm", EW * b + 66, EW * b + EW), 0.0)
        fill(V("rm", EW * b, EW * b + 1), 0.0)
    for b in range(3):
        act(V("flip3", 104 * b, 104 * b + 104), V("io", 0, 104), AF.Abs, bias=c(C32 + b))
    for b in range(2):
        act(V("rm", EW * b + 1, EW * b + 66), V("flip3", 104 * b, 104 * b + 65), AF.Relu, scale=-1.0, bias=1.0)
        act(V("thr", 64 * b, 64 * b + 64), V("io", 0, 64), AF.Sign, bias=c(C32 + b))
    ms(c(43), -0.5)
    act(V("flip3"), V("flip3"), AF.Sign, bias=c(43))
    act(V("flip3", 208, 312), V("flip3", 208, 312), AF.Identity, scale=c(PAD3))
    act(V("thr"), V("thr"), AF.Relu, scale=0.5)
    act(V("thr"), V("thr"), AF.Identity, scale=-1.0, bias=-3.0)
    op("g", "affine_select", [V("seg48"), V("ones", 0, 192), [[0, 4], [1, 48]], A.not_equal, 0.0, 0, 0])
    fill(V("tb"), 0.0)
    for b in range(2):
        fill(V("ee", EW * b + 336, EW * b + EW), 1.0)
        fill(V("nn", 128 * b + 65, 128 * b + 128), 1.0)
        fill(V("nn", 128 * b + 64, 128 * b + 65), 0.0)
        ms(V("nn", 128 * b + 80, 128 * b + 128, 32), -15.0)
    for m in range(2):
        ts(V("pbw", 48 + m, 200, 50), V("ones", 0, 4), c(P32), A.mult, 0.0, A.is_equal)
        fill(V("skw", 48 + m, 200, 50), 0.0)
        ms(V("kt0", 512 * m + 384, 512 * m + 512), 0.0)
    fill(V("zero"), 0.0)
    iota(V("cm2", 72, 80), [[1, 8]], 25, 0)
    ms(V("sc", 80, 96), LOW)
    iota(V("mk0", 192, 200), [[0, 8]], 1024, 0)
    iota(V("mk192", 192, 200), [[0, 8]], 1024, 0)
    fill(V("yc", 192, 208), 0.0)
    iota(V("r3"), [[1, 208]], -128, 0)
    iota(V("r3c"), [[1, 96]], 64, 0)
    iota(V("t24"), [[16, 12], [0, 2]], 0, 0)
    iota(V("alt"), [[0, 16], [-2, 2]], 1, 0)
    ts(V("ofd"), V("t24"), c(P16), A.add)
    copy_pool(("hw0", "hw1"), "hw", 0, "qx", 0, 192)
    mm(6, "wm", 0, "qx", 0, 192)
    act(V("yc", 0, 192), bank(6, 0, 192), AF.Copy)

    arrive("am", 1, [V("mland")])
    arrive("ap", 2, [V("pac", O0, O0 + 72), V("pas", O0, O0 + 72)])
    arrive("ar", 2, [V("pac", O1, O1 + 72), V("pas", O1, O1 + 72)])
    arrive("as", 2, [V("pac", O1 + 96, O1 + 168), V("pas", O1 + 96, O1 + 168)])

    def to_all(o, i, f):
        for q in range(4):
            ts(o(G(q)), i, f, A.mult)

    def state_in():
        for q in range(4):
            for s in range(3):
                cp(V("mf", s, 12, 3, G(q)), V("mk16", 0, 4, 1, G(s)) if q == rank else V("mland", 8 * q, 8 * q + 4, 1, G(s)))
        for b in range(6):
            act(V("pb0", 32 * b, 32 * b + 32), V("zero", 0, 32), AF.Identity, bias=col("mf", 6 + b))
        ts(V("mz"), V("mf", 6, 12), 23.5, A.is_gt)
        tt(V("mf", 0, 6), V("mf", 0, 6), V("mz"), A.mult)
        for b in range(6):
            act(V("mb", 32 * b, 32 * b + 32), V("zero", 0, 32), AF.Identity, bias=col("mf", b))
        tr(V("prow", 0, 192), V("pb0"))
        tr(V("mk0", 0, 192), V("mb"))
        cp(V("rem0"), V("mk0"))
        ts(V("mz"), V("mf", 6, 12), 71.5, A.is_gt)
        tt(V("mz"), V("mf", 0, 6), V("mz"), A.mult)
        for b in range(6):
            act(V("mb2", 32 * b, 32 * b + 32), V("zero", 0, 32), AF.Identity, bias=col("mz", b))
        tr(V("mk192", 0, 192), V("mb2"))
        ts(V("fl"), V("prow", 0, 192), 71.5, A.is_lt)
        scan(V("cm", 0, 192), V("ones", 0, 192), V("fl"), 0.0, A.mult, A.add)
        for k in range(5):
            act(V("junk", 384 + 200 * k, 520 + 200 * k), V("cm", 16 * k, 16 * k + 136), AF.Sign, bias=c(H16 + k), scale=-1.0, accum_out=col("a5", k))
        tt(V("a5", 0, 5), V("a5", 0, 5), V("io", 136, 296, 32), A.add)
        ts(V("alw", 0, 5), V("a5", 0, 5), 0.5, A.mult)
        cp(V("p80"), ind(V("prow"), V("alw", 0, 5)))
        ts(V("t192"), V("p80"), 23.5, A.is_gt, 112.0, A.mult)
        ts(V("u80"), V("p80"), 47.5, A.is_gt, 72.0, A.mult)
        tt(V("t192"), V("t192"), V("p80"), A.add)
        tt(V("t192"), V("t192"), V("u80"), A.add)
        act(V("idr"), V("t192"), AF.Identity, scale=-SC, bias=c(IDB))
        act(V("cbr", 0, 80), V("t192"), AF.Identity, scale=-2 * SC, bias=c(CBB))
        tt(V("u80"), V("t192"), V("dg", 0, 80), A.mult)
        scan(V("s192"), V("seg16", 0, 80), V("u80"), 0.0, A.mult, A.add)
        ts(V("idw", 0, 5), V("s192", 15, 80, 16), c(B24), A.add)
        act(V("mka"), ind(V("mk0"), V("alw", 0, 5)), AF.Copy)
        act(V("plr"), ind(V("io"), V("alw", 0, 5)), AF.Identity, scale=-SC)
        cp(V("rem", 0, 200), V("mk192"))

    def opened1(t):
        if t == 0:
            ts(V("fl", 0, 72), V("p80", 0, 72), 23.5, A.is_lt)
        else:
            ts(V("fl", 0, 72), V("pv", 0, 72), -25.0, A.is_lt)
        scan(V("cm2", 0, 72), V("ones", 0, 72), V("fl", 0, 72), 0.0, A.mult, A.add)
        for k in range(2):
            act(V("junk", 80 * k, 80 * k + 80), V("cm2"), AF.Sign, bias=c(H16 + k), scale=-1.0, accum_out=col("d2", k))

    def opened2(t):
        ts(V("olw"), V("d2", 0, 2), 0.5, A.mult, 40.0, A.add)
        act(V("nk1"), ind(V("idr"), V("olw")), AF.Identity, scale=-16.0)
        tt(V("nk2"), V("nk1"), V("io", 0, 32), A.add)
        act(V("wr", 0, 32) if t else V("wr", 32, 64), ind(V("plr"), V("olw")), AF.Copy)
        if t < R - 1:
            cp(ind(V("cbr"), V("olw")), V("hcb", 32 * t, 32 * t + 32))
            tr(V("tcb"), V("cbr"))
            act(V("e3", 72, 312, 104), V("tcb", 0, 96, 32), AF.Copy)
            act(V("dc"), V("tcb", 0, 96, 32), AF.Sign, bias=(S0 - CT - 0.5) * SC)
            act(V("dc"), V("dc"), AF.Identity, scale=63.5 * SC, bias=-64.5 * SC)
            for b in range(3):
                act(V("e3", 104 * b + 73, 104 * b + 104), V("alt", 0, 31), AF.Identity, scale=col("dc", b))

    def opened3(t):
        cp(ind(V("mka"), V("olw")), V("zero", 0, 32))
        cp(V("rem", 200, 272), V("mka", 0, 72))

    def wrap(t, n):
        tt(V("d32", 0, n), V("wr", 0, n), V("dg", 0, n), A.mult)
        scan(V("s64", 0, n), V("seg16", 0, n), V("d32", 0, n), 0.0, A.mult, A.add)
        to_all(lambda p: V("ol", 4 * t - 4, 4 * t - 4 + n // 16, 1, p), V("s64", 15, n, 16, G(rank)), -65536.0)

    def places(t):
        cp(ind(V("r3"), V("ol", OL[t], OL[t] + 2)), V("r3c", 32 * t, 32 * t + 32))
        if t == R - 1:
            for b in range(3):
                act(V("r3d", 128 * b, 128 * b + 128), ind(V("r3"), V("ofd", 8 * b, 8 * b + 8)), AF.Copy)
                tr(V("r3t", 128 * b, 128 * b + 128), V("r3d", 128 * b, 128 * b + 128))
            ts(V("of3"), V("r3t", 0, 384, 32), 128.0, A.add)

    pools, END = ("pa", "pb", "pc"), (B1, S1, PW)

    def y_out(t, q="y"):
        cp(ind(V("yc"), V("ol", OL[t], OL[t] + 2)), V("yn"))
        dma(q, "y%d" % t, V("y", P * t, P * t + P), V("yc", 0, P))

    def children(p0, b0, kt, pool, c0, on_s):
        for i in range(8):
            mm(i, "wm", 128 * i, "pa", p0, 128)
            if i in on_s:
                act(V(kt, i, 768, 8), bank(i, b0, b0 + 96), AF.Relu, scale=C05)
            else:
                ts(V(kt, i, 768, 8), bank(i, b0, b0 + 96), 0.0, A.max, C05, A.mult)
        quant(pool, c0, c0 + 192, V(kt))

    def numbers(pool, c0, n, k=0, f0=0):
        for b, s0 in enumerate((256, 384, 128, 0)):
            mm(k + b, "um", s0, pool, c0, n)
        act(V("fa", f0, f0 + n), bank(k, 0, n), AF.Sign, bias=c(SB), scale=c(SG))
        ts(V("fb", f0, f0 + n), bank(k + 1, 0, n), c(TAUB), A.is_gt, -EPS, A.mult)
        scan(V("fzt", c0 - CT, c0 - CT + n), V("fa", f0, f0 + n), V("fb", f0, f0 + n), 0.0, A.max, A.mult)
        act(V("pbt", c0 - CT, c0 - CT + n), bank(k + 2, 0, n), AF.Sign, bias=c(PBI), scale=c(PSC))
        act(V("stb", c0, c0 + n), bank(k + 3, 0, n), AF.Copy)

    for i in range(8):
        mm(i, "wm", 128 * i, "pa", O0, 128)
        o = V("kt0", 512 * (i // 4) + i % 4, 512 * (i // 4) + 384, 4)
        if i % 2:
            act(o, bank(i, 0, 96), AF.Relu, scale=C05)
        else:
            ts(o, bank(i, 0, 96), 0.0, A.max, C05, A.mult)
    for m in range(2):
        c0, k = B0 + 128 * m, 4 * m
        quant("pa", c0, c0 + 128, V("kt0", 512 * m, 512 * m + 512))
        for b, s0 in enumerate((256, 384, 128, 0)):
            mm(k + b, "um", s0, "pa", c0, 128)
        act(V("fa", 128 * m, 128 * m + 96), bank(k, 0, 96), AF.Sign, bias=c(SB), scale=c(SG))
        ts(V("fb", 128 * m, 128 * m + 96), bank(k + 1, 0, 96), c(TAUB), A.is_gt, -EPS, A.mult)
        scan(V("fz", m, 192, 2), V("fa", 128 * m, 128 * m + 96), V("fb", 128 * m, 128 * m + 96), 0.0, A.max, A.mult)
        for b in range(4):
            act(V("pbw", 50 * b + m, 50 * b + 48, 2), bank(k + 2, 24 * b, 24 * b + 24), AF.Sign, bias=c(PBI), scale=c(PSC))
        for b in range(4):
            act(V("skw", 50 * b + m, 50 * b + 48, 2), bank(k + 3, 24 * b, 24 * b + 24), AF.Copy)
        act(V("stb", c0, c0 + 128), bank(k + 3, 0, 128), AF.Copy)
    for t in range(R):
        pool, last = pools[t], t == R - 1
        if t == 0:
            sw, seg, pb, sk = 48, 50, V("pbw", 0, 200), V("skw")
            scan(V("cum", 0, 192), V("seg48"), V("fz"), 0.0, A.mult, A.subtract)
        else:
            sw, seg, pb, sk = 64, 64, V("pbr"), V("skr")
            cp(V("fzr", 0, 128), ind(V("fzt", 0, END[t] - CT), V("ofc", 0, 8)))
            act(V("fzr", 128, 256), ind(V("fzt", 0, END[t] - CT), V("ofc", 8, 16)), AF.Copy)
            act(V("pbr"), ind(V("pbt", 0, END[t] - CT), V("ofc")), AF.Copy)
            act(V("skr"), ind(V("stb", CT, END[t]), V("ofc")), AF.Copy)
            act(V("kidr"), ind(V("iob"), V("ofc")), AF.Identity, scale=-SC, bias=-CT * SC)
            scan(V("cum"), V("seg64"), V("fzr"), 0.0, A.mult, A.subtract)
            opened3(t)
            places(t)
        for k in range(4):
            b = (rank + k) % 4
            act(V("le", sw * b, sw * b + 48), V("cum", sw * b, sw * b + 48), AF.Sign, bias=c(NREV), scale=-1.0 / EPS, accum_out=col("alf", k))
            ts(col("ofe", k), col("alf", k), 0.5, A.mult, 24.0 + seg * b, A.add)
        if t == 0:
            state_in()
            opened1(0)
        cp(V("abw"), ind(pb, V("ofe")))
        act(V("asw"), ind(sk, V("ofe")), AF.Copy)
        if t == 0:
            act(V("aiw"), ind(V("kid"), V("ofe")), AF.Identity, scale=-SC, bias=-B0 * SC)
            opened2(0)
        else:
            act(V("aiw"), ind(V("kidr"), V("ofe")), AF.Copy)
        for b in range(2):
            tr(V("tb", 48 * b, 48 * b + 32), V("abw", 32 * b, 32 * b + 32))
        scan(V("kb"), V("hd"), V("tb"), 0.0, A.mult, A.subtract)
        for b in range(2):
            tr(V("akw", 32 * b, 32 * b + 32), V("kb", 48 * b + 16, 48 * b + 48))
        tr(V("at"), V("asw"))
        for b in range(2):
            act(V("dd", 64 * b, 64 * b + 64), V("asw"), AF.Sign, bias=col("at", 32 * b), scale=-1.0)
        z = 0 if t else 72
        ts(V("ee", z + 64, 336), V("rem") if t else V("rem0"), col("kb", 16), A.add, 0.0, A.not_equal)
        act(V("ee", EW + z + 64, EW + 336), V("mkall", 0, 272) if t else V("mk0"), AF.Abs, bias=col("kb", 64))
        for b in range(2):
            ts(V("ee", EW * b + z, EW * b + z + 64), V("akw"), col("kb", 48 * b + 16), A.not_equal)
        if t > 0:
            y_out(t - 1)
        scan(V("cmpm"), V("dd"), V("thr"), -2.0, A.max, A.add)
        ts(V("bt"), V("cmpm"), -3.25, A.is_lt, -1.0, A.mult)
        for b in range(2):
            scan(V("eo", EW * b + z, EW * b + EW), V("rm", EW * b, EW * b + EW - z), V("ee", EW * b + z, EW * b + EW), 0.0, A.max, A.min)
        tr(V("tid"), V("aiw"))
        act(V("ib"), V("tid", 0, 64, 32), AF.Identity, scale=-16.0, bias=256.0)
        for b in range(2):
            tr(V("fr", 32 * b, 32 * b + 32), V("eo", EW * b + 336, EW * b + EW))
        for b in range(2):
            act(col("ini", b), col("eo", EW * b + 336), AF.Identity, scale=-256.0, bias=col("ib", b))
        act(V("junk", 400, 464), V("fr"), AF.Identity, bias=-1.0 / 128, accum_out=V("ns"))
        for b in range(2):
            scan(V("nn", 128 * b, 128 * b + 64), V("fr"), V("bt", 64 * b, 64 * b + 64), 0.0, A.max, A.mult)
        for b in range(2):
            scan(V("vv", 128 * b, 128 * b + 128), V("ones", 0, 128), V("nn", 128 * b, 128 * b + 128), col("ini", b), A.mult, A.subtract)
        for k in range(2):
            ts(V("rv", 96 * k + 64, 96 * k + 96), V("nk2"), V("ns"), A.max, c(T16 + k), A.subtract)
        for k in range(2):
            for b in range(2):
                tr(V("rv", 96 * k + 32 * b, 96 * k + 32 * b + 32), V("vv", 128 * b + 64 + 32 * k, 128 * b + 96 + 32 * k))
        for k in range(2):
            red(col("best", k), V("rv", 96 * k, 96 * k + 96), A.min, True)
        if last:
            to_all(lambda p: V("idx", 0, 2, 1, p), V("best", 0, 2, 1, G(rank)), 4096.0)
            pick("hw", 192 + 32 * t, 224 + 32 * t, pool, V("idx"))
            pick("fin", 0, 192, "hw", V("of3"))
            act(V("yn"), ind(V("yp"), V("idx")), AF.Copy)
            dma("y", "oc", V("oc"), bc(V("finc"), dt.uint8))
            for k in range(4):
                dma("sy"[k % 2], "os%d" % k, V("osc", 0, P, 1, (4 * k, 4 * k + 4)), V("fins", 0, P, 1, (32 * k, 32 * k + 4)))
            y_out(t, "s")
            break
        if t == 0:
            children(O1 - 32, 32, "ktb", "pa", B1, range(8))
            numbers("pa", B1, 192)
            mm(4, "um", 0, "pa", O0, 328)
            act(V("stb", O0, B0), bank(4, 0, 328), AF.Copy)
            act(V("sc", 0, 80), ind(V("stb", O0, B0), V("idw", 0, 5)), AF.Copy)
            copy_pool(("cb0", "cb1"), "pb", O0, "pa", O0, B2)
            copy_pool(("cc0", "cc1"), "pc", O0, "pa", O0, B2)
        else:
            children(O1 + 64, 32, "ktc", "pc", B2, range(8))
            numbers("pc", B2, 192)
        ts(V("idx"), V("best", 0, 2), 4096.0, A.mult)
        cp(V("nsr"), ind(V("stb", 0, END[t]), V("idx")))
        act(V("nid"), ind(V("iob"), V("idx")), AF.Identity, scale=-SC)
        cp(ind(V("sc"), V("olw")), V("nsr"))
        cp(ind(V("idr"), V("olw")), V("nid"))
        for q in range(4):
            o, i = V("hl", 2 * beta[q], 2 * beta[q] + 2, 1, G(0)), V("best", 0, 2, 1, G(q))
            if q:
                act(o, i, AF.Copy)
            else:
                cp(o, i)
        for q in range(4):
            ts(V("ofh", 8 * t, 8 * t + 8, 1, G(q)), V("hl", 0, 8, 1, G(0)), 4096.0, A.mult)
        par, c0, kt = "par%d" % (t + 1), (S0, S1)[t], "kt%d" % (t + 1)
        pick(par, 0, 128, pool, V("ofh", 8 * t, 8 * t + 8))
        for i in range(8):
            mm(i, "wm", 128 * i, par, 0, 128)
            o = V(kt, 512 * (i // 4) + i % 4, 512 * (i // 4) + 512, 4)
            if i in ONS3:
                act(o, bank(i, 0, 128), AF.Relu, scale=C05)
            else:
                ts(o, bank(i, 0, 128), 0.0, A.max, C05, A.mult)
        act(V("yn"), bank(0, 96, 128), AF.Copy)
        mm(6, "um", 128, par, 0, 128)
        for q in range(4):
            act(V("pbh", 0, 32, 1, G(q)), V("ps", 3072 + 32 * beta[q], 3104 + 32 * beta[q], 1, G(q)), AF.Sign, bias=c(PBI, G(q)), scale=c(PSC, G(q)))
        for m in range(2):
            quant(pools[t + 1], c0 + 128 * m, c0 + 128 * m + 128, V(kt, 512 * m, 512 * m + 512))
            numbers(pools[t + 1], c0 + 128 * m, 128, 4 * m, 128 * m)
        if t == 0:
            copy_pool(("cc2", "cc3"), "pc", S0, "pb", S0, S1)
        else:
            for j, o in enumerate(range(O0, PW, 186)):
                n = min(186, PW - o)
                mm(4 + j % 4, "wm", 0, "pc", o, n)
                act(V("yp", o, o + n), bank(4 + j % 4, 0, n), AF.Copy)
        tr(V("tb2", 0, 32), V("pbh"))
        scan(V("kb2"), V("hd", 0, 48), V("tb2"), 0.0, A.mult, A.add)
        tr(V("nkr"), V("kb2", 16, 48))
        cp(ind(V("mka"), V("olw")), V("nkr"))
        tr(V("tsc"), V("sc"))
        for b in range(3):
            ts(V("e3", 104 * b, 104 * b + 72), V("sc", 0, 72), col("tsc", 32 * b), A.is_equal)
            act(V("junk", 160 + 72 * b, 232 + 72 * b), V("sc", 0, 72), AF.Sign, bias=col("tsc", 32 * b), scale=-1.0, accum_out=col("gn", b))
        for b in range(3):
            scan(V("v3", 104 * b, 104 * b + 104), V("flip3", 104 * b, 104 * b + 104), V("e3", 104 * b, 104 * b + 104), col("gn", b), A.mult, A.subtract)
        for b in range(3):
            tr(V("pv", 32 * b, 32 * b + 32), V("v3", 104 * b + 72, 104 * b + 104))
        for k in range(3):
            act(V("su", 104 * k, 104 * k + 72), V("pv", 0, 72), AF.Abs, scale=-1.0, bias=c(TP + k))
        for k in range(3):
            red(col("best3", k), V("su", 104 * k, 104 * k + 72), A.min)
        for q in range(4):
            o, i = V("cl", 4 * beta[q], 4 * beta[q] + 3, 1, G(0)), V("best3", 0, 3, 1, G(q))
            if q % 2:
                act(o, i, AF.Identity, scale=65536.0)
            else:
                ts(o, i, 65536.0, A.mult)
        for q in range(4):
            cp(V("ofc", 0, 16, 1, G(q)), V("cl", 0, 16, 1, G(0)))
        opened1(t + 1)
        opened2(t + 1)
        wrap(t + 1, 32 if t else 64)
        if t == 0:
            places(0)
        copy_pool(("hw%d" % (2 * t + 2), "hw%d" % (2 * t + 3)), "hw", 192 + 32 * t, par, 96, 128)

    emit(g, T, ops, sent[0])


def emit(g, T, ops, sent):
    queue = {"v": g.vector, "s": g.scalar, "t": g.tensor, "g": g, "y": g.sync}
    size = {F32: 4, I32: 4, X4: 4, BF: 2, U16: 2, U8: 1}
    seen = {}

    def meet(a, b):
        if a["n"] == "ps":
            return a["c"][0] // 512 == b["c"][0] // 512
        if a["s"] == b["s"] and (a["c"][0] - b["c"][0]) % a["s"]:
            return False
        return a["p"][0] < b["p"][1] and b["p"][0] < a["p"][1] and a["c"][0] < b["c"][1] and b["c"][0] < a["c"][1]

    def two(v):
        return size[SCRATCH[v["n"]][2]] == 2

    def width(v):
        return 16 * (v["off"]["c"][1] - v["off"]["c"][0]) if "off" in v else -(-(v["c"][1] - v["c"][0]) // v["s"])

    def cost(o):
        n, a = o["name"], o.get("args")
        if o["q"] == "arr":
            return 0, 0
        if n == "dma_start":
            v = a[0] if a[0]["n"] in SCRATCH else a[1]
            return 60, DM + width(v) * size[SCRATCH[v["n"]][2]] * 0.5 + (4500 if v["n"] == "wms" else 800 if o["sem"] in ("dy0", "dy1") else 0)
        if n == "remote_dma_fused":
            return 250, 250
        e = width(a[0])
        if n == "matmul_mx":
            d = (e + 16) * 0.6
        elif n == "quantize_mx":
            d = 15 + 0.92 * e
        elif n in ("iota", "affine_select"):
            d = 150 + 2 * CY * e
        elif "off" in a[0]:
            d = 50 + 3.5 * CY * e
        elif len(a) > 1 and isinstance(a[1], dict) and "off" in a[1]:
            d = 60 + 1.5 * CY * e
        elif n == "tensor_reduce":
            d = max(64, width(a[1])) * CY
        elif n == "tensor_tensor":
            d = max(64, 2 * e) * CY
        else:
            full = [v for v in a[:3 if n == "tensor_tensor_scan" else 2] if isinstance(v, dict)]
            d = max(64, e * (0.5 if n != "activation" and all(two(v) for v in full) else 1)) * CY + (20 if "accum_out" in o["kw"] else 0)
        return d, d + (1000 if a[0]["n"] == "of3" or (n == "quantize_mx" and a[2]["n"] in ("ktb", "ktc")) else 0)

    last_send, sends = None, {}
    for i, o in enumerate(ops):
        q = o["q"]
        o["i"], o["dep"], o["lag"] = i, set(), {}
        if q == "arr" or o["name"] == "dma_start":
            for j, v in enumerate(o["w"]):
                if v["n"] in SCRATCH:
                    k = 16 // size[SCRATCH[v["n"]][2]]
                    o["w"][j] = dict(v, c=(v["c"][0] - v["c"][0] % k, v["c"][1] + -v["c"][1] % k))
        for kind, views in (("w", o["w"]), ("r", o["r"])):
            for v in views:
                for (k2, v2, o2) in seen.get(v["n"], []):
                    if (kind == "w" or k2 == "w" or (v["n"] == "ps" and o2["q"] != q)) and meet(v, v2):
                        if q != "arr" or o2["name"] != "dma_start":
                            o["dep"].add(o2["i"])
        if o["name"] == "remote_dma_fused":
            if last_send is not None:
                o["lag"][last_send] = 1500 if ops[last_send]["to"] == "am" else 0
            last_send = sends[o["to"]] = i
        if q == "arr":
            o["lag"][sends[o["sem"]]] = LAND[o["sem"]]
        for kind, views in (("w", o["w"]), ("r", o["r"])):
            for v in views:
                seen.setdefault(v["n"], []).append((kind, v, o))
        o["busy"], o["took"] = cost(o)
    for o in ops:
        o["pre"], o["post"] = [(d, WAKE) for d in sorted(o["dep"])] + list(o["lag"].items()), []
        o["rest"] = o["took"] + FIRST.get(o["name"], 0)
    for o in reversed(ops):
        for d, lag in o["pre"]:
            ops[d]["rest"] = max(ops[d]["rest"], ops[d]["took"] + lag + o["rest"] + FIRST.get(ops[d]["name"], 0))
            ops[d]["post"].append((o["i"], lag))

    def place(order, back):
        busy, at = {q: [] for q in list(queue) + ["arr"]}, {}
        for o in order:
            if back:
                t = max([at[d] + ops[d]["busy"] + lag + o["took"] - o["busy"] for d, lag in o["post"]] + [o["took"] - o["busy"]])
            else:
                t = max([at[d] + ops[d]["took"] + lag for d, lag in o["pre"]] + [0])
            line = busy[o["q"]]
            j, hi = 0, len(line)
            while j < hi:
                mid = (j + hi) // 2
                if line[mid][1] <= t:
                    j = mid + 1
                else:
                    hi = mid
            while j < len(line) and line[j][0] < t + o["busy"]:
                t = max(t, line[j][1])
                j += 1
            line.insert(j, (t, t + o["busy"]))
            at[o["i"]] = t
        return at

    tails = {}

    def length(at, f):
        free, end = {}, {}
        for o in sorted(ops, key=lambda e: (at[e["i"]], e["i"])):
            k = f if o["q"] in "vst" else 1
            t = max([end[d] + lag for d, lag in o["pre"]] + [free.get(o["q"], 0)])
            free[o["q"]] = t + k * o["busy"]
            end[o["i"]] = t + k * o["took"]
        if f not in tails:
            tails[f] = {}
            for o in reversed(topo_order(ops, at)):
                tails[f][o["i"]] = max([lag + (f if ops[d]["q"] in "vst" else 1) * ops[d]["took"] + tails[f][d] for d, lag in o["post"]] + [0])
        return max(end.values()) + SOFT * sum(end[i] + tails[f][i] for i in end) / len(end)

    at = place(sorted(ops, key=lambda e: (-e["rest"], e["i"])), False)
    for turn in range(4):
        for o in ops:
            late = o["i"] in MEMO["late"] if "late" in MEMO else at[o["i"]] + o["busy"] > at[sends["am"]] - GAP
            if o["q"] == "g" and "to" not in o and late and (last_send, 0) not in o["pre"]:
                o["pre"].append((last_send, 0))
                ops[last_send]["post"].append((o["i"], 0))
        at = place(topo_order(ops, at), False)
    if "at" not in MEMO:
        MEMO["late"] = {o["i"] for o in ops if (last_send, 0) in o["pre"]}
        best, seed = None, SEED
        for turn in range(TURNS):
            score = length(at, 1.0) + length(at, 1.4)
            if best is None or score < best[0]:
                best = (score, at)
            key = {}
            if turn % 3 == 0:
                seed = (seed * 1103515245 + 12345) % 2147483648
                t0 = seed % 40000
                for o in ops:
                    seed = (seed * 1103515245 + 12345) % 2147483648
                    t = best[1][o["i"]]
                    key[o["i"]] = t + (NOISE * (seed / 2147483648) ** 3 if t0 <= t < t0 + SPAN else 0)
            else:
                late = place(sorted(ops, key=lambda e: (-at[e["i"]] - e["took"], -e["i"])), True)
                for o in ops:
                    key[o["i"]] = -late[o["i"]] - o["busy"]
            at = place(topo_order(ops, key), False)
        MEMO["at"], MEMO["score"] = best[1], best[0]
    at = place(topo_order(ops, MEMO["at"]), False)
    for o in ops:
        o["t"] = at[o["i"]]
    count = {}
    clock = {q: {} for q in queue}
    for o in sorted(ops, key=lambda e: (e["t"], e["i"])):
        q = o["q"]
        if q == "arr":
            o["key"], o["clk"] = o["sem"], {}
            count[o["key"]] = o["val"]
            continue
        for o2 in sorted([ops[d] for d in o["dep"]], key=lambda e: -e["t"]):
            key, val = o2["key"], o2["val"]
            if clock[q].get(key, 0) < val and key != "rl":
                queue[q].wait_ge(T.sem[key], val)
                for k2, v2 in list(o2["clk"].items()) + [(key, val)]:
                    clock[q][k2] = max(clock[q].get(k2, 0), v2)
        args = [a["ap"] if isinstance(a, dict) else a for a in o["args"]]
        kw = {k: (a["ap"] if isinstance(a, dict) else a) for k, a in o["kw"].items()}
        ins = call(queue[q], o["name"], args, kw)
        o["clk"] = dict(clock[q])
        if o["name"] == "remote_dma_fused":
            o["key"], o["val"] = "rl", sent
        elif o["name"] == "dma_start":
            o["key"], o["val"] = o["sem"], 16
            ins.then_inc(T.sem[o["sem"]], 16)
        else:
            o["key"] = "q" + q
            o["val"] = count.get(o["key"], 0) + 1
            ins.then_inc(T.sem[o["key"]], 1)
        count[o["key"]] = o["val"]
    for key, val in count.items():
        g.wait_ge(T.sem[key], val)


def topo_order(ops, key):
    done, out = set(), []

    def visit(o):
        if o["i"] not in done:
            done.add(o["i"])
            for d in sorted(d for d, lag in o["pre"]):
                visit(ops[d])
            out.append(o)
    for o in sorted(ops, key=lambda e: (key[e["i"]], e["i"])):
        visit(o)
    return out


def call(q, name, a, kw):
    if name == "tensor_scalar":
        return q.tensor_scalar(*a)
    if name == "tensor_tensor":
        return q.tensor_tensor(*a)
    if name == "tensor_copy":
        return q.tensor_copy(*a)
    if name == "activation":
        return q.activation(*a, **kw)
    if name == "tensor_tensor_scan":
        return q.tensor_tensor_scan(*a)
    if name == "transpose":
        return q.transpose(*a)
    if name == "tensor_reduce":
        return q.tensor_reduce(*a, **kw)
    if name == "memset":
        return q.memset(*a)
    if name == "iota":
        return q.iota(*a, **kw)
    if name == "affine_select":
        return q.affine_select(*a)
    if name == "matmul_mx":
        return q.matmul_mx(*a)
    if name == "quantize_mx":
        return q.quantize_mx(*a)
    if name == "dma_start":
        return q.dma_start(*a)
    return q.remote_dma_fused(*a, **kw)
